import numpy as np, ml_dtypes
CORES = [16,18,20,22]
N = 4
BF = ml_dtypes.bfloat16
W, K, RO = 7168, 192, 4
M = N * K
def rows(rng, n):
    return np.argsort(rng.random(n.shape + (16,)), axis=-1) < n[..., None]
def swaps(rng, q, k):
    u = np.argsort(rng.random((k.size, 2, 8)), axis=-1) < k[:, None, None]
    a = np.zeros((k.size, 16), bool); a[:, q] = u[:, 0]; a[:, ~q] = u[:, 1]
    return a
def off(rng, q, lo, hi):
    e = rng.integers(lo, hi, q.shape); up = rng.random(q.shape) < 0.5
    return np.where((up & (q + e <= 63)) | (q - e < 0), q + e, q - e)
def mix(rng, q, far, lo, hi):
    y = np.broadcast_to(q, far.shape + (16,))
    return np.where(rows(rng, far), off(rng, y, lo, hi), y)
def put(x, r, g, p, v):
    x[r, g, 2 * p] = v; x[r, g, 2 * p + 1] = v
def names(rng, lim=W // 2):
    p = np.argsort(rng.random((8, 16, W // 2)) + 2.0 * (np.arange(W // 2) >= lim), axis=-1)[..., :M]
    return np.ascontiguousarray((2 * p + rng.integers(0, 2, p.shape)).reshape(8, 16, N, K).transpose(2, 0, 1, 3))
def spots(rng, pairs, alike):
    p = np.repeat(pairs[:, None], 16, axis=1); q = np.take_along_axis(p, np.argsort(rng.random(p.shape), axis=-1), -1)
    for g in alike: q[g] = p[g]
    return np.ascontiguousarray((2 * q + rng.integers(0, 2, q.shape)).transpose(2, 0, 1, 3))
def lay(pairs, rec, rest):
    z = rest.copy()
    for g in range(8): z[:, g, pairs[g].reshape(-1)] = rec[:, g]
    return np.repeat(z, 2, axis=2)
def near(rng, a, p, amp=1):
    a = np.broadcast_to(a, (N, 8, W, 16)); e = np.where(rng.random(a.shape) < 0.5, 1, rng.integers(2, 6, a.shape)) * (2 * rng.integers(0, 2, a.shape) - 1)
    return np.clip(a + amp * e * (rng.random(a.shape) < p), 0, 63)
def pack(fa, cl, ru):
    b = np.ascontiguousarray(ru.transpose(0, 2, 1)).reshape(128, 16).astype(np.float32).astype(BF)
    return {"fa": np.ascontiguousarray(fa.transpose(0, 1, 3, 2)).reshape(N, 128, W).astype(np.float32).astype(BF),
            "cl": np.ascontiguousarray(cl).reshape(N, 128, K).astype(np.int32), "ru": np.stack([b] * N)}
def setup_inputs(rng):
    a = rng.integers(1, 63, (8, 16)); e = (rng.random((N, 8, 16)) < 0.12) * (2 * rng.integers(0, 2, (N, 8, 16)) - 1)
    fa = near(rng, (a + e)[:, :, None], 0.3 + 0.6 * rng.random((N, 8, W, 1)))
    ru = np.clip(a[:, None] + (rng.random((8, 16, 16)) < 0.1) * (2 * rng.integers(0, 2, (8, 16, 16)) - 1), 0, 63)
    return pack(fa, names(rng), ru)
def setup_inputs_spread(rng):
    a = rng.integers(0, 64, (1, 8, 1, 16)); e = (rng.random((N, 8, 1, 16)) < 0.12) * (2 * rng.integers(0, 2, (N, 8, 1, 16)) - 1)
    fa = near(rng, np.clip(a + e, 0, 63), rng.random((N, 8, W, 1)) ** 2 + 0.1, 2 ** rng.integers(0, 5, (N, 8, W, 1)))
    s = np.where(rng.random((N, 4, W, 1)) < 0.6, 16, rng.choice(np.array([1, 3, 8]), (N, 4, W, 1)))
    u = np.minimum((64 * rng.random((N, 4, W, 16)) ** s).astype(np.int64), 63)
    fa[:, 1::2] = np.where(rng.random((1, 4, 1, 16)) < 0.5, 63 - u, u)
    ru = fa[rng.integers(0, N, (8, 16)), np.arange(8)[:, None], rng.integers(0, W, (8, 16))]
    cl = names(rng, rng.choice(np.array([M, M + M // 2, W // 2]), (8, 16, 1))); cl[:, 4:] = W - 1 - cl[:, 4:]
    return pack(fa, cl, ru)
def setup_inputs_ends(rng):
    h = M // 2; s = np.concatenate([np.arange(h), np.arange(W // 2 - h, W // 2)]); o = np.stack([rng.permutation(s) for g in range(8)])
    for g in (1, 3, 5, 7):
        j = int(np.argmax(o[g])); o[g, j] = o[g, M - 1]; o[g, M - 1] = W // 2 - 1
    pairs = o.reshape(8, N, K); cl = spots(rng, pairs, (1, 3, 5, 7)); cl[N - 1, 7, :, K - 1] = W - 1
    q = np.argsort(rng.random((N, 8, 16)), axis=-1) < 8; q[:, 2] = q[0, 2].copy(); q[:, 6] = q[0, 6].copy()
    n = rng.integers(0, 7, (N, 8, M)); n[:, 3] = rng.integers(1, 7, (N, M)); n[:, 7] = rng.integers(1, 7, (N, M))
    n[:, 3, M - 2:] = 0; n[:, 7, M - 1] = 0
    for g in (2, 6):
        for r in range(N - 1): n[r, g, r * K + int(rng.integers(0, K))] = 8
    flip = rows(rng, n); rec = 63 * (q[:, :, None] ^ flip).astype(np.int64)
    for g in (0, 1, 4, 5):
        for r in range(N):
            if g % 4 == 0:
                k = rng.integers(0, 4, h); k[0] = 0; a = swaps(rng, q[r, g], k)
            else:
                a = flip[r, g, :h].copy(); a[0] = False
            e = a[rng.permutation(h)]
            if g % 4 == 1: a, e = np.concatenate([a, a[:1]]), a[1:]
            t = np.concatenate([q[r, g] ^ a, ~q[r, g] ^ e]); v = 63 * t.astype(np.int64)
            if g % 4 == 0:
                u = rows(rng, rng.integers(0, 8, M)).astype(np.int64); u = u[:, :8] + u[:, 8:]; u[0] = 1; v[~t] = u.reshape(-1)
            rec[r, g] = np.concatenate([v[1:][rng.permutation(M - 1)], v[:1]])
    ru = np.stack([q[k % N] if k % 5 != 4 else ~q[0] for k in range(16)], axis=1)
    rest = 63 * (rng.random((N, 8, W // 2, 16)) < 0.5).astype(np.int64)
    return pack(lay(pairs, rec, rest), cl, 63 * ru.astype(np.int64))
def setup_inputs_corners(rng):
    o = np.stack([rng.permutation(M) for g in range(8)]); o[0] = np.arange(M); o[1] = np.arange(M)[::-1]
    o[1::2] += W // 2 - M; pairs = o.reshape(8, N, K); cl = spots(rng, pairs, ())
    bit = rng.integers(0, 2, (8, N, K)); bit[0] = 0; bit[1] = 1
    for g in (0, 1, 2, 3, 6, 7): cl[:, g] = (2 * pairs[g] + bit[g])[:, None]
    q = np.repeat(rng.choice(np.array([0, 1, 31, 32, 62, 63]), (1, 8, 16)), N, axis=0)
    q = np.where(rows(rng, np.full((N, 8), 2)), off(rng, q, 1, 4), q)
    x = np.repeat(q[:, :, None], W, axis=2); far = rng.integers(3, 6, (N, 8, W, 1)); eq = rng.integers(8, 11, (N, 8, W, 1))
    pos = np.argsort(rng.random(x.shape), axis=-1)
    x = np.where(pos < far, off(rng, x, 2, 3), np.where(pos < 16 - eq, off(rng, x, 1, 2), x))
    x = np.where(rng.random((N, 8, W, 1)) < 0.125, rng.integers(0, 64, x.shape), x)
    x[:, 4:] = np.where(rng.random((N, 4, W, 1)) < 0.03, q[:, 4:, None], x[:, 4:])
    for g, js in ((0, (0,)), (1, (M - 1,)), (2, (M - 2, M - 1)), (3, (K, M - 1))):
        for j in js: x[:, g, int(cl[:, g, 0].reshape(-1)[j])] = q[:, g]
    return pack(x, cl, np.stack([q[k % N] for k in range(16)], axis=1))
def camps(rng, q, n):
    pairs = np.stack([rng.permutation(W // 2)[:M] for g in range(8)]).reshape(8, N, K)
    far = rng.integers(0, 7, (N, 8, N, K)); u = np.argsort(rng.random((N, 8, K)), axis=-1)
    for r in range(N):
        far[r, :, r] = np.where(u[r] < n[:, r, None], 7, 8); far[r, :, (r + 1) % N, K - 1] = 0
    x = np.broadcast_to(q[None, :, None, None], (N, 8, N, K, 16)); rec = np.where(rows(rng, far), off(rng, x, 2, 8), x).reshape(N, 8, M, 16)
    y = np.broadcast_to(q[None, :, None], (N, 8, W // 2, 16)); rest = np.where(rows(rng, rng.integers(0, 7, (N, 8, W // 2))), off(rng, y, 2, 8), y)
    t = np.repeat(q[:, None], 16, axis=1); v = np.where(rows(rng, np.full((8, 16), 2)), off(rng, t, 1, 2), t)
    return lay(pairs, rec, rest), spots(rng, pairs, ()), np.where((np.arange(16) % 2 == 0)[None, :, None], t, v)
def setup_inputs_crowd(rng):
    n = K - rng.integers(0, 2, (8, N)); n[0] = K - 1; n[0, N - 1] = K; n[1] = K; n[2] = 0; n[3] = 0; n[3, 0] = K; n[7] = K; n[7, 0] = K - 1
    q = rng.integers(0, 4, (8, 16)); q[::2] += 60
    x, cl, ru = camps(rng, q, n)
    p = rng.permutation(np.setdiff1d(np.arange(W // 2), cl[:, 1] >> 1))[:M].reshape(N, K)
    cl[:, 1, 16 - N:] = (2 * p + rng.integers(0, 2, p.shape))[:, None]; ru[1, 16 - N:] = q[1]
    for r in range(N):
        far = rng.integers(0, 7, (N, K)); far[0] = rng.integers(0, 5, K); far[r] = 7; far[(r + 1) % N, K - 1] = 0
        v = mix(rng, q[1], far, 2, 8)
        if r == 0:
            u = np.argsort(rng.random((K, 16)), axis=-1); y = np.broadcast_to(q[1], (K, 16))
            v[0] = np.where(u < rng.integers(0, 5, (K, 1)), off(rng, y, 2, 8), np.where(u < 8, off(rng, y, 1, 2), y))
        put(x, r, 1, p, v)
    p = cl[:, 4, 0] >> 1
    for r in range(N):
        far = rng.integers(0, 5, (N, K)); far[(r + 1) % N, K - 1] = 0
        put(x, r, 4, p, mix(rng, q[4], far, 2, 8))
    p = cl[:, 5, 0] >> 1; s = rng.integers(0, 2, W // 2); cl[:, 5] = 2 * (cl[:, 5] >> 1) + s[cl[:, 5] >> 1]
    for r in range(N):
        far = rng.integers(5, 7, (N, K)); far[(r + 1) % N, K - 1] = 0; x[r, 5, 2 * p + s[p]] = mix(rng, q[5], far, 2, 8)
        far = rng.integers(1, 5, (N, K)); far[(r + 1) % N, K - 1] = 0; x[r, 5, 2 * p + 1 - s[p]] = mix(rng, q[5], far, 16, 32)
    p = (cl[:, 6, 0] >> 1).reshape(M); low = q[6] - rng.integers(8, 16, 16)
    for r in range(N):
        v = np.repeat(np.stack([q[6], low]), M // 2, axis=0)
        v = np.clip(v + rows(rng, np.full(M, 2)) * np.where(np.arange(M) < M // 2, 1, -1)[:, None], 0, 63)
        e = rng.permutation(16)[:(4, 12)[r % 2]]; v[rng.permutation(M // 2)[:e.size], e] = low[e]
        put(x, r, 6, p, v)
    return pack(x, cl, ru)
def setup_inputs_calm(rng):
    n = rng.integers(0, 4, (8, N))
    for g in (0, 2, 4, 6): n[g] = rng.permutation(N) % 4
    q = rng.integers(0, 4, (8, 16)); q[1::2] += 60
    return pack(*camps(rng, q, n))
def check_inputs(d):
    bad = []
    for k, lo, hi in (("fa", 0, 63), ("cl", 0, W - 1), ("ru", 0, 63)):
        v = np.asarray(d[k], np.float64)
        if not (np.min(v) >= lo and np.max(v) <= hi): bad.append("range of " + k)
        elif np.any(v != np.floor(v)): bad.append("whole numbers of " + k)
    v = np.asarray(d["ru"], np.float64)
    if np.any(v != v[:1]): bad.append("ru alike on all ranks")
    p = (np.asarray(d["cl"]).astype(np.int64) >> 1).reshape(N, 8, 16, K).transpose(1, 2, 0, 3).reshape(8, 16, M)
    p = np.sort(p, axis=-1)
    if np.any(p[..., 1:] == p[..., :-1]): bad.append("pairs of cl differ in a group and issue")
    return bad
def reference(fa, cl, ru):
    x = np.ascontiguousarray(np.asarray(fa, np.float32).astype(np.int64).reshape(N, 8, 16, W).transpose(0, 1, 3, 2))
    c = cl.astype(np.int64).reshape(N, 8, 16, K)
    b = np.asarray(ru[0], np.float32).astype(np.int64).reshape(8, 16, 16).transpose(0, 2, 1).copy()
    g8 = np.arange(8)[:, None]
    for rnd in range(RO):
        vote = np.zeros((N, 8, 16), np.int64)
        for r in range(N):
            z = x[r][g8[:, :, None], c[r]]
            eq = np.add.reduce((z == b[:, :, None]).astype(np.int64), axis=3)
            vote[r] = np.add.reduce((eq >= 9).astype(np.int64), axis=2)
        court = np.zeros((8, 16), np.int64)
        for g in range(8):
            taken = np.zeros(N, bool)
            for k in range(16):
                if k % N == 0: taken = np.zeros(N, bool)
                court[g, k] = np.argmax(np.where(taken, -1, vote[:, g, k])); taken[court[g, k]] = True
        up = np.zeros((N, 8, 16, K), bool)
        for k in range(16):
            r = court[:, k][:, None]; nm = c[:, :, k].transpose(1, 0, 2).reshape(8, M)
            z = x[r, g8, nm]
            med = np.sort(z, axis=1)[:, M // 2]
            dist = np.add.reduce(np.abs(z - med[:, None]), axis=2)
            b[:, k] = z[np.arange(8), np.argmin(dist, axis=1)]
            diff = b[:, k][:, None] - z
            ok = np.add.reduce((np.abs(diff) <= 1).astype(np.int64), axis=2) >= 12
            x[r, g8, nm] = z + np.where(ok[..., None], np.sign(diff), 0)
            up[:, :, k] = ok.reshape(8, N, K).transpose(1, 0, 2)
        c = np.where(up, c, c ^ 1)
    yb = np.ascontiguousarray(b.transpose(0, 2, 1)).reshape(128, 16).astype(np.float32).astype(BF)
    return {"yf": np.ascontiguousarray(x.transpose(0, 1, 3, 2)).reshape(N, 128, W).astype(np.float32).astype(BF), "yc": c.reshape(N, 128, K).astype(np.float32), "yr": np.stack([yb] * N)}

@@ -1,0 +1,628 @@
+from concourse.bass import DstId, RemoteDMATransfer
+from concourse.mybir import AluOpType as ALU, AxisListType, ActivationFunctionType as AF
+
+W, RO = 7168, 4
+TR = 8192
+CN = float(2 ** 24 + 4)
+CK = float(3 * 2 ** 32)
+CP = float(3 * 2 ** 23)
+BF, F, U, I = "bfloat16", "float32", "uint16", "int32"
+CFG = {"help": [384, 384, 384, 384], "sfull": [11, 12, 13, 14, 15], "per": 3, "st1": 5, "win": 4, "mix": 0}
+
+
+def _sb(n, d):
+    return ("sbuf", [128] + (n if isinstance(n, list) else [n]), d)
+
+
+SCRATCH = {
+    "TB": _sb(TR + W, BF), "Z0": _sb(768, BF), "Z1": _sb(768, BF), "ZS": _sb(768, BF), "JS": _sb(768, BF),
+    "IN": _sb(768, BF), "SC": _sb(768, BF), "DM": _sb(768, BF), "NR": _sb(768, BF), "I0": _sb(768, BF),
+    "I1": _sb(768, BF), "KS": _sb(384, F), "BIG": _sb(384, BF), "SM": _sb(512, F), "SB": _sb(256, BF),
+    "NE": _sb(3072, BF), "SG": _sb(384, BF), "TH": _sb(256, BF), "S1": _sb(32, F), "JU": _sb(4, U),
+    "CL": _sb(192, I), "RU": _sb(16, BF), "YR": _sb(16, BF), "X1": _sb(384, F), "X2": _sb(384, F), "YC": _sb(192, F),
+    "NM": _sb(448, F), "PB": _sb(448, F), "BT": _sb(448, BF), "FI": _sb(448, BF), "VO": _sb(256, U),
+    "L0": _sb(256, U), "L0F": _sb(256, F), "LV": _sb(384, BF), "SN": _sb(768, U),
+    "LN1": _sb([16, 16], U), "LN2": _sb([16, 32], U), "MSG": _sb([80, 16], BF), "FL0": _sb(1024, BF), "FLO": _sb(768, BF),
+    "NM8": _sb(96, F), "GG": _sb(48, F), "OS": _sb(48, U), "O48": _sb(4, U), "N48": _sb(192, U),
+    "OF0": _sb(16, U), "OF1": _sb(8, U), "OF2": _sb(12, U), "QB": _sb(8, BF),
+    "PI": _sb(4, I), "PC": _sb(40, F), "XI": _sb(160, F), "XD": _sb(128, F), "XB": _sb(128, F), "XT": _sb(128, F),
+    "UU": _sb(144, BF), "BP": _sb(128, BF), "BM": _sb(128, BF), "G8": _sb(8, BF), "MA": _sb(384, BF),
+    "MB": _sb(384, BF), "MC": _sb(384, BF), "IDX": _sb(768, BF), "W32": _sb(128, BF), "ONE": _sb(8, BF),
+    "CR": _sb(8, F), "C48": _sb(4, F), "SL": _sb(128, U),
+    "D0": ("psum", [128, 512], F), "D1": ("psum", [128, 512], F), "CT": ("psum", [128, 512], F),
+    "VA": ("psum", [128, 512], F), "VB": ("psum", [128, 512], F), "PW": ("psum", [128, 512], F),
+    "PK": ("psum", [128, 512], F), "PQ": ("psum", [128, 512], F),
+}
+POOL = {"v": 44, "s": 28, "t": 20, "y": 10, "g": 9}
+ARR = ["n0"] + ["%s%d" % (k, r) for r in range(RO) for k in ("va", "vb", "vc", "nb", "nc", "fa", "fb", "fc", "fd")]
+SEMAPHORES = ["%s%d" % (q, i) for q in POOL for i in range(POOL[q])] + ["r" + a for a in ARR] + ["sent"]
+
+
+def rank_program(g, core, T, topo):
+    me = T.rank_of(core)
+    if me is None:
+        return
+    N = len(T.cores)
+    peers = [r for r in range(N) if r != me]
+    Q = {"v": g.vector, "s": g.scalar, "t": g.tensor, "y": g.sync, "g": g}
+    ops = []
+    seen = {}
+
+    def A(name, *ix, p=None):
+        shape = SCRATCH[name][1][1:]
+        ix = list(ix) + [slice(None)] * (len(shape) - len(ix))
+        rows = [0]
+        for i, n in zip(ix[:-1], shape[:-1]):
+            rows = [r * n + j for r in rows for j in (range(n)[i] if isinstance(i, slice) else [i])]
+        rg = range(shape[-1])[ix[-1]] if isinstance(ix[-1], slice) else range(ix[-1], ix[-1] + 1)
+        row = ((1 << len(rg)) - 1) << rg[0] if rg.step == 1 else sum(1 << j for j in rg)
+        m = 0
+        for r in rows:
+            m |= row << (r * shape[-1])
+        if SCRATCH[name][0] == "psum":
+            m = 1
+        ps = slice(None) if p is None else slice(p[0], p[1])
+        return (T[name][tuple([ps] + ix)], [(name, m)])
+
+    def C(name, a, n=1, p=None, step=1):
+        return A(name, slice(a, a + n * step - step + 1, step) if step > 1 else slice(a, a + n), p=p)
+
+    def ind(win, off):
+        return (win[0].indirect(off[0]), win[1] + off[1], off[1])
+
+    def ap(x):
+        return x[0] if isinstance(x, tuple) else x
+
+    def rec(q, calls, outs, ins, inc=1, fixed=None):
+        n = len(ops)
+        acc = []
+        for o in outs:
+            if len(o) == 3:
+                acc += [(r, False) for r in o[2]] + [(o[1][0], True)]
+            else:
+                acc += [(r, True) for r in o[1]]
+        for x in ins:
+            if isinstance(x, tuple):
+                acc += [(r, False) for r in x[1]]
+        deps = set()
+        for (name, m), wr in acc:
+            psum = SCRATCH[name][0] == "psum"
+            for e in seen.setdefault(name, []):
+                if e[0] & m and e[1] != n:
+                    if psum and q == "t" and e[3] == "t":
+                        continue
+                    if wr or e[2] or (psum and e[3] != q):
+                        deps.add(e[1])
+        for (name, m), wr in acc:
+            psum = SCRATCH[name][0] == "psum"
+            if psum:
+                seen[name] = [e for e in seen[name] if e[3] == q]
+            elif wr:
+                seen[name] = [e for e in seen[name] if e[0] & ~m]
+            seen[name].append([m, n, wr, q])
+        ops.append([q, calls, deps, inc, fixed])
+        return n
+
+    def ts(o, x, s1, op0, s2=None, op1=None):
+        if op1 is None:
+            rec("v", [lambda: g.vector.tensor_scalar(o[0], x[0], ap(s1), None, op0)], [o], [x, s1])
+        else:
+            rec("v", [lambda: g.vector.tensor_scalar(o[0], x[0], ap(s1), ap(s2), op0, op1)], [o], [x, s1, s2])
+
+    def tt(o, x, y, op):
+        rec("v", [lambda: g.vector.tensor_tensor(o[0], x[0], y[0], op)], [o], [x, y])
+
+    def cp(o, x):
+        rec("v", [lambda: g.vector.tensor_copy(o[0], x[0])], [o], [x])
+
+    def red(o, x, op):
+        rec("v", [lambda: g.vector.tensor_reduce(o[0], x[0], AxisListType.X, op)], [o], [x])
+
+    def scan(o, x, y, init, op0, op1):
+        rec("v", [lambda: g.vector.tensor_tensor_scan(o[0], x[0], y[0], ap(init), op0, op1)], [o], [x, y, init])
+
+    def fill(o, c):
+        rec("v", [lambda: g.vector.memset(o[0], c)], [o], [])
+
+    def vtr(o, x):
+        rec("v", [lambda: g.vector.transpose(o[0], x[0])], [o], [x])
+
+    def act(o, x, f, bias=0.0, scale=1.0, acc=None):
+        if acc is None:
+            rec("s", [lambda: g.scalar.activation(o[0], x[0], f, bias=ap(bias), scale=scale)], [o], [x, bias])
+        else:
+            rec("s", [lambda: g.scalar.activation(o[0], x[0], f, bias=ap(bias), scale=scale, accum_out=acc[0])],
+                [o, acc], [x, bias])
+
+    def mm(items):
+        def one(o, l, r, a, b):
+            return lambda: g.tensor.matmul(o[0], l[0], r[0], a, b)
+        rec("t", [one(*it) for it in items], [it[0] for it in items], [x for it in items for x in it[1:3]])
+
+    def iota(o, pattern, base=0, ch=0, flag=True):
+        if flag:
+            rec("g", [lambda: g.iota(o[0], pattern, base, ch, allow_small_or_imprecise_dtypes=True)], [o], [])
+        else:
+            rec("g", [lambda: g.iota(o[0], pattern, base, ch)], [o], [])
+
+    def dma(o, x):
+        outs = [o] if isinstance(o, tuple) else []
+        return rec("y", [lambda: g.sync.dma_start(ap(o), ap(x))], outs, [x], inc=16)
+
+    def dst_id(r):
+        rid, pid = topo.addr(T.cores[r])[0:2]
+        return DstId(rid=rid, pnc=pid)
+
+    def engines(a):
+        es = None
+        for r in range(N):
+            if r != a:
+                e = topo.engines(T.cores[a], T.cores[r])
+                es = e if es is None else [x for x in es if x in e]
+        return es
+
+    def shares(a):
+        es = engines(a)
+        k = len(es) // 4
+        ps = [r for r in range(N) if r != a]
+        return {ps[0]: es[0:k], ps[1]: es[k:2 * k], ps[2]: es[2 * k:4 * k]}
+
+    sent = [0]
+
+    def send_all(tag, src, slot):
+        es = engines(me)
+        m = sum(1 << e for e in es)
+        sem = T.sem["r" + tag]
+        rec("g", [lambda: g.remote_dma_fused([RemoteDMATransfer(
+            dst_ids=[dst_id(r) for r in peers], dma_engine_mask=m, remote_sem=sem, srcs=[src[0]],
+            dsts=[slot(me)[0] for r in peers])], local_sem=T.sem.sent)], [], [src], inc=0)
+        sent[0] += len(es)
+        rec("r", [], [slot(r) for r in peers], [], fixed=("r" + tag, sum(len(engines(r)) for r in peers)))
+
+    def send_each(tag, src, slot):
+        sh = shares(me)
+        sem = T.sem["r" + tag]
+        rec("g", [lambda: g.remote_dma_fused([RemoteDMATransfer(
+            dst_ids=[dst_id(r)], dma_engine_mask=sum(1 << e for e in sh[r]), remote_sem=sem, src=src(r)[0],
+            dst=slot(me)[0]) for r in peers], local_sem=T.sem.sent)], [], [src(r) for r in peers], inc=0)
+        sent[0] += sum(len(sh[r]) for r in peers)
+        rec("r", [], [slot(r) for r in peers], [], fixed=("r" + tag, sum(len(shares(r)[me]) for r in peers)))
+
+    nsm = [0, 0]
+
+    def sm(n=1):
+        if nsm[0] + n > 512:
+            nsm[0] = 0
+        nsm[0] += n
+        return nsm[0] - n
+
+    def sb():
+        nsm[1] = (nsm[1] + 2) % 256
+        return C("SB", nsm[1])
+
+    def run(lst, n=None):
+        for _ in range(len(lst) if n is None else min(n, len(lst))):
+            f = lst.pop(0)
+            if f:
+                f()
+
+    TBr, TBw = C("TB", 0, W), C("TB", 0, TR + W)
+
+    dma(A("CL"), T.cl[:])
+    dma(A("RU"), T.ru[:])
+    dma(TBr, T.fa[:])
+    iota(C("PI", 0), [[1, 1]], 0, 1, False)
+    iota(C("XT", 0, 24), [[16, 12], [0, 2]])
+    iota(A("XI"), [[1, 160]])
+    iota(A("XD"), [[1, 8], [0, 16]])
+    iota(C("XT", 24, 16), [[16, 4], [64, 4]])
+    iota(A("XB"), [[1, 8], [32, 4], [0, 4]])
+    iota(C("XT", 40, 24), [[1, 12], [0, 2]])
+    ts(C("PI", 1), C("PI", 0), 15, ALU.bitwise_and)
+    ts(C("PI", 2), C("PI", 0), 16, ALU.bitwise_and)
+    ts(C("PI", 3), C("PI", 0), 4, ALU.arith_shift_right)
+    fill(C("LV", 96 * me, 96), 0.0)
+    cp(C("PC", 0, 4), A("PI"))
+    fill(C("LV", 96 * me, 96, p=(96, 128)), float(N - me))
+    pcol, acol, ggc, gcol = [C("PC", i) for i in range(4)]
+    ts(C("SL", 0, 24), C("XT", 0, 24), acol, ALU.add)
+    ts(C("PC", 4), acol, 11.0, ALU.min, 32.0, ALU.mult)
+    fill(A("ONE"), 1.0)
+    ts(C("SL", 24, 16), C("XI", 0, 16), C("PC", 4), ALU.add, ggc, ALU.add)
+    ts(A("G8"), C("XI", 0, 8), gcol, ALU.is_equal)
+    ts(C("PC", 5, 3), C("XI", 0, 3), -8.0, ALU.mult, pcol, ALU.add)
+    ts(C("PC", 32, 3), C("XI", 0, 3), -4.0, ALU.mult, pcol, ALU.add)
+    ts(C("PC", 11, 3), C("XI", 0, 3), 64.0, ALU.mult, acol, ALU.add)
+    ts(C("PC", 35, 4), C("XI", 0, 4), 16.0, ALU.mult, acol, ALU.add)
+    ts(C("PC", 8, 3), C("PC", 32, 3), 1.0 / 16, ALU.mult)
+    ts(C("PC", 14, 4), C("PC", 35, 4), -192.0, ALU.add)
+    fill(A("W32"), 1.0 / 32)
+    cp(A("X1"), ind(A("CL"), C("SL", 0, 24)))
+    vtr(A("X2"), A("X1"))
+    ts(C("PC", 18), gcol, 16.0, ALU.mult, 15.0, ALU.add)
+    cp(C("L0", 64 * me, 64), ind(A("X2"), C("SL", 24, 4)))
+    send_all("n0", C("L0", 64 * me, 64), lambda r: C("L0", 64 * r, 64))
+    iota(A("IDX", p=(0, 32)), [[0, 3], [1, 256]])
+    iota(A("IDX", p=(32, 64)), [[256, 3], [0, 256]], -384)
+    cp(C("NM", 256, 192), ind(A("X2"), C("SL", 28, 12)))
+    cp(C("VO", 0, 64), C("L0", 64 * me, 64))
+    cp(C("VO", 64, 192), C("NM", 256, 192))
+    for q in range(3):
+        ts(C("MA", 128 * q, 128), A("XD"), C("PC", 5 + q), ALU.is_equal, 4.0, ALU.mult)
+    ts(C("PC", 20, 3), C("XI", 0, 3), 4.0, ALU.mult, acol, ALU.add)
+    act(A("MA", p=(96, 128)), A("X1", p=(96, 128)), AF.Identity, bias=1.0 / 32, scale=0.0)
+    ts(C("PC", 24, 3), C("PC", 20, 3), 12.0, ALU.is_ge, 4.0, ALU.mult)
+    ts(C("PC", 20, 3), C("XI", 0, 3), 20.0, ALU.mult, acol, ALU.add)
+    ts(C("SL", 40, 16), C("XT", 24, 16), acol, ALU.add)
+    tt(C("PC", 24, 3), C("PC", 24, 3), C("PC", 20, 3), ALU.add)
+    ts(A("BM"), A("XD"), gcol, ALU.is_equal, -1024.0, ALU.mult)
+    ts(C("C48", 0, 3), C("PC", 24, 3), 1.0 / 64, ALU.mult, -3.0, ALU.add)
+    ts(A("BP"), A("XD"), gcol, ALU.is_equal, 2048.0, ALU.mult)
+    ts(A("UU"), C("XI", 0, 144), C("PC", 18), ALU.is_equal)
+    fill(C("CR", 0, 4), CN - 64.0)
+    fill(C("CR", 4, 1), CN - 129.0)
+    act(A("BIG"), A("X1"), AF.Identity, bias=1e9, scale=0.0)
+    act(A("MSG", slice(0, 80), slice(13, 16)), C("X1", 0, 240), AF.Identity, bias=0.0, scale=0.0)
+    for q in range(3):
+        ts(C("MB", 128 * q, 128), A("XB"), C("PC", 5 + q), ALU.is_equal, 4.0, ALU.mult)
+    for q in range(2):
+        ts(C("MC", 128 * q, 128), A("XD"), C("PC", 8 + q), ALU.is_equal)
+    ts(C("PC", 27), acol, 16.0 * me, ALU.add)
+    act(A("MB", p=(96, 128)), A("X1", p=(96, 128)), AF.Identity, bias=1.0 / 32, scale=0.0)
+    ts(C("SL", 56, 4), C("XI", 0, 4), 64.0, ALU.mult, C("PC", 27), ALU.add)
+
+    def bases(lo, n):
+        return [lambda: ts(C("PB", lo, n), C("NM", lo, n), -0.5, ALU.add, CP, ALU.add),
+                lambda: ts(C("VB", 64 + lo, n), C("PB", lo, n), -CP, ALU.add),
+                lambda: tt(C("BT", lo, n), C("NM", lo, n), C("VB", 64 + lo, n), ALU.subtract)]
+    run(bases(256, 192))
+    late = bases(0, 256)
+    first0 = [lambda: cp(A("L0F"), A("L0")), lambda: cp(C("NM", 0, 256), ind(A("L0F"), C("SL", 40, 16)))]
+    ends = [
+        lambda: ts(C("PC", 28), acol, 48.0, ALU.mult, 16.0 * me - 192.0, ALU.add),
+        lambda: ts(C("PC", 30), acol, 16.0, ALU.mult, 192.0, ALU.add),
+        lambda: ts(C("PC", 29), acol, 4.0, ALU.is_lt, C("PC", 28), ALU.mult),
+        lambda: ts(C("PC", 31), acol, ggc, ALU.add),
+        lambda: ts(C("SL", 60, 24), C("XT", 40, 24), C("PC", 29), ALU.add, C("PC", 30), ALU.add),
+        lambda: ts(C("SL", 84, 12), C("XI", 0, 12), 32.0, ALU.mult, C("PC", 31), ALU.add),
+    ]
+
+    def rul(rnd, k):
+        if rnd == 0:
+            return C("RU", k)
+        return C("FI", 64 * k + 12) if k < 4 else C("FI", 192 + 16 * k + 12)
+
+    def vote_v(rnd, k):
+        ts(C("NE", 192 * k, 192), ind(TBr, C("VO", 16 * k, 12)), rul(rnd, k), ALU.not_equal)
+
+    def vote_s(rnd, k):
+        t = C("SG", 192 * (k % 2), 192)
+        act(t, ind(TBr, C("VO", 16 * k, 12)), AF.Sign, bias=rul(rnd, k), scale=-1.0)
+        act(C("NE", 192 * k, 192), t, AF.Square)
+
+    def vote_m(rnd, k):
+        act(C("NE", 192 * k, 192), ind(TBr, C("VO", 16 * k, 12)), AF.Sign, bias=rul(rnd, k), scale=-1.0)
+
+    def vote_mm(bank, k, k0, n):
+        mm([(C(bank, 8 * (n * h + k - k0), 8, p=(0, 96)), C("NE", 192 * k + 96 * h, 96), A("G8"), True, True)
+            for h in range(2)])
+
+    def vote_send(off, bank, n, th, tag):
+        act(C("TH", th, 16 * n, p=(0, 96)), C(bank, 0, 16 * n, p=(0, 96)), AF.Sign, bias=7.5, scale=-1.0)
+        mm([(C("PW", 0, 1, p=(0, 8 * n)), C("TH", th + 8 * n * h, 8 * n, p=(0, 96)), C("ONE", 0, 1, p=(0, 96)),
+             h == 0, h == 1) for h in range(2)])
+        act(C("LV", 96 * me + off, 1, p=(0, 8 * n)), C("PW", 0, 1, p=(0, 8 * n)), AF.Identity, bias=96.0, scale=0.5)
+        send_all(tag, C("LV", 96 * me + off, 4), lambda r: C("LV", 96 * r + off, 4))
+
+    def courts(off, mat, bank):
+        c = sm(32)
+        K = [C(bank, 4 * q, 4) for q in range(3)]
+        m0, m1, m2 = C("SM", c), C("SM", c + 1), C("SM", c + 2)
+        al0, al1, k1, k2p, k2, pre = [C("SM", c + 4 + 4 * i, 4) for i in range(6)]
+        return [
+            lambda: mm([(K[q], C(mat, 128 * q, 128), C("LV", off, 4, step=96), True, True) for q in range(3)]),
+            lambda: red(m0, K[0], ALU.max),
+            lambda: ts(al0, K[0], m0, ALU.not_equal, 3.0, ALU.mult),
+            lambda: tt(k1, K[1], al0, ALU.mult),
+            lambda: tt(k2p, K[2], al0, ALU.mult),
+            lambda: red(m1, k1, ALU.max),
+            lambda: ts(al1, k1, m1, ALU.not_equal, 2.0, ALU.mult),
+            lambda: tt(k2, k2p, al1, ALU.mult),
+            lambda: tt(pre, al0, al1, ALU.add),
+            lambda: red(m2, k2, ALU.max),
+        ], c
+
+    def update(b, rnd):
+        if b == 0:
+            lo, n = 0, 256
+            put = [(lambda r=r: cp(ind(C("FI", 0, 256), C("OF0", 4 * r, 4)), C("FL0", 256 * rnd + 64 * r, 64)))
+                   for r in range(N)]
+            vo = lambda: cp(C("VO", 0, 64), ind(C("NM", 0, 256), C("SL", 56, 4)))
+        else:
+            lo, n = 192 + 64 * b, 64
+            put = [lambda: cp(ind(C("FI", lo, n), C("OF2", 4 * b - 4, 4)), C("FLO", 192 * rnd + 64 * b - 64, 64))]
+            vo = lambda: cp(C("VO", 64 * b, 64), C("NM", lo, 64))
+        return put + [
+            lambda: tt(C("BT", lo, n), C("FI", lo, n), C("BT", lo, n), ALU.not_equal),
+            lambda: tt(C("NM", lo, n), C("BT", lo, n), C("VB", 64 + lo, n), ALU.add),
+        ] + ([vo] if rnd < RO - 1 else [])
+
+    def seg(rnd, b, r):
+        row = slice(4 * rnd, 4 * rnd + 4) if r is None else 4 * rnd + r
+        return A("LN1", row, slice(0, 12)) if b == 1 else A("LN2", row, slice(16 * b - 32, 16 * b - 20))
+
+    def compact(rnd, b):
+        cp(C("N48", 48 * b, 48), seg(rnd, b, None))
+
+    def stale(rnd, b, steps):
+        if b == 1:
+            for r in range(N):
+                act(C("ZS", 192 * r, 192), ind(TBr, seg(rnd, b, r)), AF.Identity, bias=64.0)
+        else:
+            act(A("ZS"), ind(TBr, C("N48", 48 * b, 48)), AF.Identity, bias=64.0)
+        t = 95.5
+        for d in (16.0, 8.0, 4.0, 2.0, 1.0)[:steps]:
+            c = sm(2)
+            act(A("JS"), A("ZS"), AF.Sign, bias=t, scale=-1.0, acc=C("SM", c))
+            act(C("SM", c + 1), C("SM", c), AF.Sign, bias=0.5, scale=-1.0)
+            t2 = sb()
+            act(t2, C("SM", c + 1), AF.Identity, bias=t, scale=d)
+            t = t2
+        if steps == 5:
+            return t, 0.5, [None, 0.5]
+        return t, 0.25, [None, 0.25, 0.5]
+
+    def idx_mm():
+        for h in range(2):
+            mm([(C("D%d" % h, 0, 384), A("W32", p=(0, 64)), C("IDX", 384 * h, 384, p=(0, 64)), True, False)])
+
+    def hearing(rnd, b, st, small, later, big, hook):
+        h = 4 * rnd + b
+        z = "Z%d" % (h % 2)
+        Z = A(z)
+        n8 = C("NM8", 48 * (h % 2), 48)
+        ts(C(z, 0, 384), ind(TBr, C("N48", 48 * b, 24)), 64.0, ALU.add)
+        act(C(z, 384, 384), ind(TBr, C("N48", 48 * b + 24, 24)), AF.Identity, bias=64.0)
+        ts(n8, C("N48", 48 * b, 48), 1.0 / TR, ALU.mult)
+        for hf in range(2):
+            mm([(C("D%d" % hf, 0, 384), A("BM"), C(z, 384 * hf, 384), False, False)])
+        ns = CFG["help"][b]
+        nv = 768 - ns
+        if not ns:
+            run(small)
+            hook("gather")
+        if b == 0:
+            w, a, scales = 95.5, 79.5 / 32, [None, 1.0 / 32, 1.0 / 16, 0.125, 0.25, 0.5]
+        else:
+            w, a, scales = st
+        for n, s in enumerate(scales):
+            hook(n)
+            if ns:
+                c = sm()
+                act(C("JS", 0, ns), C(z, nv, ns), AF.Sign, bias=w, scale=-(s or 1.0), acc=C("SM", c))
+            if s is None:
+                ts(C("IN", 0, nv), C(z, 0, nv), w, ALU.is_gt)
+                if b:
+                    a, f = C("SM", sm()), a
+                    ts(a, w, f, ALU.mult, -0.5, ALU.add)
+                else:
+                    run(small, 1)
+            else:
+                ts(C("IN", 0, nv), C(z, 0, nv), s, ALU.mult, w, ALU.is_gt)
+                a = C("SM", sm())
+                ts(a, w, 2.0, ALU.mult, -0.5, ALU.add)
+            w = sb()
+            if ns:
+                scan(C("SC", 0, nv), C("IN", 0, nv), C("IN", 0, nv), -float(nv), ALU.add, ALU.add)
+                run(small, CFG["per"])
+                ts(w, C("SC", nv - 1), C("SM", c), ALU.is_ge, a, ALU.add)
+            else:
+                scan(C("SC", 0, 384), C("IN", 0, 384), C("IN", 384, 384), -383.5, ALU.add, ALU.add)
+                run(small, 1)
+                ts(w, C("SC", 383), 0.0, ALU.is_gt, a, ALU.add)
+            run(small, 1)
+        run(small)
+        if ns:
+            hook("gather")
+        small += later[0]
+        if b == 3:
+            act(A("I0"), Z, AF.Identity, bias=-64.0)
+        for hf in range(2):
+            ts(C("DM", 384 * hf, 384), C(z, 384 * hf, 384), w, ALU.max)
+            mm([(C("D%d" % hf, 0, 384), A("BP"), C("DM", 384 * hf, 384), False, True)])
+        run(big[0])
+        c = sm(2)
+        red(C("SM", c), C("D0", 0, 384), ALU.min)
+        run(small, 1)
+        scan(A("KS"), C("D1", 0, 384), A("BIG"), C("SM", c), ALU.min, ALU.min)
+        run(small, 1)
+        key = C("KS", 383)
+        ts(C("SM", c + 1), key, CK, ALU.add, CK, ALU.subtract)
+        run(small, 1)
+        ju = C("JU", 2 * (h % 2))
+        ts(ju, key, C("SM", c + 1), ALU.subtract, 384.0, ALU.add)
+        run(small, 1)
+        s1 = 16 * (h % 2)
+        ts(C("S1", s1, 16), ind(Z, ju), -1.0, ALU.mult, CN, ALU.add)
+        run(small, 1)
+        ts(A("NR"), Z, C("S1", s1), ALU.add, CN, ALU.is_equal)
+        mm([(C("CT", 0, 48), C("UU", 15 - a_, 128), C("NR", a_, 48, step=16), a_ == 0, a_ == 15) for a_ in range(16)])
+        tt(A("MSG", slice(5 * h, 5 * h + 5), 12), C("CR", 0, 5), C("S1", s1, 5), ALU.subtract)
+        run(small, 1)
+        if b == 3:
+            act(A("I1"), A("I0"), AF.Sign, bias=A("MSG", 5 * h, slice(12, 13)), scale=-1.0)
+        else:
+            ts(A("I0"), Z, -128.0, ALU.add, A("MSG", 5 * h + 4, slice(12, 13)), ALU.min)
+            ts(A("I1"), Z, A("MSG", 5 * h, slice(12, 13)), ALU.subtract, 65.0, ALU.max)
+        run(big[1])
+        small += later[1]
+        fl = A("MSG", slice(5 * h, 5 * h + 4), slice(0, 12))
+        ts(fl, C("CT", 0, 48), 11.5, ALU.is_lt)
+        run(small, 1)
+        tt(A("GG"), fl, n8, ALU.add)
+        run(small, 1)
+        ts(A("OS"), A("GG"), float(TR), ALU.mult)
+        run(small)
+        tag = "f%s%d" % ("abcd"[b], rnd)
+        if b == 0:
+            whole = A("MSG", slice(5 * h, 5 * h + 4))
+            send_all(tag, whole, lambda r: C("FL0", 256 * rnd + 64 * r, 64))
+            dma(C("FL0", 256 * rnd + 64 * me, 64), whole)
+        else:
+            base = 192 * rnd + 64 * b - 64
+            send_each(tag, lambda r: A("MSG", 5 * h + r), lambda r: C("FLO", base + 16 * r, 16))
+            dma(C("FLO", base + 16 * me, 16), A("MSG", 5 * h + me))
+        tt(ind(TBw, A("OS")), A("I0"), A("I1"), ALU.add)
+        if h + 1 < 4 * RO:
+            idx_mm()
+
+    idx_mm()
+    SF = CFG["sfull"]
+    for rnd in range(RO):
+        vote_s(rnd, 3)
+        for k in range(3):
+            vote_v(rnd, k)
+        for k in (0, 3, 1, 2):
+            vote_mm("VA", k, 0, 4)
+        vote_s(rnd, 7)
+        vote_send(8 * rnd, "VA", 4, 0, "va%d" % rnd)
+        for k in (4, 5, 6):
+            vote_v(rnd, k)
+        vote_s(rnd, SF[0])
+        for k in (7, 4, 5, 6):
+            vote_mm("VB", k, 4, 4)
+        vote_send(32 + 8 * rnd, "VB", 4, 64, "vb%d" % rnd)
+        run(update(3, rnd - 1) if rnd else first0)
+        vk = [k for k in range(8, 16) if k not in SF]
+        for k in vk:
+            vote_v(rnd, k)
+        for k in SF[1:]:
+            vote_s(rnd, k)
+        early = SF[:1] + vk[:-1]
+        for k in early:
+            vote_mm("VA", k, 8, 8)
+        ca, c = courts(8 * rnd, "MA", "PK")
+        cb, d = courts(32 + 8 * rnd, "MA", "PQ")
+        run(ca, 1)
+        for k in vk[-1:] + SF[1:-1]:
+            vote_mm("VA", k, 8, 8)
+        run(cb, 1)
+        vote_mm("VA", SF[-1], 8, 8)
+
+        def names1(rnd=rnd):
+            cp(C("SN", 192 * rnd, 64), ind(C("NM", 256, 64), C("OF2", 0, 4)))
+            send_each("nb%d" % rnd, lambda r: C("SN", 192 * rnd + 16 * r, 16), lambda r: A("LN1", 4 * rnd + r))
+            dma(A("LN1", 4 * rnd + me), C("SN", 192 * rnd + 16 * me, 16))
+
+        def last_of(d):
+            return lambda: ts(C("SM", d + 28, 4), C("SM", d + 20, 4), C("SM", d + 2), ALU.not_equal, -3.0, ALU.add)
+
+        cb += [last_of(d), lambda d=d: tt(C("SM", d + 28, 4), C("SM", d + 28, 4), C("SM", d + 24, 4), ALU.add),
+               lambda d=d: ts(C("OF2", 0, 4), C("SM", d + 28, 4), 16.0, ALU.mult, acol, ALU.add), names1]
+        qme = C("SM", c + 3)
+        ca += [lambda: ts(qme, C("SM", c + 20 + me), C("SM", c + 2), ALU.not_equal, C("SM", c + 24 + me), ALU.add),
+               lambda: ts(C("O48", 0, 3), C("C48", 0, 3), qme, ALU.add, 64.0, ALU.mult),
+               lambda: cp(C("N48", 0, 48), ind(C("NM", 0, 256), C("O48", 0, 3)))]
+        run(ca, len(ca) - CFG["mix"])
+        while ca:
+            run(cb, 1)
+            run(ca, 1)
+        lists0 = [lambda c=c: ts(C("SM", c + 28, 4), C("SM", c + 20, 4), C("SM", c + 2), ALU.not_equal),
+                  lambda c=c: tt(C("SM", c + 28, 4), C("SM", c + 28, 4), C("SM", c + 24, 4), ALU.add)]
+        lists0 += [(lambda m=m, c=c: ts(C("OF0", m, 4, step=4), C("SM", c + 28, 4), 64.0, ALU.mult, C("PC", 14 + m),
+                                        ALU.add)) for m in range(4)]
+        cc, e = courts(64 + 8 * rnd, "MB", "PK")
+        st = [None]
+
+        def names2(rnd=rnd):
+            base = 192 * rnd + 64
+            cp(C("SN", base, 128), ind(C("NM", 320, 128), A("OF1")))
+            send_each("nc%d" % rnd, lambda r: C("SN", base + 32 * r, 32), lambda r: A("LN2", 4 * rnd + r))
+            dma(A("LN2", 4 * rnd + me), C("SN", base + 32 * me, 32))
+
+        def bcast(e=e):
+            tt(C("QB", 0, 4), C("SM", e + 28, 4), C("SM", e + 24, 4), ALU.add)
+            mm([(C("PQ", 4 * x, 4), C("MC", 128 * x, 128), C("QB", 0, 4), True, True) for x in range(2)])
+
+        first = cc.pop(0)
+        cc += [last_of(e), bcast]
+        cc += [(lambda x=x: ts(C("OF1", x, 4, step=2), C("PQ", 4 * x, 4), 16.0, ALU.mult, C("PC", 11 + x), ALU.add))
+               for x in range(2)]
+        cc += [lambda: ts(C("OF2", 4, 8), C("PQ", 0, 8), 16.0, ALU.mult, acol, ALU.add), names2,
+               lambda rnd=rnd: compact(rnd, 1)]
+        small = cb + lists0[:2]
+
+        def hook0(n, rnd=rnd, small=small, cc=cc, first=first, st=st):
+            if n == 1:
+                vote_send(64 + 8 * rnd, "VA", 8, 128, "vc%d" % rnd)
+            if n == 5:
+                first()
+            if n == "gather":
+                st[0] = stale(rnd, 1, CFG["st1"])
+
+        hearing(rnd, 0, None, small, [cc, []], [[lambda: run(small, CFG["win"])], [lambda: run(small, 2)]], hook0)
+        u0, u1, u2 = update(0, rnd), update(1, rnd), update(2, rnd)
+        plan = {1: (lists0[2:] + [lambda: compact(rnd, 2)], [[], []], [u0[0:1] + late[0:1], u0[1:2] + late[1:2]]),
+                2: ([lambda: compact(rnd, 3)] + ends, [[], []], [u0[2:3] + late[2:3], u0[3:4]]),
+                3: ([], [u1[1:], u2[2:]], [u1[0:1], [u2[0], u0[4], u2[1], u0[5]] + u0[6:]])}
+        late, ends = [], []
+        for b in range(1, 4):
+            def hook(n, b=b, rnd=rnd, st=st):
+                if n == "gather" and b < 3:
+                    st[0] = stale(rnd, b + 1, 5)
+            hearing(rnd, b, st[0], plan[b][0], plan[b][1], plan[b][2], hook)
+
+    outs = [dma(T.yf[:], TBr)]
+    run(update(3, RO - 1))
+    cp(C("YR", 0, 4), C("FI", 12, 4, step=64))
+    cp(C("YR", 4, 12), C("FI", 268, 12, step=16))
+    outs.append(dma(T.yr[:], A("YR")))
+    cp(A("X1"), ind(A("NM"), C("SL", 60, 24)))
+    vtr(A("X2"), A("X1"))
+    cp(A("YC"), ind(A("X2"), C("SL", 84, 12)))
+    outs.append(dma(T.yc[:], A("YC")))
+    ops.append(["y", [], set(outs), 0, None])
+
+    known = {q: 0 for q in Q}
+    implies, waits, needed = [], [], set()
+    for n, (q, calls, deps, inc, fixed) in enumerate(ops):
+        ws = []
+        if q != "r":
+            for x in sorted(deps, reverse=True):
+                if not known[q] >> x & 1:
+                    ws.append(x)
+                    needed.add(x)
+                    known[q] |= implies[x]
+            implies.append(known[q] | 1 << n)
+        else:
+            implies.append(1 << n)
+        waits.append(ws)
+    known = {q: 0 for q in Q}
+    last = {q: [None] * POOL[q] for q in POOL}
+    count = {}
+    token = {}
+    for n, (q, calls, deps, inc, fixed) in enumerate(ops):
+        if q == "r":
+            token[n] = fixed
+            continue
+        for x in waits[n]:
+            Q[q].wait_ge(T.sem[token[x][0]], token[x][1])
+            known[q] |= implies[x]
+        if n in needed:
+            free = [i for i, x in enumerate(last[q]) if x is None or known[q] >> x & 1]
+            if not free:
+                i = min(range(POOL[q]), key=lambda j: last[q][j])
+                x = last[q][i]
+                Q[q].wait_ge(T.sem[token[x][0]], token[x][1])
+                known[q] |= implies[x]
+                free = [i]
+            name = "%s%d" % (q, free[0])
+            last[q][free[0]] = n
+            count[name] = count.get(name, 0) + inc * len(calls)
+            token[n] = (name, count[name])
+            for f in calls:
+                f().then_inc(T.sem[name], inc)
+        else:
+            for f in calls:
+                f()
+    g.wait_ge(T.sem.sent, sent[0])

@@ -7,7 +7,7 @@ CN = float(2 ** 24 + 4)
 CK = float(3 * 2 ** 32)
 CP = float(3 * 2 ** 23)
 BF, F, U, I = "bfloat16", "float32", "uint16", "int32"
-CFG = {"help": [384, 384, 384, 384], "sfull": [11, 12, 13, 14, 15], "per": 3, "st1": 5, "win": 4, "mix": 0}
+CFG = {"help": [384, 384, 384, 384], "sfull": [11, 10, 12, 13, 14], "per": 1, "pa": 1, "hs": [2, 1, 1, 2], "st1": 6, "st": 6, "win": 2, "mix": 4, "cb": 4}
 
 
 def _sb(n, d):
@@ -16,8 +16,8 @@ def _sb(n, d):
 
 SCRATCH = {
     "TB": _sb(TR + W, BF), "Z0": _sb(768, BF), "Z1": _sb(768, BF), "ZS": _sb(768, BF), "JS": _sb(768, BF),
-    "IN": _sb(768, BF), "SC": _sb(768, BF), "DM": _sb(768, BF), "NR": _sb(768, BF), "I0": _sb(768, BF),
-    "I1": _sb(768, BF), "KS": _sb(384, F), "BIG": _sb(384, BF), "SM": _sb(512, F), "SB": _sb(256, BF),
+    "IN": _sb(1536, BF), "SC": _sb(768, BF), "DM": _sb(768, BF), "NR": _sb(768, BF), "I0": _sb(768, BF),
+    "I1": _sb(768, BF), "SM": _sb(512, F), "SB": _sb(256, BF),
     "NE": _sb(3072, BF), "SG": _sb(384, BF), "TH": _sb(256, BF), "S1": _sb(32, F), "JU": _sb(4, U),
     "CL": _sb(192, I), "RU": _sb(16, BF), "YR": _sb(16, BF), "X1": _sb(384, F), "X2": _sb(384, F), "YC": _sb(192, F),
     "NM": _sb(448, F), "PB": _sb(448, F), "BT": _sb(448, BF), "FI": _sb(448, BF), "VO": _sb(256, U),
@@ -28,7 +28,7 @@ SCRATCH = {
     "PI": _sb(4, I), "PC": _sb(40, F), "XI": _sb(160, F), "XD": _sb(128, F), "XB": _sb(128, F), "XT": _sb(128, F),
     "UU": _sb(144, BF), "BP": _sb(128, BF), "BM": _sb(128, BF), "G8": _sb(8, BF), "MA": _sb(384, BF),
     "MB": _sb(384, BF), "MC": _sb(384, BF), "IDX": _sb(768, BF), "W32": _sb(128, BF), "ONE": _sb(8, BF),
-    "CR": _sb(8, F), "C48": _sb(4, F), "SL": _sb(128, U),
+    "CR": _sb(8, F), "UN": _sb(448, F), "C48": _sb(4, F), "SL": _sb(128, U),
     "D0": ("psum", [128, 512], F), "D1": ("psum", [128, 512], F), "CT": ("psum", [128, 512], F),
     "VA": ("psum", [128, 512], F), "VB": ("psum", [128, 512], F), "PW": ("psum", [128, 512], F),
     "PK": ("psum", [128, 512], F), "PQ": ("psum", [128, 512], F),
@@ -242,8 +242,8 @@ def rank_program(g, core, T, topo):
     ts(C("PC", 18), gcol, 16.0, ALU.mult, 15.0, ALU.add)
     cp(C("L0", 64 * me, 64), ind(A("X2"), C("SL", 24, 4)))
     send_all("n0", C("L0", 64 * me, 64), lambda r: C("L0", 64 * r, 64))
-    iota(A("IDX", p=(0, 32)), [[0, 3], [1, 256]])
-    iota(A("IDX", p=(32, 64)), [[256, 3], [0, 256]], -384)
+    iota(A("IDX", p=(0, 32)), [[0, 3], [-1, 256]])
+    iota(A("IDX", p=(32, 64)), [[-256, 3], [0, 256]], 384)
     cp(C("NM", 256, 192), ind(A("X2"), C("SL", 28, 12)))
     cp(C("VO", 0, 64), C("L0", 64 * me, 64))
     cp(C("VO", 64, 192), C("NM", 256, 192))
@@ -255,13 +255,16 @@ def rank_program(g, core, T, topo):
     ts(C("PC", 20, 3), C("XI", 0, 3), 20.0, ALU.mult, acol, ALU.add)
     ts(C("SL", 40, 16), C("XT", 24, 16), acol, ALU.add)
     tt(C("PC", 24, 3), C("PC", 24, 3), C("PC", 20, 3), ALU.add)
-    ts(A("BM"), A("XD"), gcol, ALU.is_equal, -1024.0, ALU.mult)
+    ts(A("BM"), A("XD"), gcol, ALU.is_equal, 1024.0, ALU.mult)
     ts(C("C48", 0, 3), C("PC", 24, 3), 1.0 / 64, ALU.mult, -3.0, ALU.add)
-    ts(A("BP"), A("XD"), gcol, ALU.is_equal, 2048.0, ALU.mult)
+    ts(A("BP"), A("XD"), gcol, ALU.is_equal, -2048.0, ALU.mult)
     ts(A("UU"), C("XI", 0, 144), C("PC", 18), ALU.is_equal)
     fill(C("CR", 0, 4), CN - 64.0)
     fill(C("CR", 4, 1), CN - 129.0)
-    act(A("BIG"), A("X1"), AF.Identity, bias=1e9, scale=0.0)
+    fill(C("CR", 6, 1), 190.0)
+    fill(C("CR", 7, 1), 192.0)
+    for n in range(6):
+        act(C("UN", 64 * n, 64), C("X1", 0, 64), AF.Identity, bias=(-1.0 if n % 2 else 1.0) / 16384, scale=0.0)
     act(A("MSG", slice(0, 80), slice(13, 16)), C("X1", 0, 240), AF.Identity, bias=0.0, scale=0.0)
     for q in range(3):
         ts(C("MB", 128 * q, 128), A("XB"), C("PC", 5 + q), ALU.is_equal, 4.0, ALU.mult)
@@ -295,13 +298,11 @@ def rank_program(g, core, T, topo):
     def vote_v(rnd, k):
         ts(C("NE", 192 * k, 192), ind(TBr, C("VO", 16 * k, 12)), rul(rnd, k), ALU.not_equal)
 
-    def vote_s(rnd, k):
-        t = C("SG", 192 * (k % 2), 192)
-        act(t, ind(TBr, C("VO", 16 * k, 12)), AF.Sign, bias=rul(rnd, k), scale=-1.0)
-        act(C("NE", 192 * k, 192), t, AF.Square)
-
-    def vote_m(rnd, k):
-        act(C("NE", 192 * k, 192), ind(TBr, C("VO", 16 * k, 12)), AF.Sign, bias=rul(rnd, k), scale=-1.0)
+    def vote_s(rnd, ks):
+        for i, k in enumerate(ks):
+            act(C("SG", 192 * i, 192), ind(TBr, C("VO", 16 * k, 12)), AF.Sign, bias=rul(rnd, k), scale=-1.0)
+        for i, k in enumerate(ks):
+            act(C("NE", 192 * k, 192), C("SG", 192 * i, 192), AF.Square)
 
     def vote_mm(bank, k, k0, n):
         mm([(C(bank, 8 * (n * h + k - k0), 8, p=(0, 96)), C("NE", 192 * k + 96 * h, 96), A("G8"), True, True)
@@ -311,8 +312,11 @@ def rank_program(g, core, T, topo):
         act(C("TH", th, 16 * n, p=(0, 96)), C(bank, 0, 16 * n, p=(0, 96)), AF.Sign, bias=7.5, scale=-1.0)
         mm([(C("PW", 0, 1, p=(0, 8 * n)), C("TH", th + 8 * n * h, 8 * n, p=(0, 96)), C("ONE", 0, 1, p=(0, 96)),
              h == 0, h == 1) for h in range(2)])
-        act(C("LV", 96 * me + off, 1, p=(0, 8 * n)), C("PW", 0, 1, p=(0, 8 * n)), AF.Identity, bias=96.0, scale=0.5)
-        send_all(tag, C("LV", 96 * me + off, 4), lambda r: C("LV", 96 * r + off, 4))
+
+        def out():
+            act(C("LV", 96 * me + off, 1, p=(0, 8 * n)), C("PW", 0, 1, p=(0, 8 * n)), AF.Identity, bias=96.0, scale=0.5)
+            send_all(tag, C("LV", 96 * me + off, 4), lambda r: C("LV", 96 * r + off, 4))
+        return out
 
     def courts(off, mat, bank):
         c = sm(32)
@@ -357,20 +361,21 @@ def rank_program(g, core, T, topo):
     def stale(rnd, b, steps):
         if b == 1:
             for r in range(N):
-                act(C("ZS", 192 * r, 192), ind(TBr, seg(rnd, b, r)), AF.Identity, bias=64.0)
+                act(C("ZS", 192 * r, 192), ind(TBr, seg(rnd, b, r)), AF.Identity, bias=-63.0, scale=2.0)
         else:
-            act(A("ZS"), ind(TBr, C("N48", 48 * b, 48)), AF.Identity, bias=64.0)
-        t = 95.5
-        for d in (16.0, 8.0, 4.0, 2.0, 1.0)[:steps]:
+            act(A("ZS"), ind(TBr, C("N48", 48 * b, 48)), AF.Identity, bias=-63.0, scale=2.0)
+        t = 0.0
+        for n in range(steps):
             c = sm(2)
-            act(A("JS"), A("ZS"), AF.Sign, bias=t, scale=-1.0, acc=C("SM", c))
-            act(C("SM", c + 1), C("SM", c), AF.Sign, bias=0.5, scale=-1.0)
-            t2 = sb()
-            act(t2, C("SM", c + 1), AF.Identity, bias=t, scale=d)
-            t = t2
+            k = 64 - (32 >> n)
+            act(A("JS"), A("ZS"), AF.Sign, bias=t, scale=1.0 if n % 2 else -1.0, acc=C("SM", c))
+            t = C("SM", c + 1)
+            act(C("UN", 64 * n + 64, k), C("UN", 64 * n, k), AF.Sign, bias=C("SM", c), scale=-8192.0, acc=t)
         if steps == 5:
-            return t, 0.5, [None, 0.5]
-        return t, 0.25, [None, 0.25, 0.5]
+            t2 = sb()
+            act(t2, t, AF.Identity, bias=95.5, scale=-0.5)
+            return t2, 0.5, [None, 0.5]
+        return t, None, None
 
     def idx_mm():
         for h in range(2):
@@ -381,9 +386,20 @@ def rank_program(g, core, T, topo):
         z = "Z%d" % (h % 2)
         Z = A(z)
         n8 = C("NM8", 48 * (h % 2), 48)
-        ts(C(z, 0, 384), ind(TBr, C("N48", 48 * b, 24)), 64.0, ALU.add)
-        act(C(z, 384, 384), ind(TBr, C("N48", 48 * b + 24, 24)), AF.Identity, bias=64.0)
-        ts(n8, C("N48", 48 * b, 48), 1.0 / TR, ALU.mult)
+        less = None
+        if b and st[2] is None:
+            for x in range(2):
+                ts(C(z, 192 * x, 192), ind(TBr, C("N48", 48 * b + 12 * x, 12)), 64.0, ALU.add)
+                if x == 0:
+                    e = sm(2)
+                    ts(C("SM", e, 2), C("CR", 6, 2), st[0], ALU.add)
+            act(C(z, 384, 384), ind(TBr, C("N48", 48 * b + 24, 24)), AF.Identity, bias=64.0)
+            run(small, 1)
+        else:
+            ts(C(z, 0, 384), ind(TBr, C("N48", 48 * b, 24)), 64.0, ALU.add)
+            act(C(z, 384, 384), ind(TBr, C("N48", 48 * b + 24, 24)), AF.Identity, bias=64.0)
+            ts(n8, C("N48", 48 * b, 48), 1.0 / TR, ALU.mult)
+            run(small, 1)
         for hf in range(2):
             mm([(C("D%d" % hf, 0, 384), A("BM"), C(z, 384 * hf, 384), False, False)])
         ns = CFG["help"][b]
@@ -395,6 +411,29 @@ def rank_program(g, core, T, topo):
             w, a, scales = 95.5, 79.5 / 32, [None, 1.0 / 32, 1.0 / 16, 0.125, 0.25, 0.5]
         else:
             w, a, scales = st
+        if scales is None:
+            c = sm(4)
+            hs = CFG["hs"][b]
+            for i in range(hs):
+                act(C("JS", 384 * i, 384), C(z, 384, 384), AF.Sign, bias=C("SM", e + i), scale=-2.0, acc=C("SM", c + i))
+            hook("gather")
+            for x in range(2):
+                for i in range(2):
+                    ts(C("IN", 768 * i + 192 * x, 192), C(z, 192 * x, 192), 2.0, ALU.mult, C("SM", e + i), ALU.is_gt)
+            for i in range(hs, 2):
+                ts(C("IN", 768 * i + 384, 384), C(z, 384, 384), 2.0, ALU.mult, C("SM", e + i), ALU.is_gt)
+            ts(C("SM", c + 2), w, 0.5, ALU.mult, 94.5, ALU.add)
+            ts(n8, C("N48", 48 * b, 48), 1.0 / TR, ALU.mult)
+            for i in range(2):
+                x = C("IN", 768 * i, 384)
+                scan(C("SC", 384 * i, 384), x, x if i < hs else C("IN", 768 * i + 384, 384), -384.0, ALU.add, ALU.add)
+            less, w = sb(), sb()
+            run(small, 1)
+            ts(less, C("SC", 383), C("SM", c) if hs > 0 else 0.0, ALU.is_ge, C("SM", c + 2), ALU.add)
+            run(small, 1)
+            ts(w, C("SC", 767), C("SM", c + 1) if hs > 1 else 0.0, ALU.is_ge)
+            scales = []
+            ns = 0
         for n, s in enumerate(scales):
             hook(n)
             if ns:
@@ -411,6 +450,7 @@ def rank_program(g, core, T, topo):
                 ts(C("IN", 0, nv), C(z, 0, nv), s, ALU.mult, w, ALU.is_gt)
                 a = C("SM", sm())
                 ts(a, w, 2.0, ALU.mult, -0.5, ALU.add)
+                run(small, CFG["pa"])
             w = sb()
             if ns:
                 scan(C("SC", 0, nv), C("IN", 0, nv), C("IN", 0, nv), -float(nv), ALU.add, ALU.add)
@@ -421,26 +461,29 @@ def rank_program(g, core, T, topo):
                 run(small, 1)
                 ts(w, C("SC", 383), 0.0, ALU.is_gt, a, ALU.add)
             run(small, 1)
-        run(small)
+        if b:
+            run(small)
         if ns:
             hook("gather")
         small += later[0]
         if b == 3:
             act(A("I0"), Z, AF.Identity, bias=-64.0)
         for hf in range(2):
-            ts(C("DM", 384 * hf, 384), C(z, 384 * hf, 384), w, ALU.max)
+            if less is None:
+                ts(C("DM", 384 * hf, 384), C(z, 384 * hf, 384), w, ALU.max)
+            else:
+                ts(C("DM", 384 * hf, 384), C(z, 384 * hf, 384), less, ALU.subtract, w, ALU.max)
             mm([(C("D%d" % hf, 0, 384), A("BP"), C("DM", 384 * hf, 384), False, True)])
         run(big[0])
-        c = sm(2)
-        red(C("SM", c), C("D0", 0, 384), ALU.min)
+        c = sm(4)
+        red(C("SM", c), C("D0", 0, 384), ALU.max)
+        red(C("SM", c + 1), C("D1", 0, 384), ALU.max)
         run(small, 1)
-        scan(A("KS"), C("D1", 0, 384), A("BIG"), C("SM", c), ALU.min, ALU.min)
-        run(small, 1)
-        key = C("KS", 383)
-        ts(C("SM", c + 1), key, CK, ALU.add, CK, ALU.subtract)
+        ts(C("SM", c + 2), C("SM", c), C("SM", c + 1), ALU.max, CK, ALU.add)
+        ts(C("SM", c + 3), C("SM", c), C("SM", c + 1), ALU.max, 384.0, ALU.subtract)
         run(small, 1)
         ju = C("JU", 2 * (h % 2))
-        ts(ju, key, C("SM", c + 1), ALU.subtract, 384.0, ALU.add)
+        ts(ju, C("SM", c + 2), CK, ALU.subtract, C("SM", c + 3), ALU.subtract)
         run(small, 1)
         s1 = 16 * (h % 2)
         ts(C("S1", s1, 16), ind(Z, ju), -1.0, ALU.mult, CN, ALU.add)
@@ -479,35 +522,39 @@ def rank_program(g, core, T, topo):
     idx_mm()
     SF = CFG["sfull"]
     for rnd in range(RO):
-        vote_s(rnd, 3)
+        vote_s(rnd, [3, 7])
         for k in range(3):
             vote_v(rnd, k)
-        for k in (0, 3, 1, 2):
+        for k in (0, 1, 3, 2):
             vote_mm("VA", k, 0, 4)
-        vote_s(rnd, 7)
-        vote_send(8 * rnd, "VA", 4, 0, "va%d" % rnd)
+        vote_send(8 * rnd, "VA", 4, 0, "va%d" % rnd)()
         for k in (4, 5, 6):
             vote_v(rnd, k)
-        vote_s(rnd, SF[0])
+        vote_s(rnd, SF[0:1])
         for k in (7, 4, 5, 6):
             vote_mm("VB", k, 4, 4)
-        vote_send(32 + 8 * rnd, "VB", 4, 64, "vb%d" % rnd)
-        run(update(3, rnd - 1) if rnd else first0)
+        vote_send(32 + 8 * rnd, "VB", 4, 64, "vb%d" % rnd)()
+        up3 = update(3, rnd - 1) if rnd else []
         vk = [k for k in range(8, 16) if k not in SF]
         for k in vk:
+            run(up3, 1 if k < 12 else 4)
             vote_v(rnd, k)
-        for k in SF[1:]:
-            vote_s(rnd, k)
+        run(up3)
+        run(first0)
+        for i in range(1, len(SF), 2):
+            vote_s(rnd, SF[i:i + 2])
         early = SF[:1] + vk[:-1]
         for k in early:
             vote_mm("VA", k, 8, 8)
         ca, c = courts(8 * rnd, "MA", "PK")
         cb, d = courts(32 + 8 * rnd, "MA", "PQ")
         run(ca, 1)
-        for k in vk[-1:] + SF[1:-1]:
+        for k in vk[-1:] + SF[1:3]:
             vote_mm("VA", k, 8, 8)
         run(cb, 1)
-        vote_mm("VA", SF[-1], 8, 8)
+        for k in SF[3:]:
+            vote_mm("VA", k, 8, 8)
+        third = vote_send(64 + 8 * rnd, "VA", 8, 128, "vc%d" % rnd)
 
         def names1(rnd=rnd):
             cp(C("SN", 192 * rnd, 64), ind(C("NM", 256, 64), C("OF2", 0, 4)))
@@ -545,31 +592,34 @@ def rank_program(g, core, T, topo):
             mm([(C("PQ", 4 * x, 4), C("MC", 128 * x, 128), C("QB", 0, 4), True, True) for x in range(2)])
 
         first = cc.pop(0)
-        cc += [last_of(e), bcast]
+        cc += [last_of(e), bcast, None]
         cc += [(lambda x=x: ts(C("OF1", x, 4, step=2), C("PQ", 4 * x, 4), 16.0, ALU.mult, C("PC", 11 + x), ALU.add))
                for x in range(2)]
-        cc += [lambda: ts(C("OF2", 4, 8), C("PQ", 0, 8), 16.0, ALU.mult, acol, ALU.add), names2,
-               lambda rnd=rnd: compact(rnd, 1)]
+        cc += [names2, lambda: ts(C("OF2", 4, 8), C("PQ", 0, 8), 16.0, ALU.mult, acol, ALU.add)]
         small = cb + lists0[:2]
 
-        def hook0(n, rnd=rnd, small=small, cc=cc, first=first, st=st):
-            if n == 1:
-                vote_send(64 + 8 * rnd, "VA", 8, 128, "vc%d" % rnd)
-            if n == 5:
+        def hook0(n, rnd=rnd, small=small, cc=cc, first=first, st=st, third=third):
+            if n == 0:
+                third()
+            if n == CFG["cb"]:
+                run(small)
                 first()
+                small += cc
             if n == "gather":
                 st[0] = stale(rnd, 1, CFG["st1"])
 
-        hearing(rnd, 0, None, small, [cc, []], [[lambda: run(small, CFG["win"])], [lambda: run(small, 2)]], hook0)
+        hearing(rnd, 0, None, small, [[], []],
+                [[lambda: run(small, CFG["win"])], [lambda: compact(rnd, 1), lambda: run(small, 2)]], hook0)
         u0, u1, u2 = update(0, rnd), update(1, rnd), update(2, rnd)
-        plan = {1: (lists0[2:] + [lambda: compact(rnd, 2)], [[], []], [u0[0:1] + late[0:1], u0[1:2] + late[1:2]]),
-                2: ([lambda: compact(rnd, 3)] + ends, [[], []], [u0[2:3] + late[2:3], u0[3:4]]),
+        plan = {1: ([lambda: compact(rnd, 2)] + lists0[2:], [[lambda: compact(rnd, 3)], []],
+                    [u0[0:1] + late[0:1], u0[1:2] + late[1:2]]),
+                2: ([], [ends, []], [u0[2:3] + late[2:3], u0[3:4]]),
                 3: ([], [u1[1:], u2[2:]], [u1[0:1], [u2[0], u0[4], u2[1], u0[5]] + u0[6:]])}
         late, ends = [], []
         for b in range(1, 4):
             def hook(n, b=b, rnd=rnd, st=st):
                 if n == "gather" and b < 3:
-                    st[0] = stale(rnd, b + 1, 5)
+                    st[0] = stale(rnd, b + 1, CFG["st"])
             hearing(rnd, b, st[0], plan[b][0], plan[b][1], plan[b][2], hook)
 
     outs = [dma(T.yf[:], TBr)]

@@ -6,8 +6,13 @@ TR = 8192
 CN = float(2 ** 24 + 4)
 CK = float(3 * 2 ** 32)
 CP = float(3 * 2 ** 23)
+C1 = float(3 * 2 ** 28)
+C2 = float(3 * 2 ** 39)
+UP = float(2 ** 17)
 BF, F, U, I = "bfloat16", "float32", "uint16", "int32"
-CFG = {"help": [384, 384, 384, 384], "sfull": [11, 10, 12, 13, 14], "per": 1, "pa": 1, "hs": [2, 1, 1, 2], "st1": 6, "st": 6, "win": 2, "mix": 4, "cb": 4}
+CFG = {"gv": [384, 448, 448, 384], "g0": 448, "help": [768, 768, 768, 0, 0], "pb": 5, "hv": [5, 12, 12], "nd": 2,
+       "dm": [0, 0, 0, 0], "dc": [0, 0, 0, 0], "sv": [6, 10], "u3": 1, "wv": "v", "so": [0, 0, 0],
+       "cr": [1, 0, 0, 1], "sa": 1, "sf": 1, "per": 3, "pa": 2, "cb": 0, "cf": 2, "cg": 11, "win": 0, "df": 3}
 
 
 def _sb(n, d):
@@ -15,26 +20,27 @@ def _sb(n, d):
 
 
 SCRATCH = {
-    "TB": _sb(TR + W, BF), "Z0": _sb(768, BF), "Z1": _sb(768, BF), "ZS": _sb(768, BF), "JS": _sb(768, BF),
-    "IN": _sb(1536, BF), "SC": _sb(768, BF), "DM": _sb(768, BF), "NR": _sb(768, BF), "I0": _sb(768, BF),
-    "I1": _sb(768, BF), "SM": _sb(512, F), "SB": _sb(256, BF),
-    "NE": _sb(3072, BF), "SG": _sb(384, BF), "TH": _sb(256, BF), "S1": _sb(32, F), "JU": _sb(4, U),
+    "TB": _sb(TR + W, BF), "ZZ": _sb(2352, BF), "ZS": _sb(840, BF), "JS": _sb(768, BF), "KK": _sb(784, BF),
+    "IN": _sb(768, BF), "SC": _sb(768, BF), "SW": _sb(1568, BF), "DM": _sb(768, BF), "NR": _sb(768, BF),
+    "I0": _sb(768, BF), "I1": _sb(768, BF), "SM": _sb(512, F), "SB": _sb(256, BF),
+    "NE": _sb(3072, BF), "SG": _sb(384, BF), "TH": _sb(576, BF), "S1": _sb(32, F), "JU": _sb(4, U),
     "CL": _sb(192, I), "RU": _sb(16, BF), "YR": _sb(16, BF), "X1": _sb(384, F), "X2": _sb(384, F), "YC": _sb(192, F),
-    "NM": _sb(448, F), "PB": _sb(448, F), "BT": _sb(448, BF), "FI": _sb(448, BF), "VO": _sb(256, U),
-    "L0": _sb(256, U), "L0F": _sb(256, F), "LV": _sb(384, BF), "SN": _sb(768, U),
-    "LN1": _sb([16, 16], U), "LN2": _sb([16, 32], U), "MSG": _sb([80, 16], BF), "FL0": _sb(1024, BF), "FLO": _sb(768, BF),
-    "NM8": _sb(96, F), "GG": _sb(48, F), "OS": _sb(48, U), "O48": _sb(4, U), "N48": _sb(192, U),
-    "OF0": _sb(16, U), "OF1": _sb(8, U), "OF2": _sb(12, U), "QB": _sb(8, BF),
-    "PI": _sb(4, I), "PC": _sb(40, F), "XI": _sb(160, F), "XD": _sb(128, F), "XB": _sb(128, F), "XT": _sb(128, F),
-    "UU": _sb(144, BF), "BP": _sb(128, BF), "BM": _sb(128, BF), "G8": _sb(8, BF), "MA": _sb(384, BF),
-    "MB": _sb(384, BF), "MC": _sb(384, BF), "IDX": _sb(768, BF), "W32": _sb(128, BF), "ONE": _sb(8, BF),
-    "CR": _sb(8, F), "UN": _sb(448, F), "C48": _sb(4, F), "SL": _sb(128, U),
+    "NM": _sb(400, F), "PB": _sb(400, F), "BT": _sb(400, BF), "FI": _sb(400, BF), "VO": _sb(256, U),
+    "L0": _sb(192, U), "LX": _sb(128, F), "SN": _sb(768, U), "LN": _sb(768, U), "DC": _sb(384, F), "DX": _sb(384, F),
+    "MSG": _sb([4, 10, 192], BF), "FL0": _sb(896, BF),
+    "NM8": _sb(96, F), "GG": _sb(48, F), "OS": _sb(48, U), "O48": _sb(4, U),
+    "OF0": _sb(16, U), "OF2": _sb(12, U), "QB": _sb(8, BF),
+    "PI": _sb(8, I), "PC": _sb(64, F), "XI": _sb(160, F), "XD": _sb(128, F), "XT": _sb(128, F),
+    "UU": _sb(144, BF), "BP": _sb(128, BF), "BM": _sb(256, BF),
+    "MB": _sb(384, F), "MC": _sb(384, BF), "IDX": _sb(384, BF), "W32": _sb(128, BF), "GQ": _sb(256, BF),
+    "LH": _sb(128, BF), "WC": _sb(144, BF), "RR": _sb(144, BF), "XP": _sb(432, F),
+    "PA": _sb(80, F), "PS": _sb(80, F), "PM": _sb(80, F), "RS": _sb(80, F), "CF": _sb(16, F), "C6": _sb(8, F),
+    "CR": _sb(8, F), "UN": _sb(1160, BF), "C48": _sb(4, F), "SL": _sb(128, U),
     "D0": ("psum", [128, 512], F), "D1": ("psum", [128, 512], F), "CT": ("psum", [128, 512], F),
-    "VA": ("psum", [128, 512], F), "VB": ("psum", [128, 512], F), "PW": ("psum", [128, 512], F),
-    "PK": ("psum", [128, 512], F), "PQ": ("psum", [128, 512], F),
+    "VA": ("psum", [128, 512], F), "VB": ("psum", [128, 512], F), "PK": ("psum", [128, 512], F),
 }
-POOL = {"v": 44, "s": 28, "t": 20, "y": 10, "g": 9}
-ARR = ["n0"] + ["%s%d" % (k, r) for r in range(RO) for k in ("va", "vb", "vc", "nb", "nc", "fa", "fb", "fc", "fd")]
+POOL = {"v": 42, "s": 30, "t": 22, "y": 8, "g": 10}
+ARR = ["n0"] + ["%s%d" % (k, r) for r in range(RO) for k in ("va", "vb", "nb", "nc", "nd", "fa", "fb", "fc", "fd")]
 SEMAPHORES = ["%s%d" % (q, i) for q in POOL for i in range(POOL[q])] + ["r" + a for a in ARR] + ["sent"]
 
 
@@ -62,6 +68,8 @@ def rank_program(g, core, T, topo):
         if SCRATCH[name][0] == "psum":
             m = 1
         ps = slice(None) if p is None else slice(p[0], p[1])
+        if name in ("RR", "IDX"):
+            m = 15 if p is None else (2 << (p[1] - 1) // 32) - (1 << p[0] // 32)
         return (T[name][tuple([ps] + ix)], [(name, m)])
 
     def C(name, a, n=1, p=None, step=1):
@@ -129,21 +137,43 @@ def rank_program(g, core, T, topo):
 
     def act(o, x, f, bias=0.0, scale=1.0, acc=None):
         if acc is None:
-            rec("s", [lambda: g.scalar.activation(o[0], x[0], f, bias=ap(bias), scale=scale)], [o], [x, bias])
+            rec("s", [lambda: g.scalar.activation(o[0], x[0], f, bias=ap(bias), scale=ap(scale))], [o],
+                [x, bias, scale])
         else:
             rec("s", [lambda: g.scalar.activation(o[0], x[0], f, bias=ap(bias), scale=scale, accum_out=acc[0])],
                 [o, acc], [x, bias])
+
+    def lin(o, x, scale, bias=0.0):
+        act(o, x, AF.Identity, bias=bias, scale=scale)
+
+    def sfill(o, x, c):
+        act(o, x, AF.Identity, bias=c, scale=0.0)
 
     def mm(items):
         def one(o, l, r, a, b):
             return lambda: g.tensor.matmul(o[0], l[0], r[0], a, b)
         rec("t", [one(*it) for it in items], [it[0] for it in items], [x for it in items for x in it[1:3]])
 
+    pool = [None, False]
+
+    def gp(call, o, ins):
+        n = rec("g", [call], [o], ins)
+        part = o[1][0][0] in ("RR", "IDX")
+        if pool[0] is not None and (part or pool[1]):
+            ops[n][2].add(pool[0])
+        pool[0], pool[1] = n, part
+
     def iota(o, pattern, base=0, ch=0, flag=True):
         if flag:
-            rec("g", [lambda: g.iota(o[0], pattern, base, ch, allow_small_or_imprecise_dtypes=True)], [o], [])
+            gp(lambda: g.iota(o[0], pattern, base, ch, allow_small_or_imprecise_dtypes=True), o, [])
         else:
-            rec("g", [lambda: g.iota(o[0], pattern, base, ch)], [o], [])
+            gp(lambda: g.iota(o[0], pattern, base, ch), o, [])
+
+    def where0(o, pattern, c):
+        gp(lambda: g.affine_select(o[0], o[0], pattern, ALU.not_equal, c, 0, 0), o, [o])
+
+    def keep0(o, pattern, base):
+        gp(lambda: g.affine_select(o[0], o[0], pattern, ALU.is_equal, 0.0, base, 1), o, [o])
 
     def dma(o, x):
         outs = [o] if isinstance(o, tuple) else []
@@ -215,116 +245,151 @@ def rank_program(g, core, T, topo):
     iota(C("XT", 0, 24), [[16, 12], [0, 2]])
     iota(A("XI"), [[1, 160]])
     iota(A("XD"), [[1, 8], [0, 16]])
-    iota(C("XT", 24, 16), [[16, 4], [64, 4]])
-    iota(A("XB"), [[1, 8], [32, 4], [0, 4]])
+    iota(C("XT", 24, 4), [[128, 4]])
+    iota(C("XT", 32, 4), [[56, 4]])
     iota(C("XT", 40, 24), [[1, 12], [0, 2]])
+    blk = [(32 * r, 32 * r + 32) for r in range(N)]
+    fill(A("RR"), 0.0)
+    fill(C("RR", 16, 64, p=blk[3]), 2.0)
+    iota(C("XP", 0, 144), [[0, 9], [1, 4], [0, 4]])
+    iota(C("XP", 144, 144), [[0, 36], [1, 4]])
+    iota(C("XP", 288, 64), [[1, 4], [0, 16]])
+    iota(C("RR", 80, 64, p=blk[0]), [[2, 4], [1, 4], [1, 4]], -6)
+    iota(C("RR", 0, 80, p=blk[0]), [[0, 5], [-8192, 4], [0, 4]], 24576)
+    iota(C("RR", 0, 80, p=blk[1]), [[0, 20], [-8, 4]], 24)
+    xs = lambda n, p=None: C("XI", 0, n, p=p)
+    ND = CFG["nd"]
+    PD = 768 // ND
+    defer = []
+    for n in range(1, 5):
+        defer.append(lambda n=n: sfill(C("UN", 290 + 96 * n, 96), xs(96), (-1.0 if n % 2 else 1.0) / 16384))
+    defer.append(lambda: sfill(C("UN", 403, 63), xs(63), 1.0))
+    defer.append(lambda: sfill(C("ZS", 768, 40), xs(40), 0.0))
+    for i, c in ((0, -4 * C1), (2, C2), (3, -C2), (4, -UP / 2), (36, 2 * UP)):
+        defer.append(lambda i=i, c=c: sfill(C("ZS", 768 + i), xs(1), c))
+    for i, c in enumerate((-C1, C2, 95.0 * UP)):
+        sfill(C("ZZ", 768 + i, 3, step=784), xs(3), c)
+    sfill(C("ZZ", 2338), xs(1), 79.5 / 32 * UP)
+    sfill(C("LX", 32 * me + 16, 16, p=(96, 128)), xs(16, (96, 128)), (384.0 + N - me) / 64)
+    sfill(C("W32", 0, 128, p=(0, 96)), xs(128, (0, 96)), 1.0 / 32)
+    sfill(A("C6"), xs(8), 0.0)
+    sfill(A("RS"), xs(80), 0.0)
+    sfill(C("PA", 0, 16), xs(16), 0.0)
+    sfill(C("RS", 15, 5, step=16), xs(5), -float(2 ** 25))
+    for o, c in ((C("C6", 4), 1.0), (C("C6", 5), -95.0), (C("CR", 6), CN)):
+        sfill(o, xs(1), c)
+    where0(C("RR", 80, 64, p=blk[1]), [[1, 4], [-1, 4], [0, 4]], -1024.0)
+    where0(C("RR", 16, 64, p=blk[3]), [[1, 4], [0, 4], [-1, 4]], 1.0)
+    where0(C("RR", 0, 80, p=blk[2]), [[0, 5], [1, 4], [-1, 4]], -float(2 ** 23))
+    where0(C("RR", 80, 64, p=blk[1]), [[1, 4], [0, 4], [-1, 4]], -1024.0)
+    where0(C("RR", 16, 64, p=blk[3]), [[1, 4], [-1, 4], [0, 4]], 0.0)
+    fill(A("KK"), -32.0)
+    fill(A("MC"), 1.0)
     ts(C("PI", 1), C("PI", 0), 15, ALU.bitwise_and)
     ts(C("PI", 2), C("PI", 0), 16, ALU.bitwise_and)
     ts(C("PI", 3), C("PI", 0), 4, ALU.arith_shift_right)
-    fill(C("LV", 96 * me, 96), 0.0)
-    cp(C("PC", 0, 4), A("PI"))
-    fill(C("LV", 96 * me, 96, p=(96, 128)), float(N - me))
+    cp(C("PC", 0, 4), C("PI", 0, 4))
     pcol, acol, ggc, gcol = [C("PC", i) for i in range(4)]
     ts(C("SL", 0, 24), C("XT", 0, 24), acol, ALU.add)
     ts(C("PC", 4), acol, 11.0, ALU.min, 32.0, ALU.mult)
-    fill(A("ONE"), 1.0)
+    ts(C("PI", 1), C("PI", 0), 7, ALU.bitwise_and)
     ts(C("SL", 24, 16), C("XI", 0, 16), C("PC", 4), ALU.add, ggc, ALU.add)
-    ts(A("G8"), C("XI", 0, 8), gcol, ALU.is_equal)
-    ts(C("PC", 5, 3), C("XI", 0, 3), -8.0, ALU.mult, pcol, ALU.add)
-    ts(C("PC", 32, 3), C("XI", 0, 3), -4.0, ALU.mult, pcol, ALU.add)
-    ts(C("PC", 11, 3), C("XI", 0, 3), 64.0, ALU.mult, acol, ALU.add)
-    ts(C("PC", 35, 4), C("XI", 0, 4), 16.0, ALU.mult, acol, ALU.add)
-    ts(C("PC", 8, 3), C("PC", 32, 3), 1.0 / 16, ALU.mult)
-    ts(C("PC", 14, 4), C("PC", 35, 4), -192.0, ALU.add)
-    fill(A("W32"), 1.0 / 32)
+    ts(C("PI", 2), C("PI", 0), 5, ALU.arith_shift_right)
+    ts(C("PI", 3), C("PI", 0), 3, ALU.arith_shift_right, 3, ALU.bitwise_and)
+    ts(C("PI", 4), C("PI", 0), 3, ALU.bitwise_and)
+    ts(C("PI", 5), C("PI", 0), 2, ALU.arith_shift_right, 3, ALU.bitwise_and)
+    fill(A("GQ"), 0.0)
+    cp(C("PC", 40, 5), C("PI", 1, 5))
+    p8, rr, qq, a4, ad = [C("PC", 40 + i) for i in range(5)]
+    ts(C("GQ", 128, 8), C("XI", 0, 8), gcol, ALU.is_equal)
+    ts(C("PC", 52), ad, 32.0, ALU.mult, a4, ALU.add)
+    ts(C("SL", 40, 4), C("XT", 24, 4), C("PC", 52), ALU.add, ggc, ALU.add)
+    lin(C("PC", 18), gcol, 16.0, 15.0)
+    lin(C("PC", 20, 3), C("XI", 0, 3), 16.0, acol)
+    lin(A("CF"), C("XI", 0, 16), 4.0, ad)
+    lin(C("C48", 0, 3), C("PC", 20, 3), 4.0)
     cp(A("X1"), ind(A("CL"), C("SL", 0, 24)))
     vtr(A("X2"), A("X1"))
-    ts(C("PC", 18), gcol, 16.0, ALU.mult, 15.0, ALU.add)
-    cp(C("L0", 64 * me, 64), ind(A("X2"), C("SL", 24, 4)))
-    send_all("n0", C("L0", 64 * me, 64), lambda r: C("L0", 64 * r, 64))
-    iota(A("IDX", p=(0, 32)), [[0, 3], [-1, 256]])
-    iota(A("IDX", p=(32, 64)), [[-256, 3], [0, 256]], 384)
-    cp(C("NM", 256, 192), ind(A("X2"), C("SL", 28, 12)))
-    cp(C("VO", 0, 64), C("L0", 64 * me, 64))
-    cp(C("VO", 64, 192), C("NM", 256, 192))
-    for q in range(3):
-        ts(C("MA", 128 * q, 128), A("XD"), C("PC", 5 + q), ALU.is_equal, 4.0, ALU.mult)
-    ts(C("PC", 20, 3), C("XI", 0, 3), 4.0, ALU.mult, acol, ALU.add)
-    act(A("MA", p=(96, 128)), A("X1", p=(96, 128)), AF.Identity, bias=1.0 / 32, scale=0.0)
-    ts(C("PC", 24, 3), C("PC", 20, 3), 12.0, ALU.is_ge, 4.0, ALU.mult)
-    ts(C("PC", 20, 3), C("XI", 0, 3), 20.0, ALU.mult, acol, ALU.add)
-    ts(C("SL", 40, 16), C("XT", 24, 16), acol, ALU.add)
-    tt(C("PC", 24, 3), C("PC", 24, 3), C("PC", 20, 3), ALU.add)
-    ts(A("BM"), A("XD"), gcol, ALU.is_equal, 1024.0, ALU.mult)
-    ts(C("C48", 0, 3), C("PC", 24, 3), 1.0 / 64, ALU.mult, -3.0, ALU.add)
-    ts(A("BP"), A("XD"), gcol, ALU.is_equal, -2048.0, ALU.mult)
+    ts(A("LH"), A("XD"), p8, ALU.is_equal)
+    cp(C("L0", 48 * me, 48), ind(A("X2"), C("SL", 40, 3)))
+    send_all("n0", C("L0", 48 * me, 48), lambda r: C("L0", 48 * r, 48))
+    cp(A("VO"), ind(A("X2"), C("SL", 24, 16)))
+    cp(C("NM", 208, 192), C("VO", 64, 192))
+    iota(C("IDX", 0, PD, p=(0, 32)), [[0, PD // 128], [-1, 128]])
+    iota(C("IDX", 0, PD, p=(32, 64)), [[-128, PD // 128], [0, 128]])
+    sfill(C("KK", 769), xs(1), -C2)
+    sfill(A("MB"), A("X1"), 2.0)
+    sfill(C("IDX", 0, PD, p=(64, 96)), A("X1", p=(64, 96)), 384.0)
+    ts(C("PC", 48), qq, 0.0, ALU.is_equal, 16384.0, ALU.mult)
+    ts(C("PC", 49), qq, 1.0, ALU.is_equal, 16.0, ALU.mult)
+    ts(C("PC", 50), qq, 2.0, ALU.is_equal, -1.0, ALU.mult)
+    ts(C("PC", 51), qq, 2.0, ALU.is_equal, -2.0, ALU.mult)
+    ts(C("BM", 0, 128), A("XD"), gcol, ALU.is_equal, 1024.0, ALU.mult)
+    for x in range(3):
+        sfill(A("MSG", slice(0, 4), slice(3 - me, 7 - me), slice(64 * x + 16 * me + 13, 64 * x + 16 * me + 16)),
+              xs(48), 0.0)
+    lin(A("BP"), C("BM", 0, 128), -2.0 / UP)
     ts(A("UU"), C("XI", 0, 144), C("PC", 18), ALU.is_equal)
-    fill(C("CR", 0, 4), CN - 64.0)
-    fill(C("CR", 4, 1), CN - 129.0)
-    fill(C("CR", 6, 1), 190.0)
-    fill(C("CR", 7, 1), 192.0)
-    for n in range(6):
-        act(C("UN", 64 * n, 64), C("X1", 0, 64), AF.Identity, bias=(-1.0 if n % 2 else 1.0) / 16384, scale=0.0)
-    act(A("MSG", slice(0, 80), slice(13, 16)), C("X1", 0, 240), AF.Identity, bias=0.0, scale=0.0)
-    for q in range(3):
-        ts(C("MB", 128 * q, 128), A("XB"), C("PC", 5 + q), ALU.is_equal, 4.0, ALU.mult)
-    for q in range(2):
-        ts(C("MC", 128 * q, 128), A("XD"), C("PC", 8 + q), ALU.is_equal)
-    ts(C("PC", 27), acol, 16.0 * me, ALU.add)
-    act(A("MB", p=(96, 128)), A("X1", p=(96, 128)), AF.Identity, bias=1.0 / 32, scale=0.0)
-    ts(C("SL", 56, 4), C("XI", 0, 4), 64.0, ALU.mult, C("PC", 27), ALU.add)
-
-    def bases(lo, n):
-        return [lambda: ts(C("PB", lo, n), C("NM", lo, n), -0.5, ALU.add, CP, ALU.add),
-                lambda: ts(C("VB", 64 + lo, n), C("PB", lo, n), -CP, ALU.add),
-                lambda: tt(C("BT", lo, n), C("NM", lo, n), C("VB", 64 + lo, n), ALU.subtract)]
-    run(bases(256, 192))
-    late = bases(0, 256)
-    first0 = [lambda: cp(A("L0F"), A("L0")), lambda: cp(C("NM", 0, 256), ind(A("L0F"), C("SL", 40, 16)))]
-    ends = [
-        lambda: ts(C("PC", 28), acol, 48.0, ALU.mult, 16.0 * me - 192.0, ALU.add),
-        lambda: ts(C("PC", 30), acol, 16.0, ALU.mult, 192.0, ALU.add),
-        lambda: ts(C("PC", 29), acol, 4.0, ALU.is_lt, C("PC", 28), ALU.mult),
-        lambda: ts(C("PC", 31), acol, ggc, ALU.add),
-        lambda: ts(C("SL", 60, 24), C("XT", 40, 24), C("PC", 29), ALU.add, C("PC", 30), ALU.add),
-        lambda: ts(C("SL", 84, 12), C("XI", 0, 12), 32.0, ALU.mult, C("PC", 31), ALU.add),
-    ]
+    ts(C("XP", 0, 80), C("XP", 0, 80), rr, ALU.is_equal, C("PC", 48), ALU.mult)
+    ts(C("XP", 144, 80), C("XP", 144, 80), rr, ALU.is_equal, C("PC", 49), ALU.mult)
+    ts(C("XP", 80, 64), C("XP", 80, 64), rr, ALU.is_equal, C("PC", 50), ALU.mult)
+    ts(C("XP", 224, 64), C("XP", 224, 64), rr, ALU.is_equal, C("PC", 50), ALU.mult)
+    ts(C("XP", 288, 64), C("XP", 288, 64), rr, ALU.is_equal, C("PC", 51), ALU.mult)
+    ts(C("RR", 80, 64, p=blk[0]), C("RR", 80, 64, p=blk[0]), 1.0, ALU.min, -1.0, ALU.max)
+    tt(C("XP", 0, 144), C("XP", 0, 144), C("XP", 144, 144), ALU.add)
+    ts(C("XP", 288, 64), C("XP", 288, 64), C("PC", 50), ALU.subtract)
+    ts(A("CF"), A("CF"), 48.0, ALU.min)
+    lin(C("WC", 0, 80), C("XP", 0, 80), 1.0)
+    tt(C("WC", 80, 64), C("XP", 80, 64), C("XP", 288, 64), ALU.add)
+    lin(C("PC", 27), C("PC", 4), 0.125, 48.0 * me)
+    ts(C("PC", 54), acol, 4.0, ALU.is_lt)
+    ts(C("PC", 55), ad, 1.0, ALU.is_equal)
+    lin(C("PC", 5), C("PC", 55), 4.0, -3.0)
+    ts(C("SL", 56, 4), C("XI", 0, 4), C("PC", 27), ALU.add)
+    ends = [lambda: lin(C("PC", 28), acol, -15.0, 48.0 * me - 144.0),
+            lambda: lin(C("PC", 30), acol, 16.0, 144.0),
+            lambda: lin(C("PC", 31), acol, 1.0, ggc),
+            lambda: lin(C("PC", 53), C("PC", 54), 3.0, 1.0),
+            lambda: lin(C("PC", 29), C("PC", 28), C("PC", 54), C("PC", 30))]
+    ends2 = [lambda: ts(C("SL", 84, 12), C("XI", 0, 12), 32.0, ALU.mult, C("PC", 31), ALU.add),
+             lambda: ts(C("SL", 60, 24), C("XT", 40, 24), C("PC", 53), ALU.mult, C("PC", 29), ALU.add)]
+    defer += [lambda: sfill(C("NM", 192, 16), xs(16), 0.0),
+              lambda: lin(A("PB"), A("NM"), 1.0 - 2.0 ** -14, CP),
+              lambda: lin(C("VB", 0, 400), A("PB"), 1.0, -CP)]
+    late = [lambda: tt(A("BT"), A("NM"), C("VB", 0, 400), ALU.subtract)]
 
     def rul(rnd, k):
         if rnd == 0:
             return C("RU", k)
-        return C("FI", 64 * k + 12) if k < 4 else C("FI", 192 + 16 * k + 12)
+        return C("FI", 192 + k) if k < 4 else C("FI", 144 + 16 * k + 12)
 
     def vote_v(rnd, k):
         ts(C("NE", 192 * k, 192), ind(TBr, C("VO", 16 * k, 12)), rul(rnd, k), ALU.not_equal)
 
-    def vote_s(rnd, ks):
-        for i, k in enumerate(ks):
-            act(C("SG", 192 * i, 192), ind(TBr, C("VO", 16 * k, 12)), AF.Sign, bias=rul(rnd, k), scale=-1.0)
-        for i, k in enumerate(ks):
-            act(C("NE", 192 * k, 192), C("SG", 192 * i, 192), AF.Square)
+    def vote_s(rnd, ks, part=None):
+        for k in ks if part != 1 else []:
+            act(C("SG", 192 * (k // 4 % 2), 192), ind(TBr, C("VO", 16 * k, 12)), AF.Sign, bias=rul(rnd, k), scale=-1.0)
+        for k in ks if part != 0 else []:
+            act(C("NE", 192 * k, 192), C("SG", 192 * (k // 4 % 2), 192), AF.Square)
 
-    def vote_mm(bank, k, k0, n):
-        mm([(C(bank, 8 * (n * h + k - k0), 8, p=(0, 96)), C("NE", 192 * k + 96 * h, 96), A("G8"), True, True)
-            for h in range(2)])
+    def vote_mm(bank, at, k, row, start, stop):
+        mm([(C(bank, at, 192), C("GQ", 128 - row, 128), C("NE", 192 * k, 192), start, stop)])
 
-    def vote_send(off, bank, n, th, tag):
-        act(C("TH", th, 16 * n, p=(0, 96)), C(bank, 0, 16 * n, p=(0, 96)), AF.Sign, bias=7.5, scale=-1.0)
-        mm([(C("PW", 0, 1, p=(0, 8 * n)), C("TH", th + 8 * n * h, 8 * n, p=(0, 96)), C("ONE", 0, 1, p=(0, 96)),
-             h == 0, h == 1) for h in range(2)])
+    def vote_send(rnd, x, bank, at):
+        p = (0, 96) if x else None
+        off = 16 * x + 4 * rnd
+        act(C("TH", 192 * x, 192, p=p), C(bank, at, 192, p=p), AF.Sign, bias=7.5, scale=-1.0,
+            acc=C("LX", 32 * me + off, p=p))
+        send_all("v%s%d" % ("ab"[x], rnd), C("LX", 32 * me + off), lambda r: C("LX", 32 * r + off))
 
-        def out():
-            act(C("LV", 96 * me + off, 1, p=(0, 8 * n)), C("PW", 0, 1, p=(0, 8 * n)), AF.Identity, bias=96.0, scale=0.5)
-            send_all(tag, C("LV", 96 * me + off, 4), lambda r: C("LV", 96 * r + off, 4))
-        return out
-
-    def courts(off, mat, bank):
+    def courts(off, mat, bank, at):
         c = sm(32)
-        K = [C(bank, 4 * q, 4) for q in range(3)]
+        K = [C(bank if q else "VA", at + 4 * q, 4) for q in range(3)]
+        votes = C("LX", off, 4, step=32)
         m0, m1, m2 = C("SM", c), C("SM", c + 1), C("SM", c + 2)
         al0, al1, k1, k2p, k2, pre = [C("SM", c + 4 + 4 * i, 4) for i in range(6)]
         return [
-            lambda: mm([(K[q], C(mat, 128 * q, 128), C("LV", off, 4, step=96), True, True) for q in range(3)]),
+            lambda: [mm([(K[q], C(mat, 128 * q, 128), votes, True, True) for q in qs]) for qs in ((0,), (1, 2))],
             lambda: red(m0, K[0], ALU.max),
             lambda: ts(al0, K[0], m0, ALU.not_equal, 3.0, ALU.mult),
             lambda: tt(k1, K[1], al0, ALU.mult),
@@ -336,170 +401,204 @@ def rank_program(g, core, T, topo):
             lambda: red(m2, k2, ALU.max),
         ], c
 
-    def update(b, rnd):
+    def update(b, nb, rnd):
         if b == 0:
-            lo, n = 0, 256
-            put = [(lambda r=r: cp(ind(C("FI", 0, 256), C("OF0", 4 * r, 4)), C("FL0", 256 * rnd + 64 * r, 64)))
-                   for r in range(N)]
-            vo = lambda: cp(C("VO", 0, 64), ind(C("NM", 0, 256), C("SL", 56, 4)))
+            lo, n = 0, 192
+            src = ind(C("FL0", 224 * rnd, 224), C("OF0", 0, 13))
+            put = lambda: lin(C("FI", 0, 208), src, 1.0) if CFG["sf"] else cp(C("FI", 0, 208), src)
+            vo = lambda: cp(C("VO", 0, 48), ind(C("NM", 0, 192), C("SL", 56, 3)))
         else:
-            lo, n = 192 + 64 * b, 64
-            put = [lambda: cp(ind(C("FI", lo, n), C("OF2", 4 * b - 4, 4)), C("FLO", 192 * rnd + 64 * b - 64, 64))]
-            vo = lambda: cp(C("VO", 64 * b, 64), C("NM", lo, 64))
-        return put + [
-            lambda: tt(C("BT", lo, n), C("FI", lo, n), C("BT", lo, n), ALU.not_equal),
-            lambda: tt(C("NM", lo, n), C("BT", lo, n), C("VB", 64 + lo, n), ALU.add),
-        ] + ([vo] if rnd < RO - 1 else [])
+            lo, n = 144 + 64 * b, 64 * nb
+            put = lambda: cp(ind(C("FI", lo, n), C("OF2", 4 * b - 4, 4 * nb)),
+                             A("MSG", rnd, 3, slice(64 * b - 64, 64 * b - 64 + n)))
+            vo = lambda: cp(C("VO", 64 * b, n - 16), C("NM", lo, n - 16))
+        return [put,
+                lambda: tt(C("BT", lo, n), C("FI", lo, n), C("BT", lo, n), ALU.not_equal),
+                lambda: tt(C("NM", lo, n), C("BT", lo, n), C("VB", lo, n), ALU.add),
+                ] + ([vo] if rnd < RO - 1 else [])
 
-    def seg(rnd, b, r):
-        row = slice(4 * rnd, 4 * rnd + 4) if r is None else 4 * rnd + r
-        return A("LN1", row, slice(0, 12)) if b == 1 else A("LN2", row, slice(16 * b - 32, 16 * b - 20))
+    def names(rnd, b, a=0, n=48):
+        return C("LN", 192 * rnd + 48 * b + a, n)
 
-    def compact(rnd, b):
-        cp(C("N48", 48 * b, 48), seg(rnd, b, None))
+    def aux(rnd, b, i, n=1):
+        if b == 0:
+            return C("FL0", 224 * rnd + 56 * me + 48 + i, n)
+        c = 64 * b - 64 + 16 * me + 12
+        return A("MSG", rnd, 6 - me + i, slice(c, c + 1))
 
-    def stale(rnd, b, steps):
-        if b == 1:
-            for r in range(N):
-                act(C("ZS", 192 * r, 192), ind(TBr, seg(rnd, b, r)), AF.Identity, bias=-63.0, scale=2.0)
-        else:
-            act(A("ZS"), ind(TBr, C("N48", 48 * b, 48)), AF.Identity, bias=-63.0, scale=2.0)
-        t = 0.0
-        for n in range(steps):
+    def stale(rnd, b):
+        act(C("ZS", 0, 768), ind(TBr, names(rnd, b)), AF.Identity, bias=191.0, scale=-2.0)
+
+    def halve():
+        scan(C("UN", 0, 403), C("ZS", 0, 403, step=2), C("ZS", 1, 403, step=2), 4 * C1 - 256.0 * 128, ALU.add, ALU.add)
+        t = C("UN", 402)
+        for n in range(1, 6):
+            c = sm(3)
+            k = 96 - (16 >> n)
+            act(A("JS"), C("ZS", 0, 768), AF.Sign, bias=t, scale=-2048.0 if n == 1 else -0.5 if n % 2 else 0.5,
+                acc=C("SM", c))
+            if n < 5:
+                t = C("SM", c + 1)
+                act(C("UN", 386 + 96 * n, k), C("UN", 290 + 96 * n, k), AF.Sign, bias=C("SM", c), scale=-8192.0, acc=t)
+        return t, c
+
+    def offset(t, rnd, b):
+        off, a = sb(), C("SM", t[1] + 2)
+        if CFG["so"][b]:
             c = sm(2)
-            k = 64 - (32 >> n)
-            act(A("JS"), A("ZS"), AF.Sign, bias=t, scale=1.0 if n % 2 else -1.0, acc=C("SM", c))
-            t = C("SM", c + 1)
-            act(C("UN", 64 * n + 64, k), C("UN", 64 * n, k), AF.Sign, bias=C("SM", c), scale=-8192.0, acc=t)
-        if steps == 5:
-            t2 = sb()
-            act(t2, t, AF.Identity, bias=95.5, scale=-0.5)
-            return t2, 0.5, [None, 0.5]
-        return t, None, None
+            act(C("SM", c), C("SM", t[1]), AF.Sign, bias=0.5)
+            lin(a, C("SM", c), -0.5, t[0])
+            act(C("SM", c + 1), aux(rnd, b, 2), AF.Sign, bias=a)
+            lin(off, C("SM", c + 1), -0.5, a)
+            return off
+        ts(a, C("SM", t[1]), 0.0, ALU.is_ge, t[0], ALU.subtract)
+        ts(off, aux(rnd, b, 2), a, ALU.is_lt, a, ALU.subtract)
+        return off
 
     def idx_mm():
-        for h in range(2):
-            mm([(C("D%d" % h, 0, 384), A("W32", p=(0, 64)), C("IDX", 384 * h, 384, p=(0, 64)), True, False)])
+        for x in range(ND):
+            p = (0, 96 - 32 * x)
+            mm([(C("D%d" % x, 0, PD), A("W32", p=p), C("IDX", 0, PD, p=p), True, False)])
 
-    def hearing(rnd, b, st, small, later, big, hook):
+    def hearing(rnd, b, off, small, later, big):
         h = 4 * rnd + b
-        z = "Z%d" % (h % 2)
-        Z = A(z)
-        n8 = C("NM8", 48 * (h % 2), 48)
-        less = None
-        if b and st[2] is None:
-            for x in range(2):
-                ts(C(z, 192 * x, 192), ind(TBr, C("N48", 48 * b + 12 * x, 12)), 64.0, ALU.add)
-                if x == 0:
-                    e = sm(2)
-                    ts(C("SM", e, 2), C("CR", 6, 2), st[0], ALU.add)
-            act(C(z, 384, 384), ind(TBr, C("N48", 48 * b + 24, 24)), AF.Identity, bias=64.0)
-            run(small, 1)
+        par = h % 2
+        zc = lambda a, n, step=1: C("ZZ", 784 * (par if b else 2) + a, n, step=step)
+        Z = zc(0, 768)
+        n8 = C("NM8", 48 * par, 48)
+        gv = CFG["gv"][b]
+        g0 = min(gv, CFG["g0"])
+        nxt = []
+
+        def at(n):
+            if b == 0:
+                big[2](n)
+            if b < 3 and n == CFG["hv"][b]:
+                nxt.append(halve())
+        ts(zc(0, g0), ind(TBr, names(rnd, b, 0, g0 // 16)), off, ALU.add)
+        act(zc(gv, 768 - gv), ind(TBr, names(rnd, b, gv // 16, 48 - gv // 16)), AF.Identity, bias=off)
+        if gv > g0:
+            ts(zc(g0, gv - g0), ind(TBr, names(rnd, b, g0 // 16, (gv - g0) // 16)), off, ALU.add)
+        dms = CFG["dm"][b]
+        if 0 < b < 3 and not dms:
+            stale(rnd, b + 1)
+        c = sm(2)
+        if not CFG["cr"][b]:
+            ts(C("CR", 0, 6), C("C6", 0, 6), off, ALU.subtract, CN, ALU.add)
+        elif b:
+            lin(C("SM", c), off, -1.0, CN)
+            lin(C("CR", 0, 6), C("C6", 0, 6), 1.0, C("SM", c))
         else:
-            ts(C(z, 0, 384), ind(TBr, C("N48", 48 * b, 24)), 64.0, ALU.add)
-            act(C(z, 384, 384), ind(TBr, C("N48", 48 * b + 24, 24)), AF.Identity, bias=64.0)
-            ts(n8, C("N48", 48 * b, 48), 1.0 / TR, ALU.mult)
-            run(small, 1)
-        for hf in range(2):
-            mm([(C("D%d" % hf, 0, 384), A("BM"), C(z, 384 * hf, 384), False, False)])
-        ns = CFG["help"][b]
-        nv = 768 - ns
-        if not ns:
-            run(small)
-            hook("gather")
+            lin(C("CR", 0, 6), C("C6", 0, 6), 1.0, CN - off)
         if b == 0:
-            w, a, scales = 95.5, 79.5 / 32, [None, 1.0 / 32, 1.0 / 16, 0.125, 0.25, 0.5]
-        else:
-            w, a, scales = st
-        if scales is None:
-            c = sm(4)
-            hs = CFG["hs"][b]
-            for i in range(hs):
-                act(C("JS", 384 * i, 384), C(z, 384, 384), AF.Sign, bias=C("SM", e + i), scale=-2.0, acc=C("SM", c + i))
-            hook("gather")
-            for x in range(2):
-                for i in range(2):
-                    ts(C("IN", 768 * i + 192 * x, 192), C(z, 192 * x, 192), 2.0, ALU.mult, C("SM", e + i), ALU.is_gt)
-            for i in range(hs, 2):
-                ts(C("IN", 768 * i + 384, 384), C(z, 384, 384), 2.0, ALU.mult, C("SM", e + i), ALU.is_gt)
-            ts(C("SM", c + 2), w, 0.5, ALU.mult, 94.5, ALU.add)
-            ts(n8, C("N48", 48 * b, 48), 1.0 / TR, ALU.mult)
-            for i in range(2):
-                x = C("IN", 768 * i, 384)
-                scan(C("SC", 384 * i, 384), x, x if i < hs else C("IN", 768 * i + 384, 384), -384.0, ALU.add, ALU.add)
-            less, w = sb(), sb()
-            run(small, 1)
-            ts(less, C("SC", 383), C("SM", c) if hs > 0 else 0.0, ALU.is_ge, C("SM", c + 2), ALU.add)
-            run(small, 1)
-            ts(w, C("SC", 767), C("SM", c + 1) if hs > 1 else 0.0, ALU.is_ge)
-            scales = []
-            ns = 0
-        for n, s in enumerate(scales):
-            hook(n)
-            if ns:
-                c = sm()
-                act(C("JS", 0, ns), C(z, nv, ns), AF.Sign, bias=w, scale=-(s or 1.0), acc=C("SM", c))
-            if s is None:
-                ts(C("IN", 0, nv), C(z, 0, nv), w, ALU.is_gt)
-                if b:
-                    a, f = C("SM", sm()), a
-                    ts(a, w, f, ALU.mult, -0.5, ALU.add)
-                else:
-                    run(small, 1)
-            else:
-                ts(C("IN", 0, nv), C(z, 0, nv), s, ALU.mult, w, ALU.is_gt)
-                a = C("SM", sm())
-                ts(a, w, 2.0, ALU.mult, -0.5, ALU.add)
-                run(small, CFG["pa"])
-            w = sb()
-            if ns:
-                scan(C("SC", 0, nv), C("IN", 0, nv), C("IN", 0, nv), -float(nv), ALU.add, ALU.add)
-                run(small, CFG["per"])
-                ts(w, C("SC", nv - 1), C("SM", c), ALU.is_ge, a, ALU.add)
-            else:
-                scan(C("SC", 0, 384), C("IN", 0, 384), C("IN", 384, 384), -383.5, ALU.add, ALU.add)
-                run(small, 1)
-                ts(w, C("SC", 383), 0.0, ALU.is_gt, a, ALU.add)
-            run(small, 1)
+            lin(n8, ind(C("NM", 0, 192), C("O48", 0, 3)), 1.0 / TR)
+        for x in range(2):
+            mm([(C("D%d" % x, 0, PD), C("BM", 128 * x * dms, 128), zc(PD * x, PD), False, False)])
+        scan(C("SW", 784 * par, 771), zc(0, 771), C("KK", 0, 771), C1 + 16512.0, ALU.add, ALU.add)
+        w = C("SW", 784 * par + 770)
         if b:
-            run(small)
-        if ns:
-            hook("gather")
+            ts(n8, names(rnd, b), 1.0 / TR, ALU.mult)
+        if b == 0:
+            run(small, 1)
+            for n, s in enumerate([UP / 32, 1.0 / 16, 0.125, 0.25, 0.5]):
+                at(n)
+                ns = CFG["help"][n]
+                nv = 768 - ns
+                c = sm()
+                a = C("SM", sm())
+                if ns:
+                    act(C("JS", 0, ns), zc(nv, ns), AF.Sign, bias=w, scale=-s, acc=C("SM", c))
+                sa = CFG["sa"] and 0 < ns < 768
+                if sa:
+                    lin(a, w, 2.0 / UP if n == 0 else 2.0, -0.5)
+                run(defer, CFG["df"] if n < 3 else 99)
+                if nv:
+                    ts(C("IN", 0, nv), zc(0, nv), s, ALU.mult, w, ALU.is_gt)
+                if not sa:
+                    ts(a, w, 2.0 / UP if n == 0 else 2.0, ALU.mult, -0.5, ALU.add)
+                run(small, CFG["pa"] if nv else CFG["pb"])
+                w = sb()
+                if not nv:
+                    ts(w, C("SM", c), 0.0, ALU.is_le, a, ALU.add)
+                elif ns:
+                    scan(C("SC", 0, nv), C("IN", 0, nv), C("IN", 0, nv), float(ns - 768), ALU.add, ALU.add)
+                    run(small, CFG["per"])
+                    ts(w, C("SC", nv - 1), C("SM", c), ALU.is_ge, a, ALU.add)
+                else:
+                    scan(C("SC", 0, 384), C("IN", 0, 384), C("IN", 384, 384), -383.5, ALU.add, ALU.add)
+                    run(small, CFG["per"])
+                    ts(w, C("SC", 383), 0.0, ALU.is_gt, a, ALU.add)
+                run(small, 1)
         small += later[0]
-        if b == 3:
-            act(A("I0"), Z, AF.Identity, bias=-64.0)
-        for hf in range(2):
-            if less is None:
-                ts(C("DM", 384 * hf, 384), C(z, 384 * hf, 384), w, ALU.max)
+        at(11)
+        for x in range(2):
+            if x and dms:
+                act(C("DM", PD, PD), zc(PD, PD), AF.Relu, bias=w, scale=-UP)
+            elif b:
+                ts(C("DM", PD * x, PD), zc(PD * x, PD), UP, ALU.mult, w, ALU.max)
             else:
-                ts(C("DM", 384 * hf, 384), C(z, 384 * hf, 384), less, ALU.subtract, w, ALU.max)
-            mm([(C("D%d" % hf, 0, 384), A("BP"), C("DM", 384 * hf, 384), False, True)])
-        run(big[0])
+                ts(C("DM", PD * x, PD), zc(PD * x, PD), w, ALU.max, UP, ALU.mult)
+            mm([(C("D%d" % x, 0, PD), A("BP"), C("DM", PD * x, PD), False, True)])
+        if 0 < b < 3 and dms:
+            stale(rnd, b + 1)
         c = sm(4)
-        red(C("SM", c), C("D0", 0, 384), ALU.max)
-        red(C("SM", c + 1), C("D1", 0, 384), ALU.max)
+        cd = CFG["dc"][b]
+        if cd:
+            lin(A("DC"), C("D0", 0, PD), 1.0)
+        if b == 3:
+            lin(C("SM", c + 3), off, -1.0)
+            lin(A("I0"), Z, 1.0, C("SM", c + 3))
+        at(12)
+        run(big[0])
+        at(5)
+        if cd:
+            scan(A("DX"), C("D1", 0, PD), A("DC"), -1e9, ALU.max, ALU.max)
+            top = C("DX", PD - 1)
+            at(6)
+            run(small, 1)
+            ts(C("SM", c), top, CK, ALU.add, CK, ALU.subtract)
+        else:
+            red(C("SM", c + 1), C("D0", 0, PD), ALU.max)
+            at(6)
+            red(C("SM", c + 2), C("D1", 0, PD), ALU.max)
+            run(small, 1)
+            top = C("SM", sm())
+            ts(C("SM", c), C("SM", c + 1), C("SM", c + 2), ALU.max, CK, ALU.add)
+            ts(top, C("SM", c + 1), C("SM", c + 2), ALU.max, 384.0, ALU.subtract)
+        at(7)
         run(small, 1)
-        ts(C("SM", c + 2), C("SM", c), C("SM", c + 1), ALU.max, CK, ALU.add)
-        ts(C("SM", c + 3), C("SM", c), C("SM", c + 1), ALU.max, 384.0, ALU.subtract)
+        ju = C("JU", 2 * par)
+        if cd:
+            ts(ju, C("SM", c), top, ALU.subtract, 384.0, ALU.add)
+        else:
+            ts(ju, C("SM", c), CK, ALU.subtract, top, ALU.subtract)
         run(small, 1)
-        ju = C("JU", 2 * (h % 2))
-        ts(ju, C("SM", c + 2), CK, ALU.subtract, C("SM", c + 3), ALU.subtract)
-        run(small, 1)
-        s1 = 16 * (h % 2)
+        s1 = 16 * par
         ts(C("S1", s1, 16), ind(Z, ju), -1.0, ALU.mult, CN, ALU.add)
+        at(8)
         run(small, 1)
-        ts(A("NR"), Z, C("S1", s1), ALU.add, CN, ALU.is_equal)
-        mm([(C("CT", 0, 48), C("UU", 15 - a_, 128), C("NR", a_, 48, step=16), a_ == 0, a_ == 15) for a_ in range(16)])
-        tt(A("MSG", slice(5 * h, 5 * h + 5), 12), C("CR", 0, 5), C("S1", s1, 5), ALU.subtract)
+        for e in range(2):
+            ts(C("NR", 384 * e, 384), zc(e, 384, 2), C("S1", s1), ALU.add, CN, ALU.is_equal)
+            mm([(C("CT", 0, 48), C("UU", 15 - 2 * i - e, 128), C("NR", 384 * e + i, 48, step=8), e + i == 0,
+                 e + i == 8) for i in range(8)])
+        mc = 64 * b - 64 + 16 * me
+        if b == 0:
+            tt(aux(rnd, b, 0, 4), C("CR", 3, 4), C("S1", s1, 4), ALU.subtract)
+            fl = C("FL0", 224 * rnd + 56 * me, 48)
+        else:
+            tt(A("MSG", rnd, slice(3 - me, 10 - me), mc + 12), C("CR", 0, 7), C("S1", s1, 7), ALU.subtract)
+            fl = A("MSG", rnd, slice(3 - me, 7 - me), slice(mc, mc + 12))
+        rho = aux(rnd, b, 3)
+        at(9)
         run(small, 1)
         if b == 3:
-            act(A("I1"), A("I0"), AF.Sign, bias=A("MSG", 5 * h, slice(12, 13)), scale=-1.0)
+            act(A("I1"), Z, AF.Sign, bias=rho, scale=-1.0)
         else:
-            ts(A("I0"), Z, -128.0, ALU.add, A("MSG", 5 * h + 4, slice(12, 13)), ALU.min)
-            ts(A("I1"), Z, A("MSG", 5 * h, slice(12, 13)), ALU.subtract, 65.0, ALU.max)
+            ts(A("I0"), Z, rho, ALU.subtract, -1.0, ALU.min)
+            ts(A("I1"), Z, off, ALU.subtract, aux(rnd, b, 1), ALU.max)
+        at(10)
         run(big[1])
         small += later[1]
-        fl = A("MSG", slice(5 * h, 5 * h + 4), slice(0, 12))
         ts(fl, C("CT", 0, 48), 11.5, ALU.is_lt)
         run(small, 1)
         tt(A("GG"), fl, n8, ALU.add)
@@ -508,124 +607,116 @@ def rank_program(g, core, T, topo):
         run(small)
         tag = "f%s%d" % ("abcd"[b], rnd)
         if b == 0:
-            whole = A("MSG", slice(5 * h, 5 * h + 4))
-            send_all(tag, whole, lambda r: C("FL0", 256 * rnd + 64 * r, 64))
-            dma(C("FL0", 256 * rnd + 64 * me, 64), whole)
+            slot = lambda r: C("FL0", 224 * rnd + 56 * r, 50)
+            send_all(tag, slot(me), slot)
         else:
-            base = 192 * rnd + 64 * b - 64
-            send_each(tag, lambda r: A("MSG", 5 * h + r), lambda r: C("FLO", base + 16 * r, 16))
-            dma(C("FLO", base + 16 * me, 16), A("MSG", 5 * h + me))
+            send_each(tag, lambda r: A("MSG", rnd, 3 - me + r, slice(mc, mc + 16)),
+                      lambda r: A("MSG", rnd, 3, slice(64 * b - 64 + 16 * r, 64 * b - 48 + 16 * r)))
         tt(ind(TBw, A("OS")), A("I0"), A("I1"), ALU.add)
         if h + 1 < 4 * RO:
             idx_mm()
+        return offset(nxt[0], rnd, b) if b < 3 else None
 
-    idx_mm()
-    SF = CFG["sfull"]
     for rnd in range(RO):
-        vote_s(rnd, [3, 7])
-        for k in range(3):
-            vote_v(rnd, k)
-        for k in (0, 1, 3, 2):
-            vote_mm("VA", k, 0, 4)
-        vote_send(8 * rnd, "VA", 4, 0, "va%d" % rnd)()
-        for k in (4, 5, 6):
-            vote_v(rnd, k)
-        vote_s(rnd, SF[0:1])
-        for k in (7, 4, 5, 6):
-            vote_mm("VB", k, 4, 4)
-        vote_send(32 + 8 * rnd, "VB", 4, 64, "vb%d" % rnd)()
-        up3 = update(3, rnd - 1) if rnd else []
-        vk = [k for k in range(8, 16) if k not in SF]
-        for k in vk:
-            run(up3, 1 if k < 12 else 4)
-            vote_v(rnd, k)
-        run(up3)
-        run(first0)
-        for i in range(1, len(SF), 2):
-            vote_s(rnd, SF[i:i + 2])
-        early = SF[:1] + vk[:-1]
-        for k in early:
-            vote_mm("VA", k, 8, 8)
-        ca, c = courts(8 * rnd, "MA", "PK")
-        cb, d = courts(32 + 8 * rnd, "MA", "PQ")
-        run(ca, 1)
-        for k in vk[-1:] + SF[1:3]:
-            vote_mm("VA", k, 8, 8)
-        run(cb, 1)
-        for k in SF[3:]:
-            vote_mm("VA", k, 8, 8)
-        third = vote_send(64 + 8 * rnd, "VA", 8, 128, "vc%d" % rnd)
+        vote_s(rnd, [2])
+        vote_v(rnd, 0)
+        vote_v(rnd, 1)
+        for i, q in enumerate((0, 1, 2)):
+            vote_mm("VA", 0, q, 32 * me + 8 * q, i == 0, i == 2)
+        sv = CFG["sv"]
+        vote_s(rnd, sv[:1], 0)
+        vote_send(rnd, 0, "VA", 0)
+        if rnd == 0:
+            for q in range(3):
+                keep0(C("MB", 128 * q, 128, p=(0, 96)), [[-1, 8], [-24, 4], [0, 4]], -8 * q)
 
-        def names1(rnd=rnd):
-            cp(C("SN", 192 * rnd, 64), ind(C("NM", 256, 64), C("OF2", 0, 4)))
-            send_each("nb%d" % rnd, lambda r: C("SN", 192 * rnd + 16 * r, 16), lambda r: A("LN1", 4 * rnd + r))
-            dma(A("LN1", 4 * rnd + me), C("SN", 192 * rnd + 16 * me, 16))
-
-        def last_of(d):
-            return lambda: ts(C("SM", d + 28, 4), C("SM", d + 20, 4), C("SM", d + 2), ALU.not_equal, -3.0, ALU.add)
-
-        cb += [last_of(d), lambda d=d: tt(C("SM", d + 28, 4), C("SM", d + 28, 4), C("SM", d + 24, 4), ALU.add),
-               lambda d=d: ts(C("OF2", 0, 4), C("SM", d + 28, 4), 16.0, ALU.mult, acol, ALU.add), names1]
-        qme = C("SM", c + 3)
-        ca += [lambda: ts(qme, C("SM", c + 20 + me), C("SM", c + 2), ALU.not_equal, C("SM", c + 24 + me), ALU.add),
-               lambda: ts(C("O48", 0, 3), C("C48", 0, 3), qme, ALU.add, 64.0, ALU.mult),
-               lambda: cp(C("N48", 0, 48), ind(C("NM", 0, 256), C("O48", 0, 3)))]
-        run(ca, len(ca) - CFG["mix"])
-        while ca:
-            run(cb, 1)
-            run(ca, 1)
-        lists0 = [lambda c=c: ts(C("SM", c + 28, 4), C("SM", c + 20, 4), C("SM", c + 2), ALU.not_equal),
-                  lambda c=c: tt(C("SM", c + 28, 4), C("SM", c + 28, 4), C("SM", c + 24, 4), ALU.add)]
-        lists0 += [(lambda m=m, c=c: ts(C("OF0", m, 4, step=4), C("SM", c + 28, 4), 64.0, ALU.mult, C("PC", 14 + m),
-                                        ALU.add)) for m in range(4)]
-        cc, e = courts(64 + 8 * rnd, "MB", "PK")
-        st = [None]
-
-        def names2(rnd=rnd):
-            base = 192 * rnd + 64
-            cp(C("SN", base, 128), ind(C("NM", 320, 128), A("OF1")))
-            send_each("nc%d" % rnd, lambda r: C("SN", base + 32 * r, 32), lambda r: A("LN2", 4 * rnd + r))
-            dma(A("LN2", 4 * rnd + me), C("SN", base + 32 * me, 32))
+        def weigh(r, on, rnd=rnd):
+            p = (32 * r, 32 * r + 24)
+            if on == "v":
+                ts(A("RR", p=p), A("WC", p=p), C("LX", 32 * r + 4 * rnd, p=p), ALU.mult)
+            else:
+                lin(A("RR", p=p), A("WC", p=p), C("LX", 32 * r + 4 * rnd, p=p))
+        up3 = update(3, 1, rnd - 1) if rnd else []
+        later = [4, 5, 6, 8, 9, 10, 12, 13, 14]
+        vote_s(rnd, sv[:1], 1)
+        weigh(me, "s")
+        for k in later:
+            if k == 12:
+                run(up3)
+            if k in sv[1:]:
+                vote_s(rnd, [k])
+            elif k not in sv:
+                vote_v(rnd, k)
+            else:
+                continue
+            if k < 12 and k not in sv:
+                run(up3, CFG["u3"] if k > 4 else 0)
+        if rnd == 0:
+            cp(C("NM", 0, 192), A("L0"))
+        for i, k in enumerate(later):
+            vote_mm("CT", 128, k, 8 * i, i == 0, i == 8)
+        if CFG["wv"] == "v":
+            vote_send(rnd, 1, "CT", 128)
+        for r in peers:
+            weigh(r, CFG["wv"])
+        mm([(C("PK", 0, 144), A("LH"), A("RR"), True, True)])
+        if CFG["wv"] != "v":
+            vote_send(rnd, 1, "CT", 128)
+        if rnd == 0:
+            keep0(A("MC"), [[-4, 3], [-16, 8], [0, 16]], 0)
+            idx_mm()
+            run(defer, 4)
+        ts(C("PA", 16, 64), C("PK", 80, 64), 0.0, ALU.is_gt)
+        tt(A("PS"), C("PK", 0, 80), A("PA"), ALU.add)
+        scan(A("PM"), A("PS"), A("RS"), -1e9, ALU.max, ALU.add)
+        ts(C("O48", 0, 3), C("C48", 0, 3), C("PM", 30 + 16 * me), ALU.add, C("PM", 14), ALU.subtract)
+        cp(names(rnd, 0), ind(C("NM", 0, 192), C("O48", 0, 3)))
+        c = sm(8)
+        lists0 = [lambda c=c: ts(C("SM", c, 4), C("PM", 30, 4, step=16), C("PM", 14), ALU.subtract, a4, ALU.is_equal),
+                  lambda c=c: tt(C("SM", c + 4, 4), C("SM", c, 4), C("XT", 32, 4), ALU.mult),
+                  lambda c=c: red(C("SM", c), C("SM", c + 4, 4), ALU.max),
+                  lambda c=c: ts(A("OF0"), A("CF"), C("SM", c), ALU.add)]
+        cc, e = courts(16 + 4 * rnd, "MB", "PK", 160)
 
         def bcast(e=e):
             tt(C("QB", 0, 4), C("SM", e + 28, 4), C("SM", e + 24, 4), ALU.add)
-            mm([(C("PQ", 4 * x, 4), C("MC", 128 * x, 128), C("QB", 0, 4), True, True) for x in range(2)])
+            mm([(C("PK", 192 + 4 * x, 4), C("MC", 128 * x, 128), C("QB", 0, 4), True, True) for x in range(3)])
 
-        first = cc.pop(0)
-        cc += [last_of(e), bcast, None]
-        cc += [(lambda x=x: ts(C("OF1", x, 4, step=2), C("PQ", 4 * x, 4), 16.0, ALU.mult, C("PC", 11 + x), ALU.add))
-               for x in range(2)]
-        cc += [names2, lambda: ts(C("OF2", 4, 8), C("PQ", 0, 8), 16.0, ALU.mult, acol, ALU.add)]
-        small = cb + lists0[:2]
+        def hand(b, rnd=rnd):
+            at = 192 * rnd + 64 * b - 64
+            win = C("NM", 208, 128) if b < 3 else C("NM", 336, 64)
+            cp(C("SN", at, 64), ind(win, C("OF2", 4 * b - 4, 4)))
+            send_each("n%s%d" % ("abcd"[b], rnd), lambda r: C("SN", at + 16 * r, 12), lambda r: names(rnd, b, 12 * r, 12))
+            dma(names(rnd, b, 12 * me, 12), C("SN", at + 16 * me, 12))
 
-        def hook0(n, rnd=rnd, small=small, cc=cc, first=first, st=st, third=third):
-            if n == 0:
-                third()
+        cc += [lambda e=e: ts(C("SM", e + 28, 4), C("SM", e + 20, 4), C("SM", e + 2), ALU.not_equal, C("PC", 5), ALU.add),
+               bcast, None, lambda: ts(A("OF2"), C("PK", 192, 12), 16.0, ALU.mult, acol, ALU.add), lambda: hand(1)]
+        rest = [lambda: hand(2), lambda: hand(3)]
+        small = []
+
+        def hook0(n, rnd=rnd, small=small, cc=cc, rest=rest):
             if n == CFG["cb"]:
-                run(small)
-                first()
+                run(cc, 1)
                 small += cc
-            if n == "gather":
-                st[0] = stale(rnd, 1, CFG["st1"])
+            if n == CFG["cf"]:
+                run(small)
+                small += rest
+            if n == CFG["cg"]:
+                stale(rnd, 1)
 
-        hearing(rnd, 0, None, small, [[], []],
-                [[lambda: run(small, CFG["win"])], [lambda: compact(rnd, 1), lambda: run(small, 2)]], hook0)
-        u0, u1, u2 = update(0, rnd), update(1, rnd), update(2, rnd)
-        plan = {1: ([lambda: compact(rnd, 2)] + lists0[2:], [[lambda: compact(rnd, 3)], []],
-                    [u0[0:1] + late[0:1], u0[1:2] + late[1:2]]),
-                2: ([], [ends, []], [u0[2:3] + late[2:3], u0[3:4]]),
-                3: ([], [u1[1:], u2[2:]], [u1[0:1], [u2[0], u0[4], u2[1], u0[5]] + u0[6:]])}
-        late, ends = [], []
+        off = hearing(rnd, 0, 64.0, small, [[], []], [[lambda: run(small, CFG["win"])], [], hook0])
+        u0, u12 = update(0, 1, rnd), update(1, 2, rnd)
+        plan = {1: ([], [[], []], [lists0[0:2] + late, lists0[2:] + u0[0:1]]),
+                2: ([], [[], []], [u0[1:2], u0[2:3]]),
+                3: ([], [u0[3:], []], [u12[0:1] + ends, u12[1:] + ends2])}
+        late, ends, ends2 = [], [], []
         for b in range(1, 4):
-            def hook(n, b=b, rnd=rnd, st=st):
-                if n == "gather" and b < 3:
-                    st[0] = stale(rnd, b + 1, CFG["st"])
-            hearing(rnd, b, st[0], plan[b][0], plan[b][1], plan[b][2], hook)
+            off = hearing(rnd, b, off, plan[b][0], plan[b][1], plan[b][2])
 
     outs = [dma(T.yf[:], TBr)]
-    run(update(3, RO - 1))
-    cp(C("YR", 0, 4), C("FI", 12, 4, step=64))
-    cp(C("YR", 4, 12), C("FI", 268, 12, step=16))
+    run(update(3, 1, RO - 1))
+    cp(C("YR", 0, 4), C("FI", 192, 4))
+    cp(C("YR", 4, 12), C("FI", 220, 12, step=16))
     outs.append(dma(T.yr[:], A("YR")))
     cp(A("X1"), ind(A("NM"), C("SL", 60, 24)))
     vtr(A("X2"), A("X1"))

@@ -9,10 +9,13 @@ CP = float(3 * 2 ** 23)
 C1 = float(3 * 2 ** 28)
 C2 = float(3 * 2 ** 39)
 UP = float(2 ** 17)
+CG = float(3 * 2 ** 29)
+UH = float(2 ** 16)
+CH = float(3 * 2 ** 38)
+C3 = float(3 * 2 ** 35)
 BF, F, U, I = "bfloat16", "float32", "uint16", "int32"
-CFG = {"gv": [384, 448, 448, 384], "g0": 448, "help": [768, 768, 768, 0, 0], "pb": 5, "hv": [5, 12, 12], "nd": 2,
-       "dm": [0, 0, 0, 0], "dc": [0, 0, 0, 0], "sv": [6, 10], "u3": 1, "wv": "v", "so": [0, 0, 0],
-       "cr": [1, 0, 0, 1], "sa": 1, "sf": 1, "per": 3, "pa": 2, "cb": 0, "cf": 2, "cg": 11, "win": 0, "df": 3}
+CFG = {"gv": [384, 448, 448, 384], "ns": 3, "pb": 5, "hv": [5, 12, 12], "sv": [6, 10], "u3": 1, "wv": "v",
+       "sf": 1, "per": 1, "cb": 0, "cf": 2, "cg": 11, "win": 0, "df": 3, "yp": 2}
 
 
 def _sb(n, d):
@@ -20,23 +23,24 @@ def _sb(n, d):
 
 
 SCRATCH = {
-    "TB": _sb(TR + W, BF), "ZZ": _sb(2352, BF), "ZS": _sb(840, BF), "JS": _sb(768, BF), "KK": _sb(784, BF),
-    "IN": _sb(768, BF), "SC": _sb(768, BF), "SW": _sb(1568, BF), "DM": _sb(768, BF), "NR": _sb(768, BF),
+    "TB": _sb(2 * TR + W, BF), "ZZ": _sb(784, BF), "ZS": _sb(840, BF), "JS": _sb(768, BF), "KK": _sb(784, BF),
+    "YY": _sb(6 * 784, BF), "SC": _sb(392, BF), "SW": _sb(784, BF), "DM": _sb(768, BF), "NR": _sb(768, BF),
+    "RW": _sb(776, BF), "ID": _sb(128, F), "CC": _sb(96, BF), "BQ": _sb(128, BF),
     "I0": _sb(768, BF), "I1": _sb(768, BF), "SM": _sb(512, F), "SB": _sb(256, BF),
     "NE": _sb(3072, BF), "SG": _sb(384, BF), "TH": _sb(576, BF), "S1": _sb(32, F), "JU": _sb(4, U),
     "CL": _sb(192, I), "RU": _sb(16, BF), "YR": _sb(16, BF), "X1": _sb(384, F), "X2": _sb(384, F), "YC": _sb(192, F),
     "NM": _sb(400, F), "PB": _sb(400, F), "BT": _sb(400, BF), "FI": _sb(400, BF), "VO": _sb(256, U),
-    "L0": _sb(192, U), "LX": _sb(128, F), "SN": _sb(768, U), "LN": _sb(768, U), "DC": _sb(384, F), "DX": _sb(384, F),
+    "L0": _sb(192, U), "LX": _sb(128, F), "SN": _sb(768, U), "LN": _sb(768, U), "DX": _sb(776, F),
     "MSG": _sb([4, 10, 192], BF), "FL0": _sb(896, BF),
-    "NM8": _sb(96, F), "GG": _sb(48, F), "OS": _sb(48, U), "O48": _sb(4, U),
+    "NM8": _sb(96, F), "OS": _sb(48, U), "O48": _sb(4, U),
     "OF0": _sb(16, U), "OF2": _sb(12, U), "QB": _sb(8, BF),
     "PI": _sb(8, I), "PC": _sb(64, F), "XI": _sb(160, F), "XD": _sb(128, F), "XT": _sb(128, F),
     "UU": _sb(144, BF), "BP": _sb(128, BF), "BM": _sb(256, BF),
-    "MB": _sb(384, F), "MC": _sb(384, BF), "IDX": _sb(384, BF), "W32": _sb(128, BF), "GQ": _sb(256, BF),
+    "MB": _sb(384, F), "MC": _sb(384, BF), "W32": _sb(128, BF), "GQ": _sb(256, BF),
     "LH": _sb(128, BF), "WC": _sb(144, BF), "RR": _sb(144, BF), "XP": _sb(432, F),
     "PA": _sb(80, F), "PS": _sb(80, F), "PM": _sb(80, F), "RS": _sb(80, F), "CF": _sb(16, F), "C6": _sb(8, F),
     "CR": _sb(8, F), "UN": _sb(1160, BF), "C48": _sb(4, F), "SL": _sb(128, U),
-    "D0": ("psum", [128, 512], F), "D1": ("psum", [128, 512], F), "CT": ("psum", [128, 512], F),
+    "DD": ("psum", [128, 1024], F), "CT": ("psum", [128, 512], F),
     "VA": ("psum", [128, 512], F), "VB": ("psum", [128, 512], F), "PK": ("psum", [128, 512], F),
 }
 POOL = {"v": 42, "s": 30, "t": 22, "y": 8, "g": 10}
@@ -66,9 +70,9 @@ def rank_program(g, core, T, topo):
         for r in rows:
             m |= row << (r * shape[-1])
         if SCRATCH[name][0] == "psum":
-            m = 1
+            m = (2 << rg[-1] // 512) - (1 << rg[0] // 512)
         ps = slice(None) if p is None else slice(p[0], p[1])
-        if name in ("RR", "IDX"):
+        if name == "RR":
             m = 15 if p is None else (2 << (p[1] - 1) // 32) - (1 << p[0] // 32)
         return (T[name][tuple([ps] + ix)], [(name, m)])
 
@@ -104,7 +108,7 @@ def rank_program(g, core, T, topo):
         for (name, m), wr in acc:
             psum = SCRATCH[name][0] == "psum"
             if psum:
-                seen[name] = [e for e in seen[name] if e[3] == q]
+                seen[name] = [e for e in seen[name] if e[3] == q or not e[0] & m]
             elif wr:
                 seen[name] = [e for e in seen[name] if e[0] & ~m]
             seen[name].append([m, n, wr, q])
@@ -158,7 +162,7 @@ def rank_program(g, core, T, topo):
 
     def gp(call, o, ins):
         n = rec("g", [call], [o], ins)
-        part = o[1][0][0] in ("RR", "IDX")
+        part = o[1][0][0] == "RR"
         if pool[0] is not None and (part or pool[1]):
             ops[n][2].add(pool[0])
         pool[0], pool[1] = n, part
@@ -236,7 +240,7 @@ def rank_program(g, core, T, topo):
             if f:
                 f()
 
-    TBr, TBw = C("TB", 0, W), C("TB", 0, TR + W)
+    TBr, TBw = C("TB", 0, W), A("TB")
 
     dma(A("CL"), T.cl[:])
     dma(A("RU"), T.ru[:])
@@ -258,8 +262,13 @@ def rank_program(g, core, T, topo):
     iota(C("RR", 0, 80, p=blk[0]), [[0, 5], [-8192, 4], [0, 4]], 24576)
     iota(C("RR", 0, 80, p=blk[1]), [[0, 20], [-8, 4]], 24)
     xs = lambda n, p=None: C("XI", 0, n, p=p)
-    ND = CFG["nd"]
-    PD = 768 // ND
+    PD = 384
+    NS = CFG["ns"]
+    STEP = [UP / 32, 1.0 / 16, 0.125, 0.25, 0.5]
+    unit = {NS: STEP[NS]}
+    for n in range(NS, 4):
+        unit[n + 1] = unit[n] * UH / (16 >> n)
+    yt = lambda n, i=0, k=6: C("YY", 784 * n + 768 + i, k)
     defer = []
     for n in range(1, 5):
         defer.append(lambda n=n: sfill(C("UN", 290 + 96 * n, 96), xs(96), (-1.0 if n % 2 else 1.0) / 16384))
@@ -267,9 +276,17 @@ def rank_program(g, core, T, topo):
     defer.append(lambda: sfill(C("ZS", 768, 40), xs(40), 0.0))
     for i, c in ((0, -4 * C1), (2, C2), (3, -C2), (4, -UP / 2), (36, 2 * UP)):
         defer.append(lambda i=i, c=c: sfill(C("ZS", 768 + i), xs(1), c))
-    for i, c in enumerate((-C1, C2, 95.0 * UP)):
-        sfill(C("ZZ", 768 + i, 3, step=784), xs(3), c)
-    sfill(C("ZZ", 2338), xs(1), 79.5 / 32 * UP)
+    for i, c in enumerate((-C1, C2, 79.5 / 32 * UP)):
+        sfill(C("ZZ", 768 + i), xs(1), c)
+    early = [lambda i=i, c=c: sfill(yt(5, i, 1), xs(1), c) for i, c in enumerate((-CG, 64.0, CH, -CH, 63.5 * UH, 0.0))]
+    early += [lambda n=n: lin(yt(n), yt(5), unit[n]) for n in range(NS, 5)]
+    early += [lambda n=n: sfill(yt(n, 4, 1), xs(1), -UH / 2 * unit[n]) for n in range(NS, 4)]
+    early.append(lambda: lin(A("BQ"), C("BM", 0, 128), -2.0 / UH / unit[4]))
+    for i, c in enumerate((-384.0, CK, -CK)):
+        defer.append(lambda i=i, c=c: sfill(C("RW", 767 + i), xs(1), c))
+    for i, c in enumerate((C3, -C3)):
+        defer.append(lambda i=i, c=c: sfill(C("CC", 48 * i, 48), xs(48), c))
+    defer.append(lambda: lin(C("CR", 0, 6), C("C6", 0, 6), 1.0, CN - 64.0))
     sfill(C("LX", 32 * me + 16, 16, p=(96, 128)), xs(16, (96, 128)), (384.0 + N - me) / 64)
     sfill(C("W32", 0, 128, p=(0, 96)), xs(128, (0, 96)), 1.0 / 32)
     sfill(A("C6"), xs(8), 0.0)
@@ -315,11 +332,11 @@ def rank_program(g, core, T, topo):
     send_all("n0", C("L0", 48 * me, 48), lambda r: C("L0", 48 * r, 48))
     cp(A("VO"), ind(A("X2"), C("SL", 24, 16)))
     cp(C("NM", 208, 192), C("VO", 64, 192))
-    iota(C("IDX", 0, PD, p=(0, 32)), [[0, PD // 128], [-1, 128]])
-    iota(C("IDX", 0, PD, p=(32, 64)), [[-128, PD // 128], [0, 128]])
     sfill(C("KK", 769), xs(1), -C2)
     sfill(A("MB"), A("X1"), 2.0)
-    sfill(C("IDX", 0, PD, p=(64, 96)), A("X1", p=(64, 96)), 384.0)
+    fill(C("RW", 0, 767), 1.0)
+    fill(C("DD", 896, 2), -1e12)
+    ts(A("ID"), C("XI", 0, 128), pcol, ALU.is_equal)
     ts(C("PC", 48), qq, 0.0, ALU.is_equal, 16384.0, ALU.mult)
     ts(C("PC", 49), qq, 1.0, ALU.is_equal, 16.0, ALU.mult)
     ts(C("PC", 50), qq, 2.0, ALU.is_equal, -1.0, ALU.mult)
@@ -328,8 +345,9 @@ def rank_program(g, core, T, topo):
     for x in range(3):
         sfill(A("MSG", slice(0, 4), slice(3 - me, 7 - me), slice(64 * x + 16 * me + 13, 64 * x + 16 * me + 16)),
               xs(48), 0.0)
-    lin(A("BP"), C("BM", 0, 128), -2.0 / UP)
-    ts(A("UU"), C("XI", 0, 144), C("PC", 18), ALU.is_equal)
+    lin(A("BP"), C("BM", 0, 128), -2.0 / UH)
+    ts(A("UU"), C("XI", 0, 144), C("PC", 18), ALU.is_equal, 896.0, ALU.mult)
+    run(early)
     ts(C("XP", 0, 80), C("XP", 0, 80), rr, ALU.is_equal, C("PC", 48), ALU.mult)
     ts(C("XP", 144, 80), C("XP", 144, 80), rr, ALU.is_equal, C("PC", 49), ALU.mult)
     ts(C("XP", 80, 64), C("XP", 80, 64), rr, ALU.is_equal, C("PC", 50), ALU.mult)
@@ -442,32 +460,27 @@ def rank_program(g, core, T, topo):
                 act(C("UN", 386 + 96 * n, k), C("UN", 290 + 96 * n, k), AF.Sign, bias=C("SM", c), scale=-8192.0, acc=t)
         return t, c
 
-    def offset(t, rnd, b):
+    def offset(t, rnd, b, small):
         off, a = sb(), C("SM", t[1] + 2)
-        if CFG["so"][b]:
-            c = sm(2)
-            act(C("SM", c), C("SM", t[1]), AF.Sign, bias=0.5)
-            lin(a, C("SM", c), -0.5, t[0])
-            act(C("SM", c + 1), aux(rnd, b, 2), AF.Sign, bias=a)
-            lin(off, C("SM", c + 1), -0.5, a)
-            return off
         ts(a, C("SM", t[1]), 0.0, ALU.is_ge, t[0], ALU.subtract)
+        run(small, 1)
         ts(off, aux(rnd, b, 2), a, ALU.is_lt, a, ALU.subtract)
         return off
 
-    def idx_mm():
-        for x in range(ND):
-            p = (0, 96 - 32 * x)
-            mm([(C("D%d" % x, 0, PD), A("W32", p=p), C("IDX", 0, PD, p=p), True, False)])
+    def count(n, u):
+        scan(C("SC", 0, 387), C("YY", 784 * n, 387, step=2), C("YY", 784 * n + 1, 387, step=2),
+             (CG - 128.0 * 384 + UH / 2) * u, ALU.add, ALU.add)
+        return C("SC", 386)
 
-    def hearing(rnd, b, off, small, later, big):
+    def hearing(rnd, b, ahead, small, later, big):
         h = 4 * rnd + b
         par = h % 2
-        zc = lambda a, n, step=1: C("ZZ", 784 * (par if b else 2) + a, n, step=step)
+        zc = lambda a, n, step=1: C("ZZ", a, n, step=step)
+        yc = lambda r, a=0, n=768: C("YY", 784 * r + a, n)
+        dd = lambda x: C("DD", 128 + PD * x, PD)
         Z = zc(0, 768)
         n8 = C("NM8", 48 * par, 48)
         gv = CFG["gv"][b]
-        g0 = min(gv, CFG["g0"])
         nxt = []
 
         def at(n):
@@ -475,112 +488,76 @@ def rank_program(g, core, T, topo):
                 big[2](n)
             if b < 3 and n == CFG["hv"][b]:
                 nxt.append(halve())
-        ts(zc(0, g0), ind(TBr, names(rnd, b, 0, g0 // 16)), off, ALU.add)
-        act(zc(gv, 768 - gv), ind(TBr, names(rnd, b, gv // 16, 48 - gv // 16)), AF.Identity, bias=off)
-        if gv > g0:
-            ts(zc(g0, gv - g0), ind(TBr, names(rnd, b, g0 // 16, (gv - g0) // 16)), off, ALU.add)
-        dms = CFG["dm"][b]
-        if 0 < b < 3 and not dms:
+        ts(zc(0, gv), ind(TBr, names(rnd, b, 0, gv // 16)), 64.0, ALU.add)
+        if gv < 768:
+            act(zc(gv, 768 - gv), ind(TBr, names(rnd, b, gv // 16, 48 - gv // 16)), AF.Identity, bias=64.0)
+        if 0 < b < 3:
             stale(rnd, b + 1)
-        c = sm(2)
-        if not CFG["cr"][b]:
-            ts(C("CR", 0, 6), C("C6", 0, 6), off, ALU.subtract, CN, ALU.add)
-        elif b:
-            lin(C("SM", c), off, -1.0, CN)
-            lin(C("CR", 0, 6), C("C6", 0, 6), 1.0, C("SM", c))
-        else:
-            lin(C("CR", 0, 6), C("C6", 0, 6), 1.0, CN - off)
         if b == 0:
-            lin(n8, ind(C("NM", 0, 192), C("O48", 0, 3)), 1.0 / TR)
+            lin(n8, ind(C("NM", 0, 192), C("O48", 0, 3)), 1.0)
         for x in range(2):
-            mm([(C("D%d" % x, 0, PD), C("BM", 128 * x * dms, 128), zc(PD * x, PD), False, False)])
-        scan(C("SW", 784 * par, 771), zc(0, 771), C("KK", 0, 771), C1 + 16512.0, ALU.add, ALU.add)
-        w = C("SW", 784 * par + 770)
+            mm([(dd(x), C("BM", 0, 128), zc(PD * x, PD), True, False)])
         if b:
-            ts(n8, names(rnd, b), 1.0 / TR, ALU.mult)
-        if b == 0:
+            small += later[0]
+            off = offset(ahead, rnd, b - 1, small)
+            cp(n8, names(rnd, b))
+            cuts = [0, gv, 768] if CFG["yp"] == 2 and gv < 768 else [0, 768]
+            for a, e in zip(cuts, cuts[1:]):
+                ts(yc(5, a, e - a), zc(a, e - a), off, ALU.add, -95.5, ALU.add)
             run(small, 1)
-            for n, s in enumerate([UP / 32, 1.0 / 16, 0.125, 0.25, 0.5]):
+            row, w = 5, count(5, 1.0)
+            run(small, 1)
+        else:
+            scan(C("SW", 0, 771), zc(0, 771), C("KK", 0, 771), C1 + 16512.0, ALU.add, ALU.add)
+            w = C("SW", 770)
+            run(small, 1)
+            for n, s in enumerate(STEP):
                 at(n)
-                ns = CFG["help"][n]
-                nv = 768 - ns
-                c = sm()
-                a = C("SM", sm())
-                if ns:
-                    act(C("JS", 0, ns), zc(nv, ns), AF.Sign, bias=w, scale=-s, acc=C("SM", c))
-                sa = CFG["sa"] and 0 < ns < 768
-                if sa:
-                    lin(a, w, 2.0 / UP if n == 0 else 2.0, -0.5)
-                run(defer, CFG["df"] if n < 3 else 99)
-                if nv:
-                    ts(C("IN", 0, nv), zc(0, nv), s, ALU.mult, w, ALU.is_gt)
-                if not sa:
-                    ts(a, w, 2.0 / UP if n == 0 else 2.0, ALU.mult, -0.5, ALU.add)
-                run(small, CFG["pa"] if nv else CFG["pb"])
-                w = sb()
-                if not nv:
+                if n < NS:
+                    c = sm()
+                    a = C("SM", sm())
+                    act(A("JS"), Z, AF.Sign, bias=w, scale=-s, acc=C("SM", c))
+                    run(defer, CFG["df"] if n < NS - 1 else 99)
+                    ts(a, w, 2.0 / UP if n == 0 else 2.0, ALU.mult, -0.5 - (64 * STEP[NS] if n == NS - 1 else 0), ALU.add)
+                    run(small, CFG["pb"])
+                    w = sb()
                     ts(w, C("SM", c), 0.0, ALU.is_le, a, ALU.add)
-                elif ns:
-                    scan(C("SC", 0, nv), C("IN", 0, nv), C("IN", 0, nv), float(ns - 768), ALU.add, ALU.add)
-                    run(small, CFG["per"])
-                    ts(w, C("SC", nv - 1), C("SM", c), ALU.is_ge, a, ALU.add)
                 else:
-                    scan(C("SC", 0, 384), C("IN", 0, 384), C("IN", 384, 384), -383.5, ALU.add, ALU.add)
+                    if n == NS:
+                        ts(yc(n), Z, s, ALU.mult, w, ALU.subtract)
+                    else:
+                        ts(yc(n), yc(n - 1), UH / (32 >> n), ALU.mult, w, ALU.subtract)
                     run(small, CFG["per"])
-                    ts(w, C("SC", 383), 0.0, ALU.is_gt, a, ALU.add)
+                    w = count(n, unit[n])
                 run(small, 1)
-        small += later[0]
+            row = 4
+            small += later[0]
         at(11)
         for x in range(2):
-            if x and dms:
-                act(C("DM", PD, PD), zc(PD, PD), AF.Relu, bias=w, scale=-UP)
-            elif b:
-                ts(C("DM", PD * x, PD), zc(PD * x, PD), UP, ALU.mult, w, ALU.max)
-            else:
-                ts(C("DM", PD * x, PD), zc(PD * x, PD), w, ALU.max, UP, ALU.mult)
-            mm([(C("D%d" % x, 0, PD), A("BP"), C("DM", PD * x, PD), False, True)])
-        if 0 < b < 3 and dms:
-            stale(rnd, b + 1)
-        c = sm(4)
-        cd = CFG["dc"][b]
-        if cd:
-            lin(A("DC"), C("D0", 0, PD), 1.0)
+            ts(C("DM", PD * x, PD), yc(row, PD * x, PD), UH, ALU.mult, w, ALU.max)
+            mm([(dd(x), A("BP" if b else "BQ"), C("DM", PD * x, PD), False, True)])
         if b == 3:
-            lin(C("SM", c + 3), off, -1.0)
-            lin(A("I0"), Z, 1.0, C("SM", c + 3))
+            lin(A("I0"), Z, 1.0, -64.0)
         at(12)
         run(big[0])
         at(5)
-        if cd:
-            scan(A("DX"), C("D1", 0, PD), A("DC"), -1e9, ALU.max, ALU.max)
-            top = C("DX", PD - 1)
-            at(6)
-            run(small, 1)
-            ts(C("SM", c), top, CK, ALU.add, CK, ALU.subtract)
-        else:
-            red(C("SM", c + 1), C("D0", 0, PD), ALU.max)
-            at(6)
-            red(C("SM", c + 2), C("D1", 0, PD), ALU.max)
-            run(small, 1)
-            top = C("SM", sm())
-            ts(C("SM", c), C("SM", c + 1), C("SM", c + 2), ALU.max, CK, ALU.add)
-            ts(top, C("SM", c + 1), C("SM", c + 2), ALU.max, 384.0, ALU.subtract)
+        scan(C("DX", 0, 770), C("DD", 128, 770), C("RW", 0, 770), -1e9, ALU.max, ALU.add)
+        mm([(C("CT", 0, 48), A("W32", p=(0, 32)), C("CC", 0, 48, p=(0, 32)), True, False)])
         at(7)
         run(small, 1)
         ju = C("JU", 2 * par)
-        if cd:
-            ts(ju, C("SM", c), top, ALU.subtract, 384.0, ALU.add)
-        else:
-            ts(ju, C("SM", c), CK, ALU.subtract, top, ALU.subtract)
+        ts(ju, C("DX", 769), C("DX", 767), ALU.subtract, 383.0, ALU.add)
         run(small, 1)
         s1 = 16 * par
         ts(C("S1", s1, 16), ind(Z, ju), -1.0, ALU.mult, CN, ALU.add)
         at(8)
         run(small, 1)
         for e in range(2):
-            ts(C("NR", 384 * e, 384), zc(e, 384, 2), C("S1", s1), ALU.add, CN, ALU.is_equal)
-            mm([(C("CT", 0, 48), C("UU", 15 - 2 * i - e, 128), C("NR", 384 * e + i, 48, step=8), e + i == 0,
-                 e + i == 8) for i in range(8)])
+            ts(C("NR", 384 * e, 384), zc(e, 384, 2), C("S1", s1), ALU.add, CN, ALU.not_equal)
+            mm([(C("CT", 0, 48), C("UU", 15 - 2 * i - e, 128), C("NR", 384 * e + i, 48, step=8), False, False)
+                for i in range(8)] +
+               ([(C("CT", 0, 48), A("W32", p=(0, 32)), C("CC", 48, 48, p=(0, 32)), False, False),
+                 (C("CT", 0, 48), A("ID"), n8, False, True)] if e else []))
         mc = 64 * b - 64 + 16 * me
         if b == 0:
             tt(aux(rnd, b, 0, 4), C("CR", 3, 4), C("S1", s1, 4), ALU.subtract)
@@ -595,15 +572,12 @@ def rank_program(g, core, T, topo):
             act(A("I1"), Z, AF.Sign, bias=rho, scale=-1.0)
         else:
             ts(A("I0"), Z, rho, ALU.subtract, -1.0, ALU.min)
-            ts(A("I1"), Z, off, ALU.subtract, aux(rnd, b, 1), ALU.max)
+            ts(A("I1"), Z, 64.0, ALU.subtract, aux(rnd, b, 1), ALU.max)
         at(10)
         run(big[1])
         small += later[1]
-        ts(fl, C("CT", 0, 48), 11.5, ALU.is_lt)
-        run(small, 1)
-        tt(A("GG"), fl, n8, ALU.add)
-        run(small, 1)
-        ts(A("OS"), A("GG"), float(TR), ALU.mult)
+        cp(A("OS"), C("CT", 0, 48))
+        ts(fl, C("CT", 0, 48), float(TR), ALU.is_ge)
         run(small)
         tag = "f%s%d" % ("abcd"[b], rnd)
         if b == 0:
@@ -613,9 +587,7 @@ def rank_program(g, core, T, topo):
             send_each(tag, lambda r: A("MSG", rnd, 3 - me + r, slice(mc, mc + 16)),
                       lambda r: A("MSG", rnd, 3, slice(64 * b - 64 + 16 * r, 64 * b - 48 + 16 * r)))
         tt(ind(TBw, A("OS")), A("I0"), A("I1"), ALU.add)
-        if h + 1 < 4 * RO:
-            idx_mm()
-        return offset(nxt[0], rnd, b) if b < 3 else None
+        return nxt[0] if b < 3 else None
 
     for rnd in range(RO):
         vote_s(rnd, [2])
@@ -664,7 +636,6 @@ def rank_program(g, core, T, topo):
             vote_send(rnd, 1, "CT", 128)
         if rnd == 0:
             keep0(A("MC"), [[-4, 3], [-16, 8], [0, 16]], 0)
-            idx_mm()
             run(defer, 4)
         ts(C("PA", 16, 64), C("PK", 80, 64), 0.0, ALU.is_gt)
         tt(A("PS"), C("PK", 0, 80), A("PA"), ALU.add)

@@ -14,8 +14,7 @@ UH = float(2 ** 16)
 CH = float(3 * 2 ** 38)
 C3 = float(3 * 2 ** 35)
 BF, F, U, I = "bfloat16", "float32", "uint16", "int32"
-CFG = {"gv": [384, 448, 448, 384], "ns": 3, "pb": 5, "hv": [5, 12, 12], "sv": [6, 10], "u3": 1, "wv": "v",
-       "sf": 1, "per": 1, "cb": 0, "cf": 2, "cg": 11, "win": 0, "df": 3, "yp": 2}
+CFG = {"gv": [384, 352, 480, 320], "ns": 0, "nv": [1, 1, 1], "sf": [1, 1], "yp": 2, "vr": "ssv", "wg": ["vvv", "vss"], "n8": [0, 0], "af": [0, 1, 0, 0], "st": [0, 0, 0, 1], "rn": [1, 1, 0, 0], "start": "vvvvvvvvvvvvvvvvvvvvvvssssss", "votes": "v0 v1 s2 q2 m0 v5 m1 Y X s6 Y Y m2 v4 m4 r0 q6 P sa X v9 Z m5 Y Y m6 X v8 X r1 qa Y Z sc qc m8 Y Y ma ve Y m9 me P Q vd mc D P md r2 P Q P", "plan": [{"g": "DQNDDDDTGT", "0a": "Q", "0b": "QQ", "1a": "TG", "1b": "G", "2a": "G", "2b": "GL", "4a": "G", "4b": "G", "c": "G", "d": "GGG", "j": "G", "t": "G", "n": "G", "3a": "G"}, {"d": "LT", "x": "TA", "j": "B", "s": "B", "n": "A", "u": "B", "c": "A", "t": "N", "o": "B"}, {"c": "L", "y": "N", "t": "E", "a": "A"}, {"g": "U", "c": "U", "d": "EEWVE", "x": "EUEW", "n": "VUWF", "f": "WF", "u": "V", "a": "V", "y": "E", "o": "NI"}]}
 
 
 def _sb(n, d):
@@ -23,28 +22,29 @@ def _sb(n, d):
 
 
 SCRATCH = {
-    "TB": _sb(2 * TR + W, BF), "ZZ": _sb(784, BF), "ZS": _sb(840, BF), "JS": _sb(768, BF), "KK": _sb(784, BF),
+    "TB": _sb(2 * TR + W, BF), "ZZ": _sb(784, BF), "ZS": _sb(2520, BF), "JS": _sb(768, BF), "KK": _sb(784, BF),
     "YY": _sb(6 * 784, BF), "SC": _sb(392, BF), "SW": _sb(784, BF), "DM": _sb(768, BF), "NR": _sb(768, BF),
-    "RW": _sb(776, BF), "ID": _sb(128, F), "CC": _sb(96, BF), "BQ": _sb(128, BF),
+    "RW": _sb(128, F), "XR": _sb(120, F), "PH": _sb(544, BF), "PL": _sb(544, BF), "IB": _sb(256, BF), "ID": _sb(128, F), "CC": _sb(160, BF), "BQ": _sb(144, BF),
     "I0": _sb(768, BF), "I1": _sb(768, BF), "SM": _sb(512, F), "SB": _sb(256, BF),
-    "NE": _sb(3072, BF), "SG": _sb(384, BF), "TH": _sb(576, BF), "S1": _sb(32, F), "JU": _sb(4, U),
+    "NE": _sb(3072, BF), "SG": _sb(384, BF), "S1": _sb(32, F), "JU": _sb(4, U),
     "CL": _sb(192, I), "RU": _sb(16, BF), "YR": _sb(16, BF), "X1": _sb(384, F), "X2": _sb(384, F), "YC": _sb(192, F),
-    "NM": _sb(400, F), "PB": _sb(400, F), "BT": _sb(400, BF), "FI": _sb(400, BF), "VO": _sb(256, U),
-    "L0": _sb(192, U), "LX": _sb(128, F), "SN": _sb(768, U), "LN": _sb(768, U), "DX": _sb(776, F),
-    "MSG": _sb([4, 10, 192], BF), "FL0": _sb(896, BF),
-    "NM8": _sb(96, F), "OS": _sb(48, U), "O48": _sb(4, U),
-    "OF0": _sb(16, U), "OF2": _sb(12, U), "QB": _sb(8, BF),
+    "NM": _sb(544, F), "PB": _sb(544, F), "BT": _sb(544, BF), "FI": _sb(544, BF), "VO": _sb(256, U),
+    "L0": _sb([4, 2, 48], U), "LX": _sb(192, F), "SN": _sb(512, U), "LN": _sb(768, U), "DX": _sb(128, F),
+    "MSG": _sb([4, 10, 128], BF), "FL0": _sb(1792, BF),
+    "NM8": _sb(96, F), "OS": _sb(48, U), "O48": _sb(8, U),
+    "OF0": _sb(32, U), "OF2": _sb(8, U), "QB": _sb(8, BF),
     "PI": _sb(8, I), "PC": _sb(64, F), "XI": _sb(160, F), "XD": _sb(128, F), "XT": _sb(128, F),
-    "UU": _sb(144, BF), "BP": _sb(128, BF), "BM": _sb(256, BF),
-    "MB": _sb(384, F), "MC": _sb(384, BF), "W32": _sb(128, BF), "GQ": _sb(256, BF),
+    "UU": _sb(144, BF), "BP": _sb(144, BF), "BM": _sb(144, BF),
+    "MB": _sb(384, F), "MC": _sb(256, BF), "W32": _sb(128, BF), "GQ": _sb(256, BF),
     "LH": _sb(128, BF), "WC": _sb(144, BF), "RR": _sb(144, BF), "XP": _sb(432, F),
-    "PA": _sb(80, F), "PS": _sb(80, F), "PM": _sb(80, F), "RS": _sb(80, F), "CF": _sb(16, F), "C6": _sb(8, F),
-    "CR": _sb(8, F), "UN": _sb(1160, BF), "C48": _sb(4, F), "SL": _sb(128, U),
-    "DD": ("psum", [128, 1024], F), "CT": ("psum", [128, 512], F),
-    "VA": ("psum", [128, 512], F), "VB": ("psum", [128, 512], F), "PK": ("psum", [128, 512], F),
+    "PM": _sb(160, F), "RS": _sb(80, F), "CF": _sb(16, F), "C6": _sb(8, F),
+    "CR": _sb(8, F), "UN": _sb(2720, BF), "C48": _sb(4, F), "SL": _sb(128, U),
+    "DD": ("psum", [128, 512], F), "CT": ("psum", [128, 512], F),
+    "VB": ("psum", [128, 1024], F), "VA": ("psum", [128, 512], F), "VC": ("psum", [128, 512], F),
+    "PK": ("psum", [128, 512], F),
 }
 POOL = {"v": 42, "s": 30, "t": 22, "y": 8, "g": 10}
-ARR = ["n0"] + ["%s%d" % (k, r) for r in range(RO) for k in ("va", "vb", "nb", "nc", "nd", "fa", "fb", "fc", "fd")]
+ARR = ["n0"] + ["%s%d" % (k, r) for r in range(RO) for k in ("va", "vb", "vc", "nc", "nd", "fa", "fb", "fc", "fd")]
 SEMAPHORES = ["%s%d" % (q, i) for q in POOL for i in range(POOL[q])] + ["r" + a for a in ARR] + ["sent"]
 
 
@@ -207,18 +207,18 @@ def rank_program(g, core, T, topo):
         es = engines(me)
         m = sum(1 << e for e in es)
         sem = T.sem["r" + tag]
-        rec("g", [lambda: g.remote_dma_fused([RemoteDMATransfer(
-            dst_ids=[dst_id(r) for r in peers], dma_engine_mask=m, remote_sem=sem, srcs=[src[0]],
-            dsts=[slot(me)[0] for r in peers])], local_sem=T.sem.sent)], [], [src], inc=0)
+        part = RemoteDMATransfer(dst_ids=[dst_id(r) for r in peers], dma_engine_mask=m, remote_sem=sem, srcs=[src[0]],
+                                 dsts=[slot(me)[0] for r in peers])
+        rec("g", [lambda: g.remote_dma_fused([part], local_sem=T.sem.sent)], [], [src], inc=0)
         sent[0] += len(es)
         rec("r", [], [slot(r) for r in peers], [], fixed=("r" + tag, sum(len(engines(r)) for r in peers)))
 
     def send_each(tag, src, slot):
         sh = shares(me)
         sem = T.sem["r" + tag]
-        rec("g", [lambda: g.remote_dma_fused([RemoteDMATransfer(
-            dst_ids=[dst_id(r)], dma_engine_mask=sum(1 << e for e in sh[r]), remote_sem=sem, src=src(r)[0],
-            dst=slot(me)[0]) for r in peers], local_sem=T.sem.sent)], [], [src(r) for r in peers], inc=0)
+        parts = [RemoteDMATransfer(dst_ids=[dst_id(r)], dma_engine_mask=sum(1 << e for e in sh[r]), remote_sem=sem,
+                                   src=src(r)[0], dst=slot(me)[0]) for r in peers]
+        rec("g", [lambda: g.remote_dma_fused(parts, local_sem=T.sem.sent)], [], [src(r) for r in peers], inc=0)
         sent[0] += sum(len(sh[r]) for r in peers)
         rec("r", [], [slot(r) for r in peers], [], fixed=("r" + tag, sum(len(shares(r)[me]) for r in peers)))
 
@@ -249,12 +249,13 @@ def rank_program(g, core, T, topo):
     iota(C("XT", 0, 24), [[16, 12], [0, 2]])
     iota(A("XI"), [[1, 160]])
     iota(A("XD"), [[1, 8], [0, 16]])
-    iota(C("XT", 24, 4), [[128, 4]])
+    iota(C("XT", 24, 8), [[4, 2], [128, 4]])
     iota(C("XT", 32, 4), [[56, 4]])
     iota(C("XT", 40, 24), [[1, 12], [0, 2]])
     blk = [(32 * r, 32 * r + 32) for r in range(N)]
     fill(A("RR"), 0.0)
     fill(C("RR", 16, 64, p=blk[3]), 2.0)
+    fill(C("RR", 80, 64, p=blk[3]), 0.5)
     iota(C("XP", 0, 144), [[0, 9], [1, 4], [0, 4]])
     iota(C("XP", 144, 144), [[0, 36], [1, 4]])
     iota(C("XP", 288, 64), [[1, 4], [0, 16]])
@@ -270,36 +271,43 @@ def rank_program(g, core, T, topo):
         unit[n + 1] = unit[n] * UH / (16 >> n)
     yt = lambda n, i=0, k=6: C("YY", 784 * n + 768 + i, k)
     defer = []
-    for n in range(1, 5):
-        defer.append(lambda n=n: sfill(C("UN", 290 + 96 * n, 96), xs(96), (-1.0 if n % 2 else 1.0) / 16384))
-    defer.append(lambda: sfill(C("UN", 403, 63), xs(63), 1.0))
-    defer.append(lambda: sfill(C("ZS", 768, 40), xs(40), 0.0))
-    for i, c in ((0, -4 * C1), (2, C2), (3, -C2), (4, -UP / 2), (36, 2 * UP)):
-        defer.append(lambda i=i, c=c: sfill(C("ZS", 768 + i), xs(1), c))
-    for i, c in enumerate((-C1, C2, 79.5 / 32 * UP)):
+    zu = [1.0, UP / 64, UP / 64 * UP / 32]
+    ue = lambda nv, i: 900 * nv - 512 + (32 >> i)
+    u0 = lambda nv: ue(nv, nv) - 1
+    early = []
+    early += [(yt(5, i, 1), 1, c) for i, c in enumerate((-CG, 64.0, CH, -CH, 63.5 * UH, 0.0))]
+    early += [(C("ZS", 768, 40), 40, 0.0), (C("NM", 192, 16), 16, 0.0), (C("NM", 400, 16), 16, 0.0)]
+    early += [(yt(n), yt(5), unit[n]) for n in range(NS, 5)]
+    early += [(C("ZS", 768 + i), 1, c) for i, c in ((0, -4 * C1), (2, C2), (3, -C2), (4, -UP / 2))]
+    early += [(yt(n, 4, 1), 1, -UH / 2 * unit[n]) for n in range(NS, 4)]
+    for nv in sorted(set(CFG["nv"]), key=CFG["nv"].index):
+        early += [(C("UN", u0(nv) + 96 * j, 96), 96, (1.0 if j % 2 else -1.0) / 16384) for j in range(5 - nv)]
+        early += [(C("ZS", 840 * i + 768, 32), C("ZS", 768, 32), zu[i]) for i in range(1, nv)]
+        early += [(C("UN", ue(nv, 0), 63), 63, 1.0)]
+        early += [(C("ZS", 840 * nv - 68 + (64 >> nv)), 1, 128 * UP / (128 >> nv) * zu[nv - 1])]
+    early += [(C("XR", 32, 2), 2, -1e12), (C("XR", 112), 1, CK), (C("XR", 113), 1, -CK)]
+
+    def const(on):
+        if early:
+            o, x, c = early.pop(0)
+            if isinstance(x, int):
+                fill(o, c) if on == "v" else sfill(o, xs(x), c)
+            else:
+                ts(o, x, c, ALU.mult) if on == "v" else lin(o, x, c)
+    for i, c in enumerate((-C1, C2, (79.5 if NS else 15.5) / 32 * UP)):
         sfill(C("ZZ", 768 + i), xs(1), c)
-    early = [lambda i=i, c=c: sfill(yt(5, i, 1), xs(1), c) for i, c in enumerate((-CG, 64.0, CH, -CH, 63.5 * UH, 0.0))]
-    early += [lambda n=n: lin(yt(n), yt(5), unit[n]) for n in range(NS, 5)]
-    early += [lambda n=n: sfill(yt(n, 4, 1), xs(1), -UH / 2 * unit[n]) for n in range(NS, 4)]
-    early.append(lambda: lin(A("BQ"), C("BM", 0, 128), -2.0 / UH / unit[4]))
-    for i, c in enumerate((-384.0, CK, -CK)):
-        defer.append(lambda i=i, c=c: sfill(C("RW", 767 + i), xs(1), c))
+    defer.append(lambda: lin(A("BQ"), A("BM"), -2.0 / UH / unit[4]))
     for i, c in enumerate((C3, -C3)):
-        defer.append(lambda i=i, c=c: sfill(C("CC", 48 * i, 48), xs(48), c))
+        sfill(C("CC", 80 * i, 80), xs(80), c)
     defer.append(lambda: lin(C("CR", 0, 6), C("C6", 0, 6), 1.0, CN - 64.0))
-    sfill(C("LX", 32 * me + 16, 16, p=(96, 128)), xs(16, (96, 128)), (384.0 + N - me) / 64)
-    sfill(C("W32", 0, 128, p=(0, 96)), xs(128, (0, 96)), 1.0 / 32)
+    sfill(C("LX", 48 * me + 32, 16, p=(96, 128)), xs(16, (96, 128)), (768.0 + N - me) / 64)
+    sfill(A("W32", p=blk[0]), xs(128, blk[0]), 1.0 / 32)
+    sfill(A("W32", p=blk[1]), xs(128, blk[1]), 1.0 / 32 / TR)
     sfill(A("C6"), xs(8), 0.0)
     sfill(A("RS"), xs(80), 0.0)
-    sfill(C("PA", 0, 16), xs(16), 0.0)
     sfill(C("RS", 15, 5, step=16), xs(5), -float(2 ** 25))
     for o, c in ((C("C6", 4), 1.0), (C("C6", 5), -95.0), (C("CR", 6), CN)):
         sfill(o, xs(1), c)
-    where0(C("RR", 80, 64, p=blk[1]), [[1, 4], [-1, 4], [0, 4]], -1024.0)
-    where0(C("RR", 16, 64, p=blk[3]), [[1, 4], [0, 4], [-1, 4]], 1.0)
-    where0(C("RR", 0, 80, p=blk[2]), [[0, 5], [1, 4], [-1, 4]], -float(2 ** 23))
-    where0(C("RR", 80, 64, p=blk[1]), [[1, 4], [0, 4], [-1, 4]], -1024.0)
-    where0(C("RR", 16, 64, p=blk[3]), [[1, 4], [-1, 4], [0, 4]], 0.0)
     fill(A("KK"), -32.0)
     fill(A("MC"), 1.0)
     ts(C("PI", 1), C("PI", 0), 15, ALU.bitwise_and)
@@ -318,9 +326,9 @@ def rank_program(g, core, T, topo):
     fill(A("GQ"), 0.0)
     cp(C("PC", 40, 5), C("PI", 1, 5))
     p8, rr, qq, a4, ad = [C("PC", 40 + i) for i in range(5)]
-    ts(C("GQ", 128, 8), C("XI", 0, 8), gcol, ALU.is_equal)
+    ts(C("GQ", 128, 8), C("XI", 0, 8), gcol, ALU.is_equal, 544.0, ALU.mult)
     ts(C("PC", 52), ad, 32.0, ALU.mult, a4, ALU.add)
-    ts(C("SL", 40, 4), C("XT", 24, 4), C("PC", 52), ALU.add, ggc, ALU.add)
+    ts(C("SL", 40, 8), C("XT", 24, 8), C("PC", 52), ALU.add, ggc, ALU.add)
     lin(C("PC", 18), gcol, 16.0, 15.0)
     lin(C("PC", 20, 3), C("XI", 0, 3), 16.0, acol)
     lin(A("CF"), C("XI", 0, 16), 4.0, ad)
@@ -328,58 +336,80 @@ def rank_program(g, core, T, topo):
     cp(A("X1"), ind(A("CL"), C("SL", 0, 24)))
     vtr(A("X2"), A("X1"))
     ts(A("LH"), A("XD"), p8, ALU.is_equal)
-    cp(C("L0", 48 * me, 48), ind(A("X2"), C("SL", 40, 3)))
-    send_all("n0", C("L0", 48 * me, 48), lambda r: C("L0", 48 * r, 48))
+    for b in range(2):
+        cp(A("L0", me, b), ind(A("X2"), C("SL", 40 + 4 * b, 3)))
+    send_all("n0", A("L0", me), lambda r: A("L0", r))
+    where0(C("RR", 80, 64, p=blk[1]), [[1, 4], [-1, 4], [0, 4]], -0.25)
+    where0(C("RR", 16, 64, p=blk[3]), [[1, 4], [0, 4], [-1, 4]], 1.0)
+    where0(C("RR", 0, 80, p=blk[2]), [[0, 5], [1, 4], [-1, 4]], -float(2 ** 23))
+    where0(C("RR", 80, 64, p=blk[1]), [[1, 4], [0, 4], [-1, 4]], -0.25)
+    where0(C("RR", 16, 64, p=blk[3]), [[1, 4], [-1, 4], [0, 4]], 0.0)
     cp(A("VO"), ind(A("X2"), C("SL", 24, 16)))
-    cp(C("NM", 208, 192), C("VO", 64, 192))
+    cp(C("NM", 416, 128), C("VO", 128, 128))
     sfill(C("KK", 769), xs(1), -C2)
-    sfill(A("MB"), A("X1"), 2.0)
-    fill(C("RW", 0, 767), 1.0)
-    fill(C("DD", 896, 2), -1e12)
+    sfill(A("MB", p=(0, 96)), A("X1", p=(0, 96)), -1.0 / 2048)
+    sfill(A("MB", p=(96, 128)), A("X1", p=(96, 128)), 2.0)
+    fill(C("RW", 0, 95), 1.0)
+    fill(C("RW", 96, 32), 0.0)
+    fill(C("XR", 32, 82), 0.0)
+    fill(C("DD", 96, 32), -1e12)
+    ts(C("PC", 33), acol, 8.0, ALU.is_ge, -float(2 ** 23), ALU.mult)
+    ts(C("RW", 96), ggc, -float(2 ** 18), ALU.mult)
+    ts(C("RW", 112), ggc, float(2 ** 19), ALU.mult, -float(2 ** 22), ALU.add)
+    lin(C("PC", 34), acol, -96.0, C("PC", 33))
+    lin(C("RW", 95), C("PC", 34), 1.0, 288.0)
     ts(A("ID"), C("XI", 0, 128), pcol, ALU.is_equal)
-    ts(C("PC", 48), qq, 0.0, ALU.is_equal, 16384.0, ALU.mult)
-    ts(C("PC", 49), qq, 1.0, ALU.is_equal, 16.0, ALU.mult)
-    ts(C("PC", 50), qq, 2.0, ALU.is_equal, -1.0, ALU.mult)
-    ts(C("PC", 51), qq, 2.0, ALU.is_equal, -2.0, ALU.mult)
-    ts(C("BM", 0, 128), A("XD"), gcol, ALU.is_equal, 1024.0, ALU.mult)
-    for x in range(3):
+    ts(C("PC", 48), qq, 0.0, ALU.is_equal, -4.0, ALU.mult)
+    ts(C("PC", 49), qq, 1.0, ALU.is_equal, -2.0 ** -8, ALU.mult)
+    ts(C("PC", 50), qq, 2.0, ALU.is_equal, 2.0 ** -24, ALU.mult)
+    ts(C("PC", 51), qq, 2.0, ALU.is_equal, 2.0 ** -23, ALU.mult)
+    ts(A("BM"), C("XI", 0, 144), C("PC", 18), ALU.is_equal, 1024.0, ALU.mult)
+    for x in range(2):
         sfill(A("MSG", slice(0, 4), slice(3 - me, 7 - me), slice(64 * x + 16 * me + 13, 64 * x + 16 * me + 16)),
               xs(48), 0.0)
-    lin(A("BP"), C("BM", 0, 128), -2.0 / UH)
-    ts(A("UU"), C("XI", 0, 144), C("PC", 18), ALU.is_equal, 896.0, ALU.mult)
-    run(early)
+    defer += [lambda: lin(A("UU"), A("BM"), 0.875), lambda: lin(A("BP"), A("BM"), -2.0 / UH)]
     ts(C("XP", 0, 80), C("XP", 0, 80), rr, ALU.is_equal, C("PC", 48), ALU.mult)
     ts(C("XP", 144, 80), C("XP", 144, 80), rr, ALU.is_equal, C("PC", 49), ALU.mult)
     ts(C("XP", 80, 64), C("XP", 80, 64), rr, ALU.is_equal, C("PC", 50), ALU.mult)
     ts(C("XP", 224, 64), C("XP", 224, 64), rr, ALU.is_equal, C("PC", 50), ALU.mult)
     ts(C("XP", 288, 64), C("XP", 288, 64), rr, ALU.is_equal, C("PC", 51), ALU.mult)
-    ts(C("RR", 80, 64, p=blk[0]), C("RR", 80, 64, p=blk[0]), 1.0, ALU.min, -1.0, ALU.max)
+    ts(C("RR", 80, 64, p=blk[0]), C("RR", 80, 64, p=blk[0]), 2.0 ** -12, ALU.min, -2.0 ** -12, ALU.max)
     tt(C("XP", 0, 144), C("XP", 0, 144), C("XP", 144, 144), ALU.add)
     ts(C("XP", 288, 64), C("XP", 288, 64), C("PC", 50), ALU.subtract)
     ts(A("CF"), A("CF"), 48.0, ALU.min)
     lin(C("WC", 0, 80), C("XP", 0, 80), 1.0)
     tt(C("WC", 80, 64), C("XP", 80, 64), C("XP", 288, 64), ALU.add)
     lin(C("PC", 27), C("PC", 4), 0.125, 48.0 * me)
-    ts(C("PC", 54), acol, 4.0, ALU.is_lt)
-    ts(C("PC", 55), ad, 1.0, ALU.is_equal)
-    lin(C("PC", 5), C("PC", 55), 4.0, -3.0)
+    ts(C("PC", 54), acol, 8.0, ALU.is_lt)
     ts(C("SL", 56, 4), C("XI", 0, 4), C("PC", 27), ALU.add)
-    ends = [lambda: lin(C("PC", 28), acol, -15.0, 48.0 * me - 144.0),
-            lambda: lin(C("PC", 30), acol, 16.0, 144.0),
+    ends = [lambda: lin(C("PC", 32), ad, 208.0, a4),
+            lambda: lin(C("PC", 33), acol, -16.0, C("PC", 32)),
+            lambda: lin(C("PC", 28), C("PC", 33), 1.0, 48.0 * me - 288.0),
+            lambda: lin(C("PC", 30), acol, 16.0, 288.0),
             lambda: lin(C("PC", 31), acol, 1.0, ggc),
             lambda: lin(C("PC", 53), C("PC", 54), 3.0, 1.0),
             lambda: lin(C("PC", 29), C("PC", 28), C("PC", 54), C("PC", 30))]
     ends2 = [lambda: ts(C("SL", 84, 12), C("XI", 0, 12), 32.0, ALU.mult, C("PC", 31), ALU.add),
              lambda: ts(C("SL", 60, 24), C("XT", 40, 24), C("PC", 53), ALU.mult, C("PC", 29), ALU.add)]
-    defer += [lambda: sfill(C("NM", 192, 16), xs(16), 0.0),
-              lambda: lin(A("PB"), A("NM"), 1.0 - 2.0 ** -14, CP),
-              lambda: lin(C("VB", 0, 400), A("PB"), 1.0, -CP)]
-    late = [lambda: tt(A("BT"), A("NM"), C("VB", 0, 400), ALU.subtract)]
+    for q in range(3):
+        keep0(C("MB", 128 * q, 128, p=(0, 96)), [[-1, 8], [-24, 4], [0, 4]], -8 * q)
+    keep0(A("MC"), [[-4, 2], [-16, 8], [0, 16]], 0)
+    for on in CFG["start"]:
+        const(on)
+    defer += [lambda: lin(A("PB"), A("NM"), 1.0 - 2.0 ** -14, CP),
+              lambda: lin(C("VB", 0, 544), A("PB"), 1.0, -CP)]
+    late = [lambda: lin(A("PH"), C("VB", 0, 544), 1.0), lambda: lin(C("IB", 0, 128), A("ID"), 1.0),
+            lambda: lin(C("IB", 128, 128), A("ID"), -1.0),
+            lambda: tt(A("BT"), A("NM"), C("VB", 0, 544), ALU.subtract),
+            lambda: tt(A("PL"), C("VB", 0, 544), A("PH"), ALU.subtract)]
 
     def rul(rnd, k):
         if rnd == 0:
             return C("RU", k)
-        return C("FI", 192 + k) if k < 4 else C("FI", 144 + 16 * k + 12)
+        return C("FI", 208 * (k // 4) + 192 + k % 4) if k < 8 else C("FI", 288 + 16 * k + 12)
+
+    def big(bank, n, sign, p, start, stop, at=0):
+        return (C(bank, at, n), A("W32", p=blk[p]), C("CC", 80 * (sign < 0), n, p=blk[p]), start, stop)
 
     def vote_v(rnd, k):
         ts(C("NE", 192 * k, 192), ind(TBr, C("VO", 16 * k, 12)), rul(rnd, k), ALU.not_equal)
@@ -390,20 +420,27 @@ def rank_program(g, core, T, topo):
         for k in ks if part != 0 else []:
             act(C("NE", 192 * k, 192), C("SG", 192 * (k // 4 % 2), 192), AF.Square)
 
-    def vote_mm(bank, at, k, row, start, stop):
-        mm([(C(bank, at, 192), C("GQ", 128 - row, 128), C("NE", 192 * k, 192), start, stop)])
+    VBANK = ("VA", "VC", "CT")
 
-    def vote_send(rnd, x, bank, at):
-        p = (0, 96) if x else None
+    def vote_mm(x, k, row, start, stop):
+        bank = VBANK[x]
+        mm([big(bank, 64, 1, 0, True, False)] * start +
+           [(C(bank, 0, 64), C("GQ", 128 - row, 128), C("NE", 192 * k + 64 * j, 64), False, False) for j in range(3)] +
+           [big(bank, 64, -1, 0, False, True)] * stop)
+
+    def vote_send(rnd, x):
+        p = (0, 96) if x == 2 else None
         off = 16 * x + 4 * rnd
-        act(C("TH", 192 * x, 192, p=p), C(bank, at, 192, p=p), AF.Sign, bias=7.5, scale=-1.0,
-            acc=C("LX", 32 * me + off, p=p))
-        send_all("v%s%d" % ("ab"[x], rnd), C("LX", 32 * me + off), lambda r: C("LX", 32 * r + off))
+        if CFG["vr"][x] == "v":
+            red(C("LX", 48 * me + off, p=p), C(VBANK[x], 0, 64, p=p), ALU.add)
+        else:
+            act(C("JS", 0, 64, p=p), C(VBANK[x], 0, 64, p=p), AF.Identity, acc=C("LX", 48 * me + off, p=p))
+        send_all("v%s%d" % ("abc"[x], rnd), C("LX", 48 * me + off), lambda r: C("LX", 48 * r + off))
 
     def courts(off, mat, bank, at):
         c = sm(32)
         K = [C(bank if q else "VA", at + 4 * q, 4) for q in range(3)]
-        votes = C("LX", off, 4, step=32)
+        votes = C("LX", off, 4, step=48)
         m0, m1, m2 = C("SM", c), C("SM", c + 1), C("SM", c + 2)
         al0, al1, k1, k2p, k2, pre = [C("SM", c + 4 + 4 * i, 4) for i in range(6)]
         return [
@@ -419,17 +456,29 @@ def rank_program(g, core, T, topo):
             lambda: red(m2, k2, ALU.max),
         ], c
 
-    def update(b, nb, rnd):
-        if b == 0:
-            lo, n = 0, 192
-            src = ind(C("FL0", 224 * rnd, 224), C("OF0", 0, 13))
-            put = lambda: lin(C("FI", 0, 208), src, 1.0) if CFG["sf"] else cp(C("FI", 0, 208), src)
-            vo = lambda: cp(C("VO", 0, 48), ind(C("NM", 0, 192), C("SL", 56, 3)))
+    def update(b, rnd):
+        if b < 2:
+            lo, n = 208 * b, 192
+            src = ind(C("FL0", 448 * rnd + 224 * b, 224), C("OF0", 16 * b, 13))
+            put = lambda: lin(C("FI", lo, 208), src, 1.0) if CFG["sf"][b] else cp(C("FI", lo, 208), src)
+            vo = lambda: cp(C("VO", 64 * b, 48), ind(C("NM", lo, 192), C("SL", 56, 3)))
         else:
-            lo, n = 144 + 64 * b, 64 * nb
-            put = lambda: cp(ind(C("FI", lo, n), C("OF2", 4 * b - 4, 4 * nb)),
-                             A("MSG", rnd, 3, slice(64 * b - 64, 64 * b - 64 + n)))
-            vo = lambda: cp(C("VO", 64 * b, n - 16), C("NM", lo, n - 16))
+            lo, n = 288 + 64 * b, 64
+            put = lambda: cp(ind(C("FI", lo, n), C("OF2", 4 * b - 8, 4)),
+                             A("MSG", rnd, 3, slice(64 * b - 128, 64 * b - 64)))
+            vo = lambda: cp(C("VO", 64 * b, 48), C("NM", lo, 48))
+        if CFG["rn"][b]:
+            bank = ("VA", "VC")[b % 2]
+
+            def flip():
+                mm([(C(bank, 0, n), C("IB", 0, 128), C("FI", lo, n), True, False),
+                    (C(bank, 0, n), C("IB", 128, 128), C("BT", lo, n), False, True)])
+                act(C("BT", lo, n), C(bank, 0, n), AF.Abs)
+
+            def name():
+                mm([(C(bank, 0, n), C("IB", 0, 128), C(k, lo, n), k == "PH", k == "BT") for k in ("PH", "PL", "BT")])
+                lin(C("NM", lo, n), C(bank, 0, n), 1.0)
+            return [put, flip, name] + ([vo] if rnd < RO - 1 else [])
         return [put,
                 lambda: tt(C("BT", lo, n), C("FI", lo, n), C("BT", lo, n), ALU.not_equal),
                 lambda: tt(C("NM", lo, n), C("BT", lo, n), C("VB", lo, n), ALU.add),
@@ -439,31 +488,52 @@ def rank_program(g, core, T, topo):
         return C("LN", 192 * rnd + 48 * b + a, n)
 
     def aux(rnd, b, i, n=1):
-        if b == 0:
-            return C("FL0", 224 * rnd + 56 * me + 48 + i, n)
-        c = 64 * b - 64 + 16 * me + 12
+        if b < 2:
+            return C("FL0", 448 * rnd + 224 * b + 56 * me + 48 + i, n)
+        c = 64 * b - 128 + 16 * me + 12
         return A("MSG", rnd, 6 - me + i, slice(c, c + 1))
 
     def stale(rnd, b):
         act(C("ZS", 0, 768), ind(TBr, names(rnd, b)), AF.Identity, bias=191.0, scale=-2.0)
 
-    def halve():
-        scan(C("UN", 0, 403), C("ZS", 0, 403, step=2), C("ZS", 1, 403, step=2), 4 * C1 - 256.0 * 128, ALU.add, ALU.add)
-        t = C("UN", 402)
-        for n in range(1, 6):
-            c = sm(3)
-            k = 96 - (16 >> n)
-            act(A("JS"), C("ZS", 0, 768), AF.Sign, bias=t, scale=-2048.0 if n == 1 else -0.5 if n % 2 else 0.5,
-                acc=C("SM", c))
-            if n < 5:
-                t = C("SM", c + 1)
-                act(C("UN", 386 + 96 * n, k), C("UN", 290 + 96 * n, k), AF.Sign, bias=C("SM", c), scale=-8192.0, acc=t)
-        return t, c
+    def halve(NV):
+        res = []
+        UE, U0 = [ue(NV, i) for i in range(NV)], u0(NV)
 
-    def offset(t, rnd, b, small):
+        def vstep(i):
+            n = 386 + (16 >> i) + (i == NV - 1)
+            scan(C("UN", UE[i] - n, n), C("ZS", 840 * i, n, step=2), C("ZS", 840 * i + 1, n, step=2),
+                 (4 * C1 - 256.0 * 128) * zu[i], ALU.add, ALU.add)
+
+        def shift(i):
+            ts(C("ZS", 840 * i, 768), C("ZS", 840 * i - 840, 768), zu[i] / zu[i - 1], ALU.mult, C("UN", UE[i - 1] - 1),
+               ALU.subtract)
+
+        def ssteps():
+            t = C("UN", UE[-1] - 1)
+            for j, n in enumerate(range(NV, 6)):
+                c = sm(3)
+                k = 96 - (16 >> n)
+                act(A("JS"), C("ZS", 0 if j else 840 * (NV - 1), 768), AF.Sign, bias=t,
+                    scale=-UP / (128 >> NV) if j == 0 else 0.5 if j % 2 else -0.5, acc=C("SM", c))
+                if n < 5:
+                    t = C("SM", c + 1)
+                    act(C("UN", U0 + 96 * j + 96, k), C("UN", U0 + 96 * j, k), AF.Sign, bias=C("SM", c), scale=-8192.0,
+                        acc=t)
+            res.extend([t, c])
+        calls = [lambda: vstep(0)]
+        for i in range(1, NV):
+            calls += [lambda i=i: shift(i), lambda i=i: vstep(i)]
+        last = calls.pop()
+        return calls + [lambda: (last(), ssteps())], res
+
+    def offset(t, rnd, b, at):
         off, a = sb(), C("SM", t[1] + 2)
-        ts(a, C("SM", t[1]), 0.0, ALU.is_ge, t[0], ALU.subtract)
-        run(small, 1)
+        if CFG["nv"][b] % 2:
+            ts(a, C("SM", t[1]), 0.0, ALU.is_ge, t[0], ALU.subtract)
+        else:
+            ts(a, C("SM", t[1]), 0.0, ALU.is_le, t[0], ALU.add)
+        at()
         ts(off, aux(rnd, b, 2), a, ALU.is_lt, a, ALU.subtract)
         return off
 
@@ -472,54 +542,62 @@ def rank_program(g, core, T, topo):
              (CG - 128.0 * 384 + UH / 2) * u, ALU.add, ALU.add)
         return C("SC", 386)
 
-    def hearing(rnd, b, ahead, small, later, big):
+    def gaps(plan, lists):
+        def at(place):
+            for k in plan.get(place, ""):
+                if k in "Yy":
+                    const("v" if k == "Y" else "s")
+                else:
+                    run(lists[k], 1)
+        return at
+
+    def hearing(rnd, b, ahead, lists):
         h = 4 * rnd + b
+        at = gaps(CFG["plan"][b], lists)
         par = h % 2
         zc = lambda a, n, step=1: C("ZZ", a, n, step=step)
         yc = lambda r, a=0, n=768: C("YY", 784 * r + a, n)
-        dd = lambda x: C("DD", 128 + PD * x, PD)
+        dd = C("DD", 0, 96)
         Z = zc(0, 768)
         n8 = C("NM8", 48 * par, 48)
         gv = CFG["gv"][b]
-        nxt = []
-
-        def at(n):
-            if b == 0:
-                big[2](n)
-            if b < 3 and n == CFG["hv"][b]:
-                nxt.append(halve())
-        ts(zc(0, gv), ind(TBr, names(rnd, b, 0, gv // 16)), 64.0, ALU.add)
+        lists["L"], nxt = halve(CFG["nv"][b]) if b < 3 else ([], None)
+        lists["N"] = [lambda: cp(n8, names(rnd, b))]
+        lists["I"] = [lambda: lin(A("I0"), Z, 1.0, -64.0)] if CFG["st"][b] else []
+        own = lambda: ts(zc(0, gv), ind(TBr, names(rnd, b, 0, gv // 16)), 64.0, ALU.add)
+        if b and CFG["af"][b]:
+            off = offset(ahead, rnd, b - 1, own)
+        else:
+            own()
         if gv < 768:
             act(zc(gv, 768 - gv), ind(TBr, names(rnd, b, gv // 16, 48 - gv // 16)), AF.Identity, bias=64.0)
         if 0 < b < 3:
             stale(rnd, b + 1)
-        if b == 0:
-            lin(n8, ind(C("NM", 0, 192), C("O48", 0, 3)), 1.0)
+        if b < 2 and CFG["n8"][b]:
+            lists["N"] = [lambda: lin(n8, ind(C("NM", 208 * b, 192), C("O48", 4 * b, 3)), 1.0)]
         for x in range(2):
-            mm([(dd(x), C("BM", 0, 128), zc(PD * x, PD), True, False)])
+            mm([(dd, C("BM", 15 - a, 128), zc(96 * a, 96), a == 0, False) for a in range(4 * x, 4 * x + 4)])
+        at("g")
         if b:
-            small += later[0]
-            off = offset(ahead, rnd, b - 1, small)
-            cp(n8, names(rnd, b))
+            if not CFG["af"][b]:
+                off = offset(ahead, rnd, b - 1, lambda: at("a"))
+            at("o")
             cuts = [0, gv, 768] if CFG["yp"] == 2 and gv < 768 else [0, 768]
             for a, e in zip(cuts, cuts[1:]):
                 ts(yc(5, a, e - a), zc(a, e - a), off, ALU.add, -95.5, ALU.add)
-            run(small, 1)
+            at("y")
             row, w = 5, count(5, 1.0)
-            run(small, 1)
         else:
             scan(C("SW", 0, 771), zc(0, 771), C("KK", 0, 771), C1 + 16512.0, ALU.add, ALU.add)
             w = C("SW", 770)
-            run(small, 1)
             for n, s in enumerate(STEP):
-                at(n)
+                at("%da" % n)
                 if n < NS:
                     c = sm()
                     a = C("SM", sm())
                     act(A("JS"), Z, AF.Sign, bias=w, scale=-s, acc=C("SM", c))
-                    run(defer, CFG["df"] if n < NS - 1 else 99)
                     ts(a, w, 2.0 / UP if n == 0 else 2.0, ALU.mult, -0.5 - (64 * STEP[NS] if n == NS - 1 else 0), ALU.add)
-                    run(small, CFG["pb"])
+                    at("%db" % n)
                     w = sb()
                     ts(w, C("SM", c), 0.0, ALU.is_le, a, ALU.add)
                 else:
@@ -527,167 +605,136 @@ def rank_program(g, core, T, topo):
                         ts(yc(n), Z, s, ALU.mult, w, ALU.subtract)
                     else:
                         ts(yc(n), yc(n - 1), UH / (32 >> n), ALU.mult, w, ALU.subtract)
-                    run(small, CFG["per"])
+                    at("%db" % n)
                     w = count(n, unit[n])
-                run(small, 1)
             row = 4
-            small += later[0]
-        at(11)
+        at("c")
         for x in range(2):
             ts(C("DM", PD * x, PD), yc(row, PD * x, PD), UH, ALU.mult, w, ALU.max)
-            mm([(dd(x), A("BP" if b else "BQ"), C("DM", PD * x, PD), False, True)])
-        if b == 3:
-            lin(A("I0"), Z, 1.0, -64.0)
-        at(12)
-        run(big[0])
-        at(5)
-        scan(C("DX", 0, 770), C("DD", 128, 770), C("RW", 0, 770), -1e9, ALU.max, ALU.add)
-        mm([(C("CT", 0, 48), A("W32", p=(0, 32)), C("CC", 0, 48, p=(0, 32)), True, False)])
-        at(7)
-        run(small, 1)
+            mm([(dd, C("BP" if b else "BQ", 15 - a, 128), C("DM", 96 * a, 96), False, a == 7)
+                for a in range(4 * x, 4 * x + 4)])
+        at("d")
+        scan(A("DX"), C("DD", 0, 128), A("RW"), -1e9, ALU.max, ALU.add)
+        mm([big("CT", 48, 1, 0, True, False)])
+        at("x")
+        vtr(C("XR", 0, 32), C("DX", 96, 32))
+        at("t")
+        scan(C("XR", 40, 34), C("XR", 0, 34), C("XR", 80, 34), -1e9, ALU.max, ALU.add)
+        at("u")
         ju = C("JU", 2 * par)
-        ts(ju, C("DX", 769), C("DX", 767), ALU.subtract, 383.0, ALU.add)
-        run(small, 1)
+        ts(ju, C("XR", 73), C("XR", 71), ALU.subtract, 383.0, ALU.add)
+        at("j")
         s1 = 16 * par
         ts(C("S1", s1, 16), ind(Z, ju), -1.0, ALU.mult, CN, ALU.add)
-        at(8)
-        run(small, 1)
+        at("s")
         for e in range(2):
             ts(C("NR", 384 * e, 384), zc(e, 384, 2), C("S1", s1), ALU.add, CN, ALU.not_equal)
             mm([(C("CT", 0, 48), C("UU", 15 - 2 * i - e, 128), C("NR", 384 * e + i, 48, step=8), False, False)
                 for i in range(8)] +
-               ([(C("CT", 0, 48), A("W32", p=(0, 32)), C("CC", 48, 48, p=(0, 32)), False, False),
-                 (C("CT", 0, 48), A("ID"), n8, False, True)] if e else []))
-        mc = 64 * b - 64 + 16 * me
-        if b == 0:
+               ([big("CT", 48, -1, 0, False, False), (C("CT", 0, 48), A("ID"), n8, False, True)] if e else []))
+        mc = 64 * b - 128 + 16 * me
+        if b < 2:
             tt(aux(rnd, b, 0, 4), C("CR", 3, 4), C("S1", s1, 4), ALU.subtract)
-            fl = C("FL0", 224 * rnd + 56 * me, 48)
+            fl = C("FL0", 448 * rnd + 224 * b + 56 * me, 48)
         else:
             tt(A("MSG", rnd, slice(3 - me, 10 - me), mc + 12), C("CR", 0, 7), C("S1", s1, 7), ALU.subtract)
             fl = A("MSG", rnd, slice(3 - me, 7 - me), slice(mc, mc + 12))
         rho = aux(rnd, b, 3)
-        at(9)
-        run(small, 1)
-        if b == 3:
+        at("n")
+        assert not lists["I"]
+        if CFG["st"][b]:
             act(A("I1"), Z, AF.Sign, bias=rho, scale=-1.0)
         else:
             ts(A("I0"), Z, rho, ALU.subtract, -1.0, ALU.min)
             ts(A("I1"), Z, 64.0, ALU.subtract, aux(rnd, b, 1), ALU.max)
-        at(10)
-        run(big[1])
-        small += later[1]
+        at("i")
         cp(A("OS"), C("CT", 0, 48))
         ts(fl, C("CT", 0, 48), float(TR), ALU.is_ge)
-        run(small)
+        at("f")
         tag = "f%s%d" % ("abcd"[b], rnd)
-        if b == 0:
-            slot = lambda r: C("FL0", 224 * rnd + 56 * r, 50)
+        if b < 2:
+            slot = lambda r: C("FL0", 448 * rnd + 224 * b + 56 * r, 50)
             send_all(tag, slot(me), slot)
         else:
             send_each(tag, lambda r: A("MSG", rnd, 3 - me + r, slice(mc, mc + 16)),
-                      lambda r: A("MSG", rnd, 3, slice(64 * b - 64 + 16 * r, 64 * b - 48 + 16 * r)))
+                      lambda r: A("MSG", rnd, 3, slice(64 * b - 128 + 16 * r, 64 * b - 112 + 16 * r)))
         tt(ind(TBw, A("OS")), A("I0"), A("I1"), ALU.add)
-        return nxt[0] if b < 3 else None
+        assert not lists["L"] and not lists["N"]
+        return nxt
 
+    left = [0, 0, 0]
     for rnd in range(RO):
-        vote_s(rnd, [2])
-        vote_v(rnd, 0)
-        vote_v(rnd, 1)
-        for i, q in enumerate((0, 1, 2)):
-            vote_mm("VA", 0, q, 32 * me + 8 * q, i == 0, i == 2)
-        sv = CFG["sv"]
-        vote_s(rnd, sv[:1], 0)
-        vote_send(rnd, 0, "VA", 0)
-        if rnd == 0:
-            for q in range(3):
-                keep0(C("MB", 128 * q, 128, p=(0, 96)), [[-1, 8], [-24, 4], [0, 4]], -8 * q)
-
-        def weigh(r, on, rnd=rnd):
+        def weigh(r, b, on):
             p = (32 * r, 32 * r + 24)
+            x = C("LX", 48 * r + 16 * b + 4 * rnd, p=p)
             if on == "v":
-                ts(A("RR", p=p), A("WC", p=p), C("LX", 32 * r + 4 * rnd, p=p), ALU.mult)
+                ts(A("RR", p=p), A("WC", p=p), x, ALU.mult)
             else:
-                lin(A("RR", p=p), A("WC", p=p), C("LX", 32 * r + 4 * rnd, p=p))
-        up3 = update(3, 1, rnd - 1) if rnd else []
-        later = [4, 5, 6, 8, 9, 10, 12, 13, 14]
-        vote_s(rnd, sv[:1], 1)
-        weigh(me, "s")
-        for k in later:
-            if k == 12:
-                run(up3)
-            if k in sv[1:]:
-                vote_s(rnd, [k])
-            elif k not in sv:
-                vote_v(rnd, k)
-            else:
-                continue
-            if k < 12 and k not in sv:
-                run(up3, CFG["u3"] if k > 4 else 0)
-        if rnd == 0:
-            cp(C("NM", 0, 192), A("L0"))
-        for i, k in enumerate(later):
-            vote_mm("CT", 128, k, 8 * i, i == 0, i == 8)
-        if CFG["wv"] == "v":
-            vote_send(rnd, 1, "CT", 128)
-        for r in peers:
-            weigh(r, CFG["wv"])
-        mm([(C("PK", 0, 144), A("LH"), A("RR"), True, True)])
-        if CFG["wv"] != "v":
-            vote_send(rnd, 1, "CT", 128)
-        if rnd == 0:
-            keep0(A("MC"), [[-4, 3], [-16, 8], [0, 16]], 0)
-            run(defer, 4)
-        ts(C("PA", 16, 64), C("PK", 80, 64), 0.0, ALU.is_gt)
-        tt(A("PS"), C("PK", 0, 80), A("PA"), ALU.add)
-        scan(A("PM"), A("PS"), A("RS"), -1e9, ALU.max, ALU.add)
-        ts(C("O48", 0, 3), C("C48", 0, 3), C("PM", 30 + 16 * me), ALU.add, C("PM", 14), ALU.subtract)
-        cp(names(rnd, 0), ind(C("NM", 0, 192), C("O48", 0, 3)))
-        c = sm(8)
-        lists0 = [lambda c=c: ts(C("SM", c, 4), C("PM", 30, 4, step=16), C("PM", 14), ALU.subtract, a4, ALU.is_equal),
-                  lambda c=c: tt(C("SM", c + 4, 4), C("SM", c, 4), C("XT", 32, 4), ALU.mult),
-                  lambda c=c: red(C("SM", c), C("SM", c + 4, 4), ALU.max),
-                  lambda c=c: ts(A("OF0"), A("CF"), C("SM", c), ALU.add)]
-        cc, e = courts(16 + 4 * rnd, "MB", "PK", 160)
+                lin(A("RR", p=p), A("WC", p=p), x)
 
-        def bcast(e=e):
+        def scored(b):
+            pm = lambda a, n=1, step=1: C("PM", 80 * b + a, n, step=step)
+            c = sm(8)
+
+            def score():
+                for r, on in zip(peers, CFG["wg"][b]):
+                    weigh(r, b, on)
+                mm([big("PK", 80, 1, 1, True, False), (C("PK", 16, 64), A("LH"), C("RR", 80, 64), False, False),
+                    big("PK", 80, -1, 1, False, False), (C("PK", 0, 80), A("LH"), C("RR", 0, 80), False, True)])
+            return ([lambda: weigh(me, b, "s"), score,
+                     lambda: scan(pm(0, 80), C("PK", 0, 80), A("RS"), -1e9, ALU.max, ALU.add),
+                     lambda: ts(C("O48", 4 * b, 3), C("C48", 0, 3), pm(30 + 16 * me), ALU.add, pm(14), ALU.subtract),
+                     lambda: cp(names(rnd, b), ind(C("NM", 208 * b, 192), C("O48", 4 * b, 3)))],
+                    [lambda: ts(C("SM", c, 4), pm(30, 4, 16), pm(14), ALU.subtract, a4, ALU.is_equal),
+                     lambda: tt(C("SM", c + 4, 4), C("SM", c, 4), C("XT", 32, 4), ALU.mult),
+                     lambda: red(C("SM", c), C("SM", c + 4, 4), ALU.max),
+                     lambda: ts(C("OF0", 16 * b, 16), A("CF"), C("SM", c), ALU.add)])
+
+        cc, e = courts(32 + 4 * rnd, "MB", "VC", 160)
+
+        def bcast():
             tt(C("QB", 0, 4), C("SM", e + 28, 4), C("SM", e + 24, 4), ALU.add)
-            mm([(C("PK", 192 + 4 * x, 4), C("MC", 128 * x, 128), C("QB", 0, 4), True, True) for x in range(3)])
+            mm([(C("VC", 192 + 4 * x, 4), C("MC", 128 * x, 128), C("QB", 0, 4), True, True) for x in range(2)])
 
-        def hand(b, rnd=rnd):
-            at = 192 * rnd + 64 * b - 64
-            win = C("NM", 208, 128) if b < 3 else C("NM", 336, 64)
-            cp(C("SN", at, 64), ind(win, C("OF2", 4 * b - 4, 4)))
+        def hand(b):
+            at = 128 * rnd + 64 * b - 128
+            cp(C("SN", at, 64), ind(C("NM", 288 + 64 * b, 64), C("OF2", 4 * b - 8, 4)))
             send_each("n%s%d" % ("abcd"[b], rnd), lambda r: C("SN", at + 16 * r, 12), lambda r: names(rnd, b, 12 * r, 12))
             dma(names(rnd, b, 12 * me, 12), C("SN", at + 16 * me, 12))
 
-        cc += [lambda e=e: ts(C("SM", e + 28, 4), C("SM", e + 20, 4), C("SM", e + 2), ALU.not_equal, C("PC", 5), ALU.add),
-               bcast, None, lambda: ts(A("OF2"), C("PK", 192, 12), 16.0, ALU.mult, acol, ALU.add), lambda: hand(1)]
-        rest = [lambda: hand(2), lambda: hand(3)]
-        small = []
-
-        def hook0(n, rnd=rnd, small=small, cc=cc, rest=rest):
-            if n == CFG["cb"]:
-                run(cc, 1)
-                small += cc
-            if n == CFG["cf"]:
-                run(small)
-                small += rest
-            if n == CFG["cg"]:
-                stale(rnd, 1)
-
-        off = hearing(rnd, 0, 64.0, small, [[], []], [[lambda: run(small, CFG["win"])], [], hook0])
-        u0, u12 = update(0, 1, rnd), update(1, 2, rnd)
-        plan = {1: ([], [[], []], [lists0[0:2] + late, lists0[2:] + u0[0:1]]),
-                2: ([], [[], []], [u0[1:2], u0[2:3]]),
-                3: ([], [u0[3:], []], [u12[0:1] + ends, u12[1:] + ends2])}
-        late, ends, ends2 = [], [], []
-        for b in range(1, 4):
-            off = hearing(rnd, b, off, plan[b][0], plan[b][1], plan[b][2])
+        cc += [lambda: ts(C("SM", e + 28, 4), C("SM", e + 20, 4), C("SM", e + 2), ALU.not_equal, -3.0, ALU.add),
+               bcast, lambda: ts(A("OF2"), C("VC", 192, 8), 16.0, ALU.mult, acol, ALU.add), lambda: hand(2), lambda: hand(3)]
+        (s0, l0), (s1, l1) = scored(0), scored(1)
+        lists = {"P": s0, "Q": s1 + [lambda: stale(rnd, 1)], "A": l0, "B": l1, "G": cc, "D": defer, "E": ends, "F": ends2,
+                 "T": late, "U": update(0, rnd), "V": update(1, rnd), "W": update(2, rnd),
+                 "X": update(3, rnd - 1) if rnd else [],
+                 "Z": [] if rnd else [lambda b=b: cp(C("NM", 208 * b, 192), A("L0", slice(0, 4), b)) for b in range(2)]}
+        msg = [(0, 1, 2), (4, 5, 6), (8, 9, 10, 12, 13, 14)]
+        for step in CFG["votes"].split():
+            k = int(step[1:], 16) if step[0] in "vsqmr" else None
+            if step[0] == "v":
+                vote_v(rnd, k)
+            elif step[0] in "sq":
+                vote_s(rnd, [k], "sq".index(step[0]))
+            elif step[0] == "m":
+                x = min(k // 4, 2)
+                i = msg[x].index(k)
+                left[x] = left[x] % len(msg[x]) + 1
+                vote_mm(x, k, 8 * i + (32 * me if x < 2 else 0), left[x] == 1, left[x] == len(msg[x]))
+            elif step[0] == "r":
+                vote_send(rnd, k)
+            else:
+                gaps({0: step}, lists)(0)
+        ahead = None
+        for b in range(4):
+            ahead = hearing(rnd, b, ahead, lists)
+        assert not any(lists.values()) and not early
 
     outs = [dma(T.yf[:], TBr)]
-    run(update(3, 1, RO - 1))
+    run(update(3, RO - 1))
     cp(C("YR", 0, 4), C("FI", 192, 4))
-    cp(C("YR", 4, 12), C("FI", 220, 12, step=16))
+    cp(C("YR", 4, 4), C("FI", 400, 4))
+    cp(C("YR", 8, 8), C("FI", 428, 8, step=16))
     outs.append(dma(T.yr[:], A("YR")))
     cp(A("X1"), ind(A("NM"), C("SL", 60, 24)))
     vtr(A("X2"), A("X1"))

from concourse.bass import DstId, RemoteDMATransfer
from concourse.mybir import AluOpType as ALU, AxisListType, ActivationFunctionType as AF

W, RO = 7168, 4
TR = 8192
CN = float(2 ** 24 + 4)
CK = float(3 * 2 ** 32)
CP = float(3 * 2 ** 23)
C1 = float(3 * 2 ** 28)
C2 = float(3 * 2 ** 39)
UP = float(2 ** 17)
CG = float(3 * 2 ** 29)
UH = float(2 ** 16)
CH = float(3 * 2 ** 38)
C3 = float(3 * 2 ** 35)
BF, F, U, I = "bfloat16", "float32", "uint16", "int32"
CFG = {"gv": [384, 352, 480, 320], "ns": 0, "nv": [1, 1, 1], "sf": [1, 1], "yp": 2, "vr": "ssv", "wg": ["vvv", "vss"], "n8": [0, 0], "af": [0, 1, 0, 0], "st": [0, 0, 0, 1], "rn": [1, 1, 0, 0], "start": "vvvvvvvvvvvvvvvvvvvvvvssssss", "votes": "v0 v1 s2 q2 m0 v5 m1 Y X s6 Y Y m2 v4 m4 r0 q6 P sa X v9 Z m5 Y Y m6 X v8 X r1 qa Y Z sc qc m8 Y Y ma ve Y m9 me P Q vd mc D P md r2 P Q P", "plan": [{"g": "DQNDDDDTGT", "0a": "Q", "0b": "QQ", "1a": "TG", "1b": "G", "2a": "G", "2b": "GL", "4a": "G", "4b": "G", "c": "G", "d": "GGG", "j": "G", "t": "G", "n": "G", "3a": "G"}, {"d": "LT", "x": "TA", "j": "B", "s": "B", "n": "A", "u": "B", "c": "A", "t": "N", "o": "B"}, {"c": "L", "y": "N", "t": "E", "a": "A"}, {"g": "U", "c": "U", "d": "EEWVE", "x": "EUEW", "n": "VUWF", "f": "WF", "u": "V", "a": "V", "y": "E", "o": "NI"}]}


def _sb(n, d):
    return ("sbuf", [128] + (n if isinstance(n, list) else [n]), d)


SCRATCH = {
    "TB": _sb(2 * TR + W, BF), "ZZ": _sb(784, BF), "ZS": _sb(2520, BF), "JS": _sb(768, BF), "KK": _sb(784, BF),
    "YY": _sb(6 * 784, BF), "SC": _sb(392, BF), "SW": _sb(784, BF), "DM": _sb(768, BF), "NR": _sb(768, BF),
    "RW": _sb(128, F), "XR": _sb(120, F), "PH": _sb(544, BF), "PL": _sb(544, BF), "IB": _sb(256, BF), "ID": _sb(128, F), "CC": _sb(160, BF), "BQ": _sb(144, BF),
    "I0": _sb(768, BF), "I1": _sb(768, BF), "SM": _sb(512, F), "SB": _sb(256, BF),
    "NE": _sb(3072, BF), "SG": _sb(384, BF), "S1": _sb(32, F), "JU": _sb(4, U),
    "CL": _sb(192, I), "RU": _sb(16, BF), "YR": _sb(16, BF), "X1": _sb(384, F), "X2": _sb(384, F), "YC": _sb(192, F),
    "NM": _sb(544, F), "PB": _sb(544, F), "BT": _sb(544, BF), "FI": _sb(544, BF), "VO": _sb(256, U),
    "L0": _sb([4, 2, 48], U), "LX": _sb(192, F), "SN": _sb(512, U), "LN": _sb(768, U), "DX": _sb(128, F),
    "MSG": _sb([4, 10, 128], BF), "FL0": _sb(1792, BF),
    "NM8": _sb(96, F), "OS": _sb(48, U), "O48": _sb(8, U),
    "OF0": _sb(32, U), "OF2": _sb(8, U), "QB": _sb(8, BF),
    "PI": _sb(8, I), "PC": _sb(64, F), "XI": _sb(160, F), "XD": _sb(128, F), "XT": _sb(128, F),
    "UU": _sb(144, BF), "BP": _sb(144, BF), "BM": _sb(144, BF),
    "MB": _sb(384, F), "MC": _sb(256, BF), "W32": _sb(128, BF), "GQ": _sb(256, BF),
    "LH": _sb(128, BF), "WC": _sb(144, BF), "RR": _sb(144, BF), "XP": _sb(432, F),
    "PM": _sb(160, F), "RS": _sb(80, F), "CF": _sb(16, F), "C6": _sb(8, F),
    "CR": _sb(8, F), "UN": _sb(2720, BF), "C48": _sb(4, F), "SL": _sb(128, U),
    "DD": ("psum", [128, 512], F), "CT": ("psum", [128, 512], F),
    "VB": ("psum", [128, 1024], F), "VA": ("psum", [128, 512], F), "VC": ("psum", [128, 512], F),
    "PK": ("psum", [128, 512], F),
}
POOL = {"v": 42, "s": 30, "t": 22, "y": 8, "g": 10}
ARR = ["n0"] + ["%s%d" % (k, r) for r in range(RO) for k in ("va", "vb", "vc", "nc", "nd", "fa", "fb", "fc", "fd")]
SEMAPHORES = ["%s%d" % (q, i) for q in POOL for i in range(POOL[q])] + ["r" + a for a in ARR] + ["sent"]


def rank_program(g, core, T, topo):
    me = T.rank_of(core)
    if me is None:
        return
    N = len(T.cores)
    peers = [r for r in range(N) if r != me]
    Q = {"v": g.vector, "s": g.scalar, "t": g.tensor, "y": g.sync, "g": g}
    ops = []
    seen = {}

    def A(name, *ix, p=None):
        shape = SCRATCH[name][1][1:]
        ix = list(ix) + [slice(None)] * (len(shape) - len(ix))
        rows = [0]
        for i, n in zip(ix[:-1], shape[:-1]):
            rows = [r * n + j for r in rows for j in (range(n)[i] if isinstance(i, slice) else [i])]
        rg = range(shape[-1])[ix[-1]] if isinstance(ix[-1], slice) else range(ix[-1], ix[-1] + 1)
        row = ((1 << len(rg)) - 1) << rg[0] if rg.step == 1 else sum(1 << j for j in rg)
        m = 0
        for r in rows:
            m |= row << (r * shape[-1])
        if SCRATCH[name][0] == "psum":
            m = (2 << rg[-1] // 512) - (1 << rg[0] // 512)
        ps = slice(None) if p is None else slice(p[0], p[1])
        if name == "RR":
            m = 15 if p is None else (2 << (p[1] - 1) // 32) - (1 << p[0] // 32)
        return (T[name][tuple([ps] + ix)], [(name, m)])

    def C(name, a, n=1, p=None, step=1):
        return A(name, slice(a, a + n * step - step + 1, step) if step > 1 else slice(a, a + n), p=p)

    def ind(win, off):
        return (win[0].indirect(off[0]), win[1] + off[1], off[1])

    def ap(x):
        return x[0] if isinstance(x, tuple) else x

    def rec(q, calls, outs, ins, inc=1, fixed=None):
        n = len(ops)
        acc = []
        for o in outs:
            if len(o) == 3:
                acc += [(r, False) for r in o[2]] + [(o[1][0], True)]
            else:
                acc += [(r, True) for r in o[1]]
        for x in ins:
            if isinstance(x, tuple):
                acc += [(r, False) for r in x[1]]
        deps = set()
        for (name, m), wr in acc:
            psum = SCRATCH[name][0] == "psum"
            for e in seen.setdefault(name, []):
                if e[0] & m and e[1] != n:
                    if psum and q == "t" and e[3] == "t":
                        continue
                    if wr or e[2] or (psum and e[3] != q):
                        deps.add(e[1])
        for (name, m), wr in acc:
            psum = SCRATCH[name][0] == "psum"
            if psum:
                seen[name] = [e for e in seen[name] if e[3] == q or not e[0] & m]
            elif wr:
                seen[name] = [e for e in seen[name] if e[0] & ~m]
            seen[name].append([m, n, wr, q])
        ops.append([q, calls, deps, inc, fixed])
        return n

    def ts(o, x, s1, op0, s2=None, op1=None):
        if op1 is None:
            rec("v", [lambda: g.vector.tensor_scalar(o[0], x[0], ap(s1), None, op0)], [o], [x, s1])
        else:
            rec("v", [lambda: g.vector.tensor_scalar(o[0], x[0], ap(s1), ap(s2), op0, op1)], [o], [x, s1, s2])

    def tt(o, x, y, op):
        rec("v", [lambda: g.vector.tensor_tensor(o[0], x[0], y[0], op)], [o], [x, y])

    def cp(o, x):
        rec("v", [lambda: g.vector.tensor_copy(o[0], x[0])], [o], [x])

    def red(o, x, op):
        rec("v", [lambda: g.vector.tensor_reduce(o[0], x[0], AxisListType.X, op)], [o], [x])

    def scan(o, x, y, init, op0, op1):
        rec("v", [lambda: g.vector.tensor_tensor_scan(o[0], x[0], y[0], ap(init), op0, op1)], [o], [x, y, init])

    def fill(o, c):
        rec("v", [lambda: g.vector.memset(o[0], c)], [o], [])

    def vtr(o, x):
        rec("v", [lambda: g.vector.transpose(o[0], x[0])], [o], [x])

    def act(o, x, f, bias=0.0, scale=1.0, acc=None):
        if acc is None:
            rec("s", [lambda: g.scalar.activation(o[0], x[0], f, bias=ap(bias), scale=ap(scale))], [o],
                [x, bias, scale])
        else:
            rec("s", [lambda: g.scalar.activation(o[0], x[0], f, bias=ap(bias), scale=scale, accum_out=acc[0])],
                [o, acc], [x, bias])

    def lin(o, x, scale, bias=0.0):
        act(o, x, AF.Identity, bias=bias, scale=scale)

    def sfill(o, x, c):
        act(o, x, AF.Identity, bias=c, scale=0.0)

    def mm(items):
        def one(o, l, r, a, b):
            return lambda: g.tensor.matmul(o[0], l[0], r[0], a, b)
        rec("t", [one(*it) for it in items], [it[0] for it in items], [x for it in items for x in it[1:3]])

    pool = [None, False]

    def gp(call, o, ins):
        n = rec("g", [call], [o], ins)
        part = o[1][0][0] == "RR"
        if pool[0] is not None and (part or pool[1]):
            ops[n][2].add(pool[0])
        pool[0], pool[1] = n, part

    def iota(o, pattern, base=0, ch=0, flag=True):
        if flag:
            gp(lambda: g.iota(o[0], pattern, base, ch, allow_small_or_imprecise_dtypes=True), o, [])
        else:
            gp(lambda: g.iota(o[0], pattern, base, ch), o, [])

    def where0(o, pattern, c):
        gp(lambda: g.affine_select(o[0], o[0], pattern, ALU.not_equal, c, 0, 0), o, [o])

    def keep0(o, pattern, base):
        gp(lambda: g.affine_select(o[0], o[0], pattern, ALU.is_equal, 0.0, base, 1), o, [o])

    def dma(o, x):
        outs = [o] if isinstance(o, tuple) else []
        return rec("y", [lambda: g.sync.dma_start(ap(o), ap(x))], outs, [x], inc=16)

    def dst_id(r):
        rid, pid = topo.addr(T.cores[r])[0:2]
        return DstId(rid=rid, pnc=pid)

    def engines(a):
        es = None
        for r in range(N):
            if r != a:
                e = topo.engines(T.cores[a], T.cores[r])
                es = e if es is None else [x for x in es if x in e]
        return es

    def shares(a):
        es = engines(a)
        k = len(es) // 4
        ps = [r for r in range(N) if r != a]
        return {ps[0]: es[0:k], ps[1]: es[k:2 * k], ps[2]: es[2 * k:4 * k]}

    sent = [0]

    def send_all(tag, src, slot):
        es = engines(me)
        m = sum(1 << e for e in es)
        sem = T.sem["r" + tag]
        part = RemoteDMATransfer(dst_ids=[dst_id(r) for r in peers], dma_engine_mask=m, remote_sem=sem, srcs=[src[0]],
                                 dsts=[slot(me)[0] for r in peers])
        rec("g", [lambda: g.remote_dma_fused([part], local_sem=T.sem.sent)], [], [src], inc=0)
        sent[0] += len(es)
        rec("r", [], [slot(r) for r in peers], [], fixed=("r" + tag, sum(len(engines(r)) for r in peers)))

    def send_each(tag, src, slot):
        sh = shares(me)
        sem = T.sem["r" + tag]
        parts = [RemoteDMATransfer(dst_ids=[dst_id(r)], dma_engine_mask=sum(1 << e for e in sh[r]), remote_sem=sem,
                                   src=src(r)[0], dst=slot(me)[0]) for r in peers]
        rec("g", [lambda: g.remote_dma_fused(parts, local_sem=T.sem.sent)], [], [src(r) for r in peers], inc=0)
        sent[0] += sum(len(sh[r]) for r in peers)
        rec("r", [], [slot(r) for r in peers], [], fixed=("r" + tag, sum(len(shares(r)[me]) for r in peers)))

    nsm = [0, 0]

    def sm(n=1):
        if nsm[0] + n > 512:
            nsm[0] = 0
        nsm[0] += n
        return nsm[0] - n

    def sb():
        nsm[1] = (nsm[1] + 2) % 256
        return C("SB", nsm[1])

    def run(lst, n=None):
        for _ in range(len(lst) if n is None else min(n, len(lst))):
            f = lst.pop(0)
            if f:
                f()

    TBr, TBw = C("TB", 0, W), A("TB")

    dma(A("CL"), T.cl[:])
    dma(A("RU"), T.ru[:])
    dma(TBr, T.fa[:])
    iota(C("PI", 0), [[1, 1]], 0, 1, False)
    iota(C("XT", 0, 24), [[16, 12], [0, 2]])
    iota(A("XI"), [[1, 160]])
    iota(A("XD"), [[1, 8], [0, 16]])
    iota(C("XT", 24, 8), [[4, 2], [128, 4]])
    iota(C("XT", 32, 4), [[56, 4]])
    iota(C("XT", 40, 24), [[1, 12], [0, 2]])
    blk = [(32 * r, 32 * r + 32) for r in range(N)]
    fill(A("RR"), 0.0)
    fill(C("RR", 16, 64, p=blk[3]), 2.0)
    fill(C("RR", 80, 64, p=blk[3]), 0.5)
    iota(C("XP", 0, 144), [[0, 9], [1, 4], [0, 4]])
    iota(C("XP", 144, 144), [[0, 36], [1, 4]])
    iota(C("XP", 288, 64), [[1, 4], [0, 16]])
    iota(C("RR", 80, 64, p=blk[0]), [[2, 4], [1, 4], [1, 4]], -6)
    iota(C("RR", 0, 80, p=blk[0]), [[0, 5], [-8192, 4], [0, 4]], 24576)
    iota(C("RR", 0, 80, p=blk[1]), [[0, 20], [-8, 4]], 24)
    xs = lambda n, p=None: C("XI", 0, n, p=p)
    PD = 384
    NS = CFG["ns"]
    STEP = [UP / 32, 1.0 / 16, 0.125, 0.25, 0.5]
    unit = {NS: STEP[NS]}
    for n in range(NS, 4):
        unit[n + 1] = unit[n] * UH / (16 >> n)
    yt = lambda n, i=0, k=6: C("YY", 784 * n + 768 + i, k)
    defer = []
    zu = [1.0, UP / 64, UP / 64 * UP / 32]
    ue = lambda nv, i: 900 * nv - 512 + (32 >> i)
    u0 = lambda nv: ue(nv, nv) - 1
    early = []
    early += [(yt(5, i, 1), 1, c) for i, c in enumerate((-CG, 64.0, CH, -CH, 63.5 * UH, 0.0))]
    early += [(C("ZS", 768, 40), 40, 0.0), (C("NM", 192, 16), 16, 0.0), (C("NM", 400, 16), 16, 0.0)]
    early += [(yt(n), yt(5), unit[n]) for n in range(NS, 5)]
    early += [(C("ZS", 768 + i), 1, c) for i, c in ((0, -4 * C1), (2, C2), (3, -C2), (4, -UP / 2))]
    early += [(yt(n, 4, 1), 1, -UH / 2 * unit[n]) for n in range(NS, 4)]
    for nv in sorted(set(CFG["nv"]), key=CFG["nv"].index):
        early += [(C("UN", u0(nv) + 96 * j, 96), 96, (1.0 if j % 2 else -1.0) / 16384) for j in range(5 - nv)]
        early += [(C("ZS", 840 * i + 768, 32), C("ZS", 768, 32), zu[i]) for i in range(1, nv)]
        early += [(C("UN", ue(nv, 0), 63), 63, 1.0)]
        early += [(C("ZS", 840 * nv - 68 + (64 >> nv)), 1, 128 * UP / (128 >> nv) * zu[nv - 1])]
    early += [(C("XR", 32, 2), 2, -1e12), (C("XR", 112), 1, CK), (C("XR", 113), 1, -CK)]

    def const(on):
        if early:
            o, x, c = early.pop(0)
            if isinstance(x, int):
                fill(o, c) if on == "v" else sfill(o, xs(x), c)
            else:
                ts(o, x, c, ALU.mult) if on == "v" else lin(o, x, c)
    for i, c in enumerate((-C1, C2, (79.5 if NS else 15.5) / 32 * UP)):
        sfill(C("ZZ", 768 + i), xs(1), c)
    defer.append(lambda: lin(A("BQ"), A("BM"), -2.0 / UH / unit[4]))
    for i, c in enumerate((C3, -C3)):
        sfill(C("CC", 80 * i, 80), xs(80), c)
    defer.append(lambda: lin(C("CR", 0, 6), C("C6", 0, 6), 1.0, CN - 64.0))
    sfill(C("LX", 48 * me + 32, 16, p=(96, 128)), xs(16, (96, 128)), (768.0 + N - me) / 64)
    sfill(A("W32", p=blk[0]), xs(128, blk[0]), 1.0 / 32)
    sfill(A("W32", p=blk[1]), xs(128, blk[1]), 1.0 / 32 / TR)
    sfill(A("C6"), xs(8), 0.0)
    sfill(A("RS"), xs(80), 0.0)
    sfill(C("RS", 15, 5, step=16), xs(5), -float(2 ** 25))
    for o, c in ((C("C6", 4), 1.0), (C("C6", 5), -95.0), (C("CR", 6), CN)):
        sfill(o, xs(1), c)
    fill(A("KK"), -32.0)
    fill(A("MC"), 1.0)
    ts(C("PI", 1), C("PI", 0), 15, ALU.bitwise_and)
    ts(C("PI", 2), C("PI", 0), 16, ALU.bitwise_and)
    ts(C("PI", 3), C("PI", 0), 4, ALU.arith_shift_right)
    cp(C("PC", 0, 4), C("PI", 0, 4))
    pcol, acol, ggc, gcol = [C("PC", i) for i in range(4)]
    ts(C("SL", 0, 24), C("XT", 0, 24), acol, ALU.add)
    ts(C("PC", 4), acol, 11.0, ALU.min, 32.0, ALU.mult)
    ts(C("PI", 1), C("PI", 0), 7, ALU.bitwise_and)
    ts(C("SL", 24, 16), C("XI", 0, 16), C("PC", 4), ALU.add, ggc, ALU.add)
    ts(C("PI", 2), C("PI", 0), 5, ALU.arith_shift_right)
    ts(C("PI", 3), C("PI", 0), 3, ALU.arith_shift_right, 3, ALU.bitwise_and)
    ts(C("PI", 4), C("PI", 0), 3, ALU.bitwise_and)
    ts(C("PI", 5), C("PI", 0), 2, ALU.arith_shift_right, 3, ALU.bitwise_and)
    fill(A("GQ"), 0.0)
    cp(C("PC", 40, 5), C("PI", 1, 5))
    p8, rr, qq, a4, ad = [C("PC", 40 + i) for i in range(5)]
    ts(C("GQ", 128, 8), C("XI", 0, 8), gcol, ALU.is_equal, 544.0, ALU.mult)
    ts(C("PC", 52), ad, 32.0, ALU.mult, a4, ALU.add)
    ts(C("SL", 40, 8), C("XT", 24, 8), C("PC", 52), ALU.add, ggc, ALU.add)
    lin(C("PC", 18), gcol, 16.0, 15.0)
    lin(C("PC", 20, 3), C("XI", 0, 3), 16.0, acol)
    lin(A("CF"), C("XI", 0, 16), 4.0, ad)
    lin(C("C48", 0, 3), C("PC", 20, 3), 4.0)
    cp(A("X1"), ind(A("CL"), C("SL", 0, 24)))
    vtr(A("X2"), A("X1"))
    ts(A("LH"), A("XD"), p8, ALU.is_equal)
    for b in range(2):
        cp(A("L0", me, b), ind(A("X2"), C("SL", 40 + 4 * b, 3)))
    send_all("n0", A("L0", me), lambda r: A("L0", r))
    where0(C("RR", 80, 64, p=blk[1]), [[1, 4], [-1, 4], [0, 4]], -0.25)
    where0(C("RR", 16, 64, p=blk[3]), [[1, 4], [0, 4], [-1, 4]], 1.0)
    where0(C("RR", 0, 80, p=blk[2]), [[0, 5], [1, 4], [-1, 4]], -float(2 ** 23))
    where0(C("RR", 80, 64, p=blk[1]), [[1, 4], [0, 4], [-1, 4]], -0.25)
    where0(C("RR", 16, 64, p=blk[3]), [[1, 4], [-1, 4], [0, 4]], 0.0)
    cp(A("VO"), ind(A("X2"), C("SL", 24, 16)))
    cp(C("NM", 416, 128), C("VO", 128, 128))
    sfill(C("KK", 769), xs(1), -C2)
    sfill(A("MB", p=(0, 96)), A("X1", p=(0, 96)), -1.0 / 2048)
    sfill(A("MB", p=(96, 128)), A("X1", p=(96, 128)), 2.0)
    fill(C("RW", 0, 95), 1.0)
    fill(C("RW", 96, 32), 0.0)
    fill(C("XR", 32, 82), 0.0)
    fill(C("DD", 96, 32), -1e12)
    ts(C("PC", 33), acol, 8.0, ALU.is_ge, -float(2 ** 23), ALU.mult)
    ts(C("RW", 96), ggc, -float(2 ** 18), ALU.mult)
    ts(C("RW", 112), ggc, float(2 ** 19), ALU.mult, -float(2 ** 22), ALU.add)
    lin(C("PC", 34), acol, -96.0, C("PC", 33))
    lin(C("RW", 95), C("PC", 34), 1.0, 288.0)
    ts(A("ID"), C("XI", 0, 128), pcol, ALU.is_equal)
    ts(C("PC", 48), qq, 0.0, ALU.is_equal, -4.0, ALU.mult)
    ts(C("PC", 49), qq, 1.0, ALU.is_equal, -2.0 ** -8, ALU.mult)
    ts(C("PC", 50), qq, 2.0, ALU.is_equal, 2.0 ** -24, ALU.mult)
    ts(C("PC", 51), qq, 2.0, ALU.is_equal, 2.0 ** -23, ALU.mult)
    ts(A("BM"), C("XI", 0, 144), C("PC", 18), ALU.is_equal, 1024.0, ALU.mult)
    for x in range(2):
        sfill(A("MSG", slice(0, 4), slice(3 - me, 7 - me), slice(64 * x + 16 * me + 13, 64 * x + 16 * me + 16)),
              xs(48), 0.0)
    defer += [lambda: lin(A("UU"), A("BM"), 0.875), lambda: lin(A("BP"), A("BM"), -2.0 / UH)]
    ts(C("XP", 0, 80), C("XP", 0, 80), rr, ALU.is_equal, C("PC", 48), ALU.mult)
    ts(C("XP", 144, 80), C("XP", 144, 80), rr, ALU.is_equal, C("PC", 49), ALU.mult)
    ts(C("XP", 80, 64), C("XP", 80, 64), rr, ALU.is_equal, C("PC", 50), ALU.mult)
    ts(C("XP", 224, 64), C("XP", 224, 64), rr, ALU.is_equal, C("PC", 50), ALU.mult)
    ts(C("XP", 288, 64), C("XP", 288, 64), rr, ALU.is_equal, C("PC", 51), ALU.mult)
    ts(C("RR", 80, 64, p=blk[0]), C("RR", 80, 64, p=blk[0]), 2.0 ** -12, ALU.min, -2.0 ** -12, ALU.max)
    tt(C("XP", 0, 144), C("XP", 0, 144), C("XP", 144, 144), ALU.add)
    ts(C("XP", 288, 64), C("XP", 288, 64), C("PC", 50), ALU.subtract)
    ts(A("CF"), A("CF"), 48.0, ALU.min)
    lin(C("WC", 0, 80), C("XP", 0, 80), 1.0)
    tt(C("WC", 80, 64), C("XP", 80, 64), C("XP", 288, 64), ALU.add)
    lin(C("PC", 27), C("PC", 4), 0.125, 48.0 * me)
    ts(C("PC", 54), acol, 8.0, ALU.is_lt)
    ts(C("SL", 56, 4), C("XI", 0, 4), C("PC", 27), ALU.add)
    ends = [lambda: lin(C("PC", 32), ad, 208.0, a4),
            lambda: lin(C("PC", 33), acol, -16.0, C("PC", 32)),
            lambda: lin(C("PC", 28), C("PC", 33), 1.0, 48.0 * me - 288.0),
            lambda: lin(C("PC", 30), acol, 16.0, 288.0),
            lambda: lin(C("PC", 31), acol, 1.0, ggc),
            lambda: lin(C("PC", 53), C("PC", 54), 3.0, 1.0),
            lambda: lin(C("PC", 29), C("PC", 28), C("PC", 54), C("PC", 30))]
    ends2 = [lambda: ts(C("SL", 84, 12), C("XI", 0, 12), 32.0, ALU.mult, C("PC", 31), ALU.add),
             lambda: ts(C("SL", 60, 24), C("XT", 40, 24), C("PC", 53), ALU.mult, C("PC", 29), ALU.add)]
    for q in range(3):
        keep0(C("MB", 128 * q, 128, p=(0, 96)), [[-1, 8], [-24, 4], [0, 4]], -8 * q)
    keep0(A("MC"), [[-4, 2], [-16, 8], [0, 16]], 0)
    for on in CFG["start"]:
        const(on)
    defer += [lambda: lin(A("PB"), A("NM"), 1.0 - 2.0 ** -14, CP),
              lambda: lin(C("VB", 0, 544), A("PB"), 1.0, -CP)]
    late = [lambda: lin(A("PH"), C("VB", 0, 544), 1.0), lambda: lin(C("IB", 0, 128), A("ID"), 1.0),
            lambda: lin(C("IB", 128, 128), A("ID"), -1.0),
            lambda: tt(A("BT"), A("NM"), C("VB", 0, 544), ALU.subtract),
            lambda: tt(A("PL"), C("VB", 0, 544), A("PH"), ALU.subtract)]

    def rul(rnd, k):
        if rnd == 0:
            return C("RU", k)
        return C("FI", 208 * (k // 4) + 192 + k % 4) if k < 8 else C("FI", 288 + 16 * k + 12)

    def big(bank, n, sign, p, start, stop, at=0):
        return (C(bank, at, n), A("W32", p=blk[p]), C("CC", 80 * (sign < 0), n, p=blk[p]), start, stop)

    def vote_v(rnd, k):
        ts(C("NE", 192 * k, 192), ind(TBr, C("VO", 16 * k, 12)), rul(rnd, k), ALU.not_equal)

    def vote_s(rnd, ks, part=None):
        for k in ks if part != 1 else []:
            act(C("SG", 192 * (k // 4 % 2), 192), ind(TBr, C("VO", 16 * k, 12)), AF.Sign, bias=rul(rnd, k), scale=-1.0)
        for k in ks if part != 0 else []:
            act(C("NE", 192 * k, 192), C("SG", 192 * (k // 4 % 2), 192), AF.Square)

    VBANK = ("VA", "VC", "CT")

    def vote_mm(x, k, row, start, stop):
        bank = VBANK[x]
        mm([big(bank, 64, 1, 0, True, False)] * start +
           [(C(bank, 0, 64), C("GQ", 128 - row, 128), C("NE", 192 * k + 64 * j, 64), False, False) for j in range(3)] +
           [big(bank, 64, -1, 0, False, True)] * stop)

    def vote_send(rnd, x):
        p = (0, 96) if x == 2 else None
        off = 16 * x + 4 * rnd
        if CFG["vr"][x] == "v":
            red(C("LX", 48 * me + off, p=p), C(VBANK[x], 0, 64, p=p), ALU.add)
        else:
            act(C("JS", 0, 64, p=p), C(VBANK[x], 0, 64, p=p), AF.Identity, acc=C("LX", 48 * me + off, p=p))
        send_all("v%s%d" % ("abc"[x], rnd), C("LX", 48 * me + off), lambda r: C("LX", 48 * r + off))

    def courts(off, mat, bank, at):
        c = sm(32)
        K = [C(bank if q else "VA", at + 4 * q, 4) for q in range(3)]
        votes = C("LX", off, 4, step=48)
        m0, m1, m2 = C("SM", c), C("SM", c + 1), C("SM", c + 2)
        al0, al1, k1, k2p, k2, pre = [C("SM", c + 4 + 4 * i, 4) for i in range(6)]
        return [
            lambda: [mm([(K[q], C(mat, 128 * q, 128), votes, True, True) for q in qs]) for qs in ((0,), (1, 2))],
            lambda: red(m0, K[0], ALU.max),
            lambda: ts(al0, K[0], m0, ALU.not_equal, 3.0, ALU.mult),
            lambda: tt(k1, K[1], al0, ALU.mult),
            lambda: tt(k2p, K[2], al0, ALU.mult),
            lambda: red(m1, k1, ALU.max),
            lambda: ts(al1, k1, m1, ALU.not_equal, 2.0, ALU.mult),
            lambda: tt(k2, k2p, al1, ALU.mult),
            lambda: tt(pre, al0, al1, ALU.add),
            lambda: red(m2, k2, ALU.max),
        ], c

    def update(b, rnd):
        if b < 2:
            lo, n = 208 * b, 192
            src = ind(C("FL0", 448 * rnd + 224 * b, 224), C("OF0", 16 * b, 13))
            put = lambda: lin(C("FI", lo, 208), src, 1.0) if CFG["sf"][b] else cp(C("FI", lo, 208), src)
            vo = lambda: cp(C("VO", 64 * b, 48), ind(C("NM", lo, 192), C("SL", 56, 3)))
        else:
            lo, n = 288 + 64 * b, 64
            put = lambda: cp(ind(C("FI", lo, n), C("OF2", 4 * b - 8, 4)),
                             A("MSG", rnd, 3, slice(64 * b - 128, 64 * b - 64)))
            vo = lambda: cp(C("VO", 64 * b, 48), C("NM", lo, 48))
        if CFG["rn"][b]:
            bank = ("VA", "VC")[b % 2]

            def flip():
                mm([(C(bank, 0, n), C("IB", 0, 128), C("FI", lo, n), True, False),
                    (C(bank, 0, n), C("IB", 128, 128), C("BT", lo, n), False, True)])
                act(C("BT", lo, n), C(bank, 0, n), AF.Abs)

            def name():
                mm([(C(bank, 0, n), C("IB", 0, 128), C(k, lo, n), k == "PH", k == "BT") for k in ("PH", "PL", "BT")])
                lin(C("NM", lo, n), C(bank, 0, n), 1.0)
            return [put, flip, name] + ([vo] if rnd < RO - 1 else [])
        return [put,
                lambda: tt(C("BT", lo, n), C("FI", lo, n), C("BT", lo, n), ALU.not_equal),
                lambda: tt(C("NM", lo, n), C("BT", lo, n), C("VB", lo, n), ALU.add),
                ] + ([vo] if rnd < RO - 1 else [])

    def names(rnd, b, a=0, n=48):
        return C("LN", 192 * rnd + 48 * b + a, n)

    def aux(rnd, b, i, n=1):
        if b < 2:
            return C("FL0", 448 * rnd + 224 * b + 56 * me + 48 + i, n)
        c = 64 * b - 128 + 16 * me + 12
        return A("MSG", rnd, 6 - me + i, slice(c, c + 1))

    def stale(rnd, b):
        act(C("ZS", 0, 768), ind(TBr, names(rnd, b)), AF.Identity, bias=191.0, scale=-2.0)

    def halve(NV):
        res = []
        UE, U0 = [ue(NV, i) for i in range(NV)], u0(NV)

        def vstep(i):
            n = 386 + (16 >> i) + (i == NV - 1)
            scan(C("UN", UE[i] - n, n), C("ZS", 840 * i, n, step=2), C("ZS", 840 * i + 1, n, step=2),
                 (4 * C1 - 256.0 * 128) * zu[i], ALU.add, ALU.add)

        def shift(i):
            ts(C("ZS", 840 * i, 768), C("ZS", 840 * i - 840, 768), zu[i] / zu[i - 1], ALU.mult, C("UN", UE[i - 1] - 1),
               ALU.subtract)

        def ssteps():
            t = C("UN", UE[-1] - 1)
            for j, n in enumerate(range(NV, 6)):
                c = sm(3)
                k = 96 - (16 >> n)
                act(A("JS"), C("ZS", 0 if j else 840 * (NV - 1), 768), AF.Sign, bias=t,
                    scale=-UP / (128 >> NV) if j == 0 else 0.5 if j % 2 else -0.5, acc=C("SM", c))
                if n < 5:
                    t = C("SM", c + 1)
                    act(C("UN", U0 + 96 * j + 96, k), C("UN", U0 + 96 * j, k), AF.Sign, bias=C("SM", c), scale=-8192.0,
                        acc=t)
            res.extend([t, c])
        calls = [lambda: vstep(0)]
        for i in range(1, NV):
            calls += [lambda i=i: shift(i), lambda i=i: vstep(i)]
        last = calls.pop()
        return calls + [lambda: (last(), ssteps())], res

    def offset(t, rnd, b, at):
        off, a = sb(), C("SM", t[1] + 2)
        if CFG["nv"][b] % 2:
            ts(a, C("SM", t[1]), 0.0, ALU.is_ge, t[0], ALU.subtract)
        else:
            ts(a, C("SM", t[1]), 0.0, ALU.is_le, t[0], ALU.add)
        at()
        ts(off, aux(rnd, b, 2), a, ALU.is_lt, a, ALU.subtract)
        return off

    def count(n, u):
        scan(C("SC", 0, 387), C("YY", 784 * n, 387, step=2), C("YY", 784 * n + 1, 387, step=2),
             (CG - 128.0 * 384 + UH / 2) * u, ALU.add, ALU.add)
        return C("SC", 386)

    def gaps(plan, lists):
        def at(place):
            for k in plan.get(place, ""):
                if k in "Yy":
                    const("v" if k == "Y" else "s")
                else:
                    run(lists[k], 1)
        return at

    def hearing(rnd, b, ahead, lists):
        h = 4 * rnd + b
        at = gaps(CFG["plan"][b], lists)
        par = h % 2
        zc = lambda a, n, step=1: C("ZZ", a, n, step=step)
        yc = lambda r, a=0, n=768: C("YY", 784 * r + a, n)
        dd = C("DD", 0, 96)
        Z = zc(0, 768)
        n8 = C("NM8", 48 * par, 48)
        gv = CFG["gv"][b]
        lists["L"], nxt = halve(CFG["nv"][b]) if b < 3 else ([], None)
        lists["N"] = [lambda: cp(n8, names(rnd, b))]
        lists["I"] = [lambda: lin(A("I0"), Z, 1.0, -64.0)] if CFG["st"][b] else []
        own = lambda: ts(zc(0, gv), ind(TBr, names(rnd, b, 0, gv // 16)), 64.0, ALU.add)
        if b and CFG["af"][b]:
            off = offset(ahead, rnd, b - 1, own)
        else:
            own()
        if gv < 768:
            act(zc(gv, 768 - gv), ind(TBr, names(rnd, b, gv // 16, 48 - gv // 16)), AF.Identity, bias=64.0)
        if 0 < b < 3:
            stale(rnd, b + 1)
        if b < 2 and CFG["n8"][b]:
            lists["N"] = [lambda: lin(n8, ind(C("NM", 208 * b, 192), C("O48", 4 * b, 3)), 1.0)]
        for x in range(2):
            mm([(dd, C("BM", 15 - a, 128), zc(96 * a, 96), a == 0, False) for a in range(4 * x, 4 * x + 4)])
        at("g")
        if b:
            if not CFG["af"][b]:
                off = offset(ahead, rnd, b - 1, lambda: at("a"))
            at("o")
            cuts = [0, gv, 768] if CFG["yp"] == 2 and gv < 768 else [0, 768]
            for a, e in zip(cuts, cuts[1:]):
                ts(yc(5, a, e - a), zc(a, e - a), off, ALU.add, -95.5, ALU.add)
            at("y")
            row, w = 5, count(5, 1.0)
        else:
            scan(C("SW", 0, 771), zc(0, 771), C("KK", 0, 771), C1 + 16512.0, ALU.add, ALU.add)
            w = C("SW", 770)
            for n, s in enumerate(STEP):
                at("%da" % n)
                if n < NS:
                    c = sm()
                    a = C("SM", sm())
                    act(A("JS"), Z, AF.Sign, bias=w, scale=-s, acc=C("SM", c))
                    ts(a, w, 2.0 / UP if n == 0 else 2.0, ALU.mult, -0.5 - (64 * STEP[NS] if n == NS - 1 else 0), ALU.add)
                    at("%db" % n)
                    w = sb()
                    ts(w, C("SM", c), 0.0, ALU.is_le, a, ALU.add)
                else:
                    if n == NS:
                        ts(yc(n), Z, s, ALU.mult, w, ALU.subtract)
                    else:
                        ts(yc(n), yc(n - 1), UH / (32 >> n), ALU.mult, w, ALU.subtract)
                    at("%db" % n)
                    w = count(n, unit[n])
            row = 4
        at("c")
        for x in range(2):
            ts(C("DM", PD * x, PD), yc(row, PD * x, PD), UH, ALU.mult, w, ALU.max)
            mm([(dd, C("BP" if b else "BQ", 15 - a, 128), C("DM", 96 * a, 96), False, a == 7)
                for a in range(4 * x, 4 * x + 4)])
        at("d")
        scan(A("DX"), C("DD", 0, 128), A("RW"), -1e9, ALU.max, ALU.add)
        mm([big("CT", 48, 1, 0, True, False)])
        at("x")
        vtr(C("XR", 0, 32), C("DX", 96, 32))
        at("t")
        scan(C("XR", 40, 34), C("XR", 0, 34), C("XR", 80, 34), -1e9, ALU.max, ALU.add)
        at("u")
        ju = C("JU", 2 * par)
        ts(ju, C("XR", 73), C("XR", 71), ALU.subtract, 383.0, ALU.add)
        at("j")
        s1 = 16 * par
        ts(C("S1", s1, 16), ind(Z, ju), -1.0, ALU.mult, CN, ALU.add)
        at("s")
        for e in range(2):
            ts(C("NR", 384 * e, 384), zc(e, 384, 2), C("S1", s1), ALU.add, CN, ALU.not_equal)
            mm([(C("CT", 0, 48), C("UU", 15 - 2 * i - e, 128), C("NR", 384 * e + i, 48, step=8), False, False)
                for i in range(8)] +
               ([big("CT", 48, -1, 0, False, False), (C("CT", 0, 48), A("ID"), n8, False, True)] if e else []))
        mc = 64 * b - 128 + 16 * me
        if b < 2:
            tt(aux(rnd, b, 0, 4), C("CR", 3, 4), C("S1", s1, 4), ALU.subtract)
            fl = C("FL0", 448 * rnd + 224 * b + 56 * me, 48)
        else:
            tt(A("MSG", rnd, slice(3 - me, 10 - me), mc + 12), C("CR", 0, 7), C("S1", s1, 7), ALU.subtract)
            fl = A("MSG", rnd, slice(3 - me, 7 - me), slice(mc, mc + 12))
        rho = aux(rnd, b, 3)
        at("n")
        assert not lists["I"]
        if CFG["st"][b]:
            act(A("I1"), Z, AF.Sign, bias=rho, scale=-1.0)
        else:
            ts(A("I0"), Z, rho, ALU.subtract, -1.0, ALU.min)
            ts(A("I1"), Z, 64.0, ALU.subtract, aux(rnd, b, 1), ALU.max)
        at("i")
        cp(A("OS"), C("CT", 0, 48))
        ts(fl, C("CT", 0, 48), float(TR), ALU.is_ge)
        at("f")
        tag = "f%s%d" % ("abcd"[b], rnd)
        if b < 2:
            slot = lambda r: C("FL0", 448 * rnd + 224 * b + 56 * r, 50)
            send_all(tag, slot(me), slot)
        else:
            send_each(tag, lambda r: A("MSG", rnd, 3 - me + r, slice(mc, mc + 16)),
                      lambda r: A("MSG", rnd, 3, slice(64 * b - 128 + 16 * r, 64 * b - 112 + 16 * r)))
        tt(ind(TBw, A("OS")), A("I0"), A("I1"), ALU.add)
        assert not lists["L"] and not lists["N"]
        return nxt

    left = [0, 0, 0]
    for rnd in range(RO):
        def weigh(r, b, on):
            p = (32 * r, 32 * r + 24)
            x = C("LX", 48 * r + 16 * b + 4 * rnd, p=p)
            if on == "v":
                ts(A("RR", p=p), A("WC", p=p), x, ALU.mult)
            else:
                lin(A("RR", p=p), A("WC", p=p), x)

        def scored(b):
            pm = lambda a, n=1, step=1: C("PM", 80 * b + a, n, step=step)
            c = sm(8)

            def score():
                for r, on in zip(peers, CFG["wg"][b]):
                    weigh(r, b, on)
                mm([big("PK", 80, 1, 1, True, False), (C("PK", 16, 64), A("LH"), C("RR", 80, 64), False, False),
                    big("PK", 80, -1, 1, False, False), (C("PK", 0, 80), A("LH"), C("RR", 0, 80), False, True)])
            return ([lambda: weigh(me, b, "s"), score,
                     lambda: scan(pm(0, 80), C("PK", 0, 80), A("RS"), -1e9, ALU.max, ALU.add),
                     lambda: ts(C("O48", 4 * b, 3), C("C48", 0, 3), pm(30 + 16 * me), ALU.add, pm(14), ALU.subtract),
                     lambda: cp(names(rnd, b), ind(C("NM", 208 * b, 192), C("O48", 4 * b, 3)))],
                    [lambda: ts(C("SM", c, 4), pm(30, 4, 16), pm(14), ALU.subtract, a4, ALU.is_equal),
                     lambda: tt(C("SM", c + 4, 4), C("SM", c, 4), C("XT", 32, 4), ALU.mult),
                     lambda: red(C("SM", c), C("SM", c + 4, 4), ALU.max),
                     lambda: ts(C("OF0", 16 * b, 16), A("CF"), C("SM", c), ALU.add)])

        cc, e = courts(32 + 4 * rnd, "MB", "VC", 160)

        def bcast():
            tt(C("QB", 0, 4), C("SM", e + 28, 4), C("SM", e + 24, 4), ALU.add)
            mm([(C("VC", 192 + 4 * x, 4), C("MC", 128 * x, 128), C("QB", 0, 4), True, True) for x in range(2)])

        def hand(b):
            at = 128 * rnd + 64 * b - 128
            cp(C("SN", at, 64), ind(C("NM", 288 + 64 * b, 64), C("OF2", 4 * b - 8, 4)))
            send_each("n%s%d" % ("abcd"[b], rnd), lambda r: C("SN", at + 16 * r, 12), lambda r: names(rnd, b, 12 * r, 12))
            dma(names(rnd, b, 12 * me, 12), C("SN", at + 16 * me, 12))

        cc += [lambda: ts(C("SM", e + 28, 4), C("SM", e + 20, 4), C("SM", e + 2), ALU.not_equal, -3.0, ALU.add),
               bcast, lambda: ts(A("OF2"), C("VC", 192, 8), 16.0, ALU.mult, acol, ALU.add), lambda: hand(2), lambda: hand(3)]
        (s0, l0), (s1, l1) = scored(0), scored(1)
        lists = {"P": s0, "Q": s1 + [lambda: stale(rnd, 1)], "A": l0, "B": l1, "G": cc, "D": defer, "E": ends, "F": ends2,
                 "T": late, "U": update(0, rnd), "V": update(1, rnd), "W": update(2, rnd),
                 "X": update(3, rnd - 1) if rnd else [],
                 "Z": [] if rnd else [lambda b=b: cp(C("NM", 208 * b, 192), A("L0", slice(0, 4), b)) for b in range(2)]}
        msg = [(0, 1, 2), (4, 5, 6), (8, 9, 10, 12, 13, 14)]
        for step in CFG["votes"].split():
            k = int(step[1:], 16) if step[0] in "vsqmr" else None
            if step[0] == "v":
                vote_v(rnd, k)
            elif step[0] in "sq":
                vote_s(rnd, [k], "sq".index(step[0]))
            elif step[0] == "m":
                x = min(k // 4, 2)
                i = msg[x].index(k)
                left[x] = left[x] % len(msg[x]) + 1
                vote_mm(x, k, 8 * i + (32 * me if x < 2 else 0), left[x] == 1, left[x] == len(msg[x]))
            elif step[0] == "r":
                vote_send(rnd, k)
            else:
                gaps({0: step}, lists)(0)
        ahead = None
        for b in range(4):
            ahead = hearing(rnd, b, ahead, lists)
        assert not any(lists.values()) and not early

    outs = [dma(T.yf[:], TBr)]
    run(update(3, RO - 1))
    cp(C("YR", 0, 4), C("FI", 192, 4))
    cp(C("YR", 4, 4), C("FI", 400, 4))
    cp(C("YR", 8, 8), C("FI", 428, 8, step=16))
    outs.append(dma(T.yr[:], A("YR")))
    cp(A("X1"), ind(A("NM"), C("SL", 60, 24)))
    vtr(A("X2"), A("X1"))
    cp(A("YC"), ind(A("X2"), C("SL", 84, 12)))
    outs.append(dma(T.yc[:], A("YC")))
    ops.append(["y", [], set(outs), 0, None])

    known = {q: 0 for q in Q}
    implies, waits, needed = [], [], set()
    for n, (q, calls, deps, inc, fixed) in enumerate(ops):
        ws = []
        if q != "r":
            for x in sorted(deps, reverse=True):
                if not known[q] >> x & 1:
                    ws.append(x)
                    needed.add(x)
                    known[q] |= implies[x]
            implies.append(known[q] | 1 << n)
        else:
            implies.append(1 << n)
        waits.append(ws)
    known = {q: 0 for q in Q}
    last = {q: [None] * POOL[q] for q in POOL}
    count = {}
    token = {}
    for n, (q, calls, deps, inc, fixed) in enumerate(ops):
        if q == "r":
            token[n] = fixed
            continue
        for x in waits[n]:
            Q[q].wait_ge(T.sem[token[x][0]], token[x][1])
            known[q] |= implies[x]
        if n in needed:
            free = [i for i, x in enumerate(last[q]) if x is None or known[q] >> x & 1]
            if not free:
                i = min(range(POOL[q]), key=lambda j: last[q][j])
                x = last[q][i]
                Q[q].wait_ge(T.sem[token[x][0]], token[x][1])
                known[q] |= implies[x]
                free = [i]
            name = "%s%d" % (q, free[0])
            last[q][free[0]] = n
            count[name] = count.get(name, 0) + inc * len(calls)
            token[n] = (name, count[name])
            for f in calls:
                f().then_inc(T.sem[name], inc)
        else:
            for f in calls:
                f()
    g.wait_ge(T.sem.sent, sent[0])
